import numpy as np
import ml_dtypes


def mxq(x, axis, fmt="e4m3"):
    dtype, down = {"e4m3": (ml_dtypes.float8_e4m3fn, 7), "e5m2": (ml_dtypes.float8_e5m2, 14)}[fmt]
    v = np.moveaxis(np.asarray(x, np.float32).astype(ml_dtypes.bfloat16).astype(np.float64), axis, -1)
    blocks = v.reshape(v.shape[:-1] + (-1, 32))
    amax = np.abs(blocks).max(-1, keepdims=True)
    byte = np.maximum(np.where(amax > 0, np.frexp(amax)[1] - 1 + 127, 0) - down, 1)
    scale = np.exp2(byte - 127.0)
    codes = (blocks / scale).astype(np.float32).astype(dtype).astype(np.float64)
    return np.moveaxis((codes * scale).reshape(v.shape), -1, axis)


WIDE = False


def mx_kscale(k):
    if not WIDE:
        return np.ones(k)
    levels = np.array([30, -30])
    if k % 512:
        return np.exp2(np.random.permutation(np.resize(levels, k // 32))).repeat(32)
    a = np.empty((k // 512, 16))
    for p in range(k // 512):
        a[p, :8] = np.random.permutation(np.resize(levels, 8))
        for g in range(8):
            far = levels[np.abs(levels - a[p, g]) >= 10]
            a[p, g + 8] = far[np.random.randint(len(far))]
    return np.exp2(a.ravel()).repeat(32)


def f64(x):
    return np.asarray(x).astype(np.float64)


def striped(idx):
    return np.tile(idx.reshape(-1, 16).T, (8, 1)).astype(np.uint16)


def unstriped(offs):
    return offs[:16].T.reshape(-1).astype(np.int64)


E2M1 = np.array([0.0, 0.5, 1.0, 1.5, 2.0, 3.0, 4.0, 6.0, -0.0, -0.5, -1.0, -1.5, -2.0, -3.0, -4.0, -6.0])


def pack_weight(w, fmt):
    k, n = w.shape
    w = f64(np.asarray(w, np.float32).astype(ml_dtypes.bfloat16)).reshape(k // 32, 32, n)
    amax = np.abs(w).max(1)
    if fmt == "e4m3":
        byte = np.frexp(amax)[1] - 1 + 127 - 7
    elif fmt == "e5m2":
        byte = np.frexp(amax)[1] - 1 + 127 - 14
    else:
        mant, ex = np.frexp(amax / 6.0)
        byte = np.where(mant > 0.5, ex, ex - 1) + 127
    byte = np.clip(np.where(amax > 0, byte, 1), 1, 254)
    scaled = (w * np.exp2(127.0 - byte)[:, None, :]).reshape(k, n).astype(np.float32)
    by_word = np.ascontiguousarray(scaled.reshape(k // 512, 128, 4, n).transpose(0, 1, 3, 2))
    if fmt == "e4m3":
        words = by_word.astype(ml_dtypes.float8_e4m3fn).view(np.uint8)
    elif fmt == "e5m2":
        words = by_word.astype(ml_dtypes.float8_e5m2).view(np.uint8)
    else:
        c = by_word.astype(ml_dtypes.float4_e2m1fn).view(np.uint8) & 0xF
        words = (c[..., 0::2] | (c[..., 1::2] << 4)).reshape(k // 512, 128, 2 * n)
    return np.ascontiguousarray(words), np.ascontiguousarray(byte.astype(np.uint8).reshape(k // 512, 16, n))


def unpack_weight(words, scales, fmt):
    g, _, n = scales.shape
    words = np.ascontiguousarray(words).reshape(g, 128, n, -1)
    if fmt == "e4m3":
        vals = words.view(ml_dtypes.float8_e4m3fn).astype(np.float64)
    elif fmt == "e5m2":
        vals = words.view(ml_dtypes.float8_e5m2).astype(np.float64)
    else:
        nib = np.empty((g, 128, n, 4), np.uint8)
        nib[..., 0::2] = words & 0xF
        nib[..., 1::2] = words >> 4
        vals = E2M1[nib]
    vals = vals * np.repeat(np.exp2(scales.astype(np.float64) - 127.0), 8, axis=1)[..., None]
    return vals.transpose(0, 1, 3, 2).reshape(g * 512, n)


def d_relu(v):
    return (v > 0).astype(np.float64)


K, T, E, C, H, N = 128, 1536, 6, 512, 1024, 512


def by_expert(wq, xq):
    return np.concatenate([wq[e].T @ xq[:, e * C:(e + 1) * C] for e in range(E)], axis=1)


def setup_inputs():
    n = np.random.standard_normal
    s = mx_kscale(N)[:, None]
    u = mx_kscale(H)
    first = np.random.permutation(np.repeat(np.arange(E), T // E))
    second = (first + 1 + np.random.permutation(np.repeat(np.arange(E - 1), -(-T // (E - 1)))[:T])) % E
    while np.bincount(second, minlength=E).max() != T // E:
        load = np.bincount(second, minlength=E); hi, lo = int(load.argmax()), int(load.argmin())
        t = np.flatnonzero((second == hi) & (first != lo))[0]; second[t] = lo
    slot_token = np.empty(E * C, np.int64); pos = np.empty((2, T), np.int64); fill = np.zeros(E, np.int64)
    place = np.stack([np.random.permutation(C) for _ in range(E)])
    for r, deal in enumerate((first, second)):
        for t in np.random.permutation(T):
            e = deal[t]; j = e * C + place[e, fill[e]]; fill[e] += 1; slot_token[j] = t; pos[r, t] = j
    g = np.random.uniform(0.2, 0.8, T)
    w_slot = np.empty(E * C); w_slot[pos[0]] = g; w_slot[pos[1]] = 1.0 - g
    dy = pack_weight(n((N, T)) * s, "e5m2")
    w2 = [pack_weight(m, "e2m1") for m in n((E, N, H)) / np.sqrt(N) / s[None] * u[None, None, :]]
    w1 = [pack_weight(m, "e2m1") for m in n((E, H, K)) / np.sqrt(H) / u[None, :, None]]
    return {
        "dy_words": dy[0],
        "dy_scales": dy[1],
        "a": n((H, E * C)).astype(np.float32),
        "w2_words": np.stack([m[0] for m in w2]),
        "w2_scales": np.stack([m[1] for m in w2]),
        "w1_words": np.stack([m[0] for m in w1]),
        "w1_scales": np.stack([m[1] for m in w1]),
        "gate": np.tile(w_slot, (H, 1)).astype(np.float32),
        "offs": striped(slot_token),
        "pos1": striped(pos[0]),
        "pos2": striped(pos[1]),
    }


def reference(dy_words, dy_scales, a, w2_words, w2_scales, w1_words, w1_scales, gate, offs, pos1, pos2):
    idx = unstriped(offs)
    w2 = np.stack([unpack_weight(w2_words[e], w2_scales[e], "e2m1") for e in range(E)])
    w1 = np.stack([unpack_weight(w1_words[e], w1_scales[e], "e2m1") for e in range(E)])
    gq = unpack_weight(dy_words, dy_scales, "e5m2")[:, idx]
    dh = f64(gate) * by_expert(w2, gq)
    da = dh * d_relu(f64(a))
    dx = by_expert(w1, mxq(da, 0, "e5m2"))
    return dx[:, unstriped(pos1)] + dx[:, unstriped(pos2)]

@@ -1,0 +1,213 @@
+from contextlib import ExitStack
+
+import concourse.mybir as mybir
+from concourse.masks import make_identity
+
+K, T, E, C, H, N = 128, 1536, 6, 512, 1024, 512
+S = E * C
+FLOPS = 2 * S * H * (N + K)
+BYTES = N * T + N * T // 32 + 4 * H * S + E * H * (N + K) // 2 + E * H * (N + K) // 32 + 4 * S + 256 * (S + 2 * T) // 16 + 4 * K * T
+
+F32 = mybir.dt.float32
+BF16 = mybir.dt.bfloat16
+I32 = mybir.dt.int32
+U32 = mybir.dt.uint32
+U16 = mybir.dt.uint16
+U8 = mybir.dt.uint8
+E5M2X4 = mybir.dt.float8_e5m2_x4
+E2M1X4 = mybir.dt.float4_e2m1fn_x4
+ALU = mybir.AluOpType
+ACT = mybir.ActivationFunctionType
+
+P = 128
+PASS = 512
+PASSES = H // PASS
+BLOCKS = C // P
+HALF = C // 2
+LIST_COL = 16
+SIGN_ON_SCALAR = ((1, 1), (2, 1), (3, 1))
+OUT_PIECES = (512, 512, 256, 256)
+
+
+def tile_moe_bdx_mlp_relu_kernel(
+    tc, dy_words, dy_scales, a, w2_words, w2_scales, w1_words, w1_scales, gate, offs, pos1, pos2, out
+):
+    nc = tc.nc
+    with ExitStack() as ctx:
+        keep = ctx.enter_context(tc.tile_pool(name="keep", bufs=1))
+        ring = ctx.enter_context(tc.tile_pool(name="ring", bufs=2))
+        psum = ctx.enter_context(tc.psum_pool(name="psum", bufs=1))
+
+        offs_sb = keep.tile([P, S // LIST_COL], U16, name="offs_sb")
+        pos1_sb = keep.tile([P, T // LIST_COL], U16, name="pos1_sb")
+        pos2_sb = keep.tile([P, T // LIST_COL], U16, name="pos2_sb")
+        dy_w = keep.tile([P, T], I32, name="dy_w", align_bytes=64)
+        dy_s = keep.tile([P, T], U8, name="dy_s", align_bytes=64)
+        w2_s = keep.tile([P, E * H], U8, name="w2_s", align_bytes=64)
+        w1_s = keep.tile([P, E * PASSES * K], U8, name="w1_s", align_bytes=64)
+        w1_w = keep.tile([P, E * PASSES * 2 * K], U8, name="w1_w", align_bytes=64)
+        w2_w = [keep.tile([P, 2 * H], U8, name="w2_w%d" % e, align_bytes=64) for e in range(E)]
+        a_sb = [[keep.tile([P, 4, C], F32, name="a%d_%d" % (e, s)) for s in range(PASSES)] for e in range(E)]
+        ident = keep.tile([P, P], F32, name="ident")
+        gate_rows = keep.tile([P, P], F32, name="gate_rows")
+        gate_col = keep.tile([P, S // P], F32, name="gate_col")
+        dx = keep.tile([P, S], F32, name="dx")
+        first_half = keep.tile([P, T], F32, name="first_half")
+
+        nc.gpsimd.memset(dy_s[:].bitcast(I32), 0)
+        nc.vector.memset(w2_s[:].bitcast(I32), 0)
+        nc.gpsimd.memset(gate_rows[:], 0.0)
+        nc.gpsimd.dma_start(gate_rows[0 : S // P, :], gate[0].rearrange("(b m) -> b m", m=P))
+        make_identity(nc, ident[:])
+        nc.gpsimd.memset(w1_s[:].bitcast(I32), 0)
+
+        def load_a(e):
+            for s in range(PASSES):
+                rows = a[s * PASS : (s + 1) * PASS, e * C : (e + 1) * C]
+                nc.sync.dma_start(a_sb[e][s][:], rows.rearrange("(p t) c -> p t c", t=4))
+
+        nc.sync.dma_start(offs_sb[:], offs)
+        nc.sync.dma_start(dy_w[:], dy_words[0].rearrange("p t d -> p (t d)").bitcast(I32))
+        for r in range(4):
+            nc.scalar.dma_start(dy_s[r:P:32, :].bitcast(I32), dy_scales[0, r:16:4, :].bitcast(I32))
+        nc.sync.dma_start(w2_w[0][:].bitcast(I32), w2_words[0, 0].bitcast(I32))
+        for r in range(4):
+            nc.sync.dma_start(
+                w2_s[r:P:32, :].bitcast(I32).rearrange("q (e i) -> q e i", e=E),
+                w2_scales[:, 0, r:16:4, :].bitcast(I32).rearrange("e q i -> q e i"),
+            )
+        load_a(0)
+        nc.sync.dma_start(w2_w[1][:].bitcast(I32), w2_words[1, 0].bitcast(I32))
+        for r in range(4):
+            nc.sync.dma_start(
+                w1_s[r:P:32, :].bitcast(I32).rearrange("q (g k) -> q g k", g=E * PASSES),
+                w1_scales.rearrange("e s f k -> (e s) f k")[:, r:16:4, :].bitcast(I32).rearrange("g q k -> q g k"),
+            )
+        nc.sync.dma_start(
+            w1_w[:].bitcast(I32).rearrange("p (g k) -> p g k", g=E * PASSES),
+            w1_words.rearrange("e s p k -> p (e s) k").bitcast(I32),
+        )
+        for e in range(1, E):
+            if e + 1 < E:
+                nc.sync.dma_start(w2_w[e + 1][:].bitcast(I32), w2_words[e + 1, 0].bitcast(I32))
+            load_a(e)
+        nc.sync.dma_start(pos1_sb[:], pos1)
+        nc.sync.dma_start(pos2_sb[:], pos2)
+
+        gate_ps = psum.tile([P, 4 * P], F32, name="gate_ps", tag="turned", bufs=3)
+        nc.tensor.transpose(gate_ps[:, 0:P], gate_rows[:], ident[:])
+        nc.scalar.activation(gate_col[:], gate_ps[:, 0 : S // P], ACT.Copy)
+
+        gathered = {}
+        rounded = {}
+        mask_of = {}
+
+        def gather(e):
+            cols = offs_sb[:, e * C // LIST_COL : (e + 1) * C // LIST_COL]
+            g_w = ring.tile([P, C], U32, name="g_w", align_bytes=64, bufs=3)
+            g_s = ring.tile([P, C], U8, name="g_s", align_bytes=64, bufs=3)
+            nc.vector.tensor_copy(g_s[:], dy_s[:].indirect(cols))
+            width = HALF if e == 0 else C
+            for c0 in range(0, C, width):
+                part = cols[:, c0 // LIST_COL : (c0 + width) // LIST_COL]
+                nc.vector.tensor_copy(g_w[:, c0 : c0 + width], dy_w[:].bitcast(U32).indirect(part))
+            gathered[e] = (g_w, g_s)
+
+        def first_product(e):
+            g_w, g_s = gathered[e]
+            for h in range(2):
+                for s in range(PASSES):
+                    for b in (2 * h, 2 * h + 1):
+                        dh = psum.tile([P, PASS], F32, name="dh", tag="dh", bufs=4)
+                        nc.tensor.matmul_mx(
+                            out=dh[:],
+                            lhsT=g_w[:, b * P : (b + 1) * P].bitcast(E5M2X4),
+                            lhsT_scale=g_s[:, b * P : (b + 1) * P],
+                            rhs=w2_w[e][:, 2 * s * PASS : 2 * (s + 1) * PASS].bitcast(E2M1X4),
+                            rhs_scale=w2_s[:, e * H + s * PASS : e * H + (s + 1) * PASS],
+                            start=True,
+                            stop=True,
+                        )
+                        x = ring.tile([P, PASS], BF16, name="x", bufs=16)
+                        nc.scalar.activation(
+                            x[:].rearrange("m (u p d) -> m u p d", u=2, d=2),
+                            dh[:].rearrange("m (p u d) -> m u p d", u=2, d=2),
+                            ACT.Copy,
+                            scale=gate_col[:, e * BLOCKS + b : e * BLOCKS + b + 1],
+                        )
+                        rounded[e, s, b] = x
+
+        def mask_views(e, s):
+            mask = ring.tile([P, 4 * C], BF16, name="mask", bufs=4)
+            mask_of[e, s] = mask
+            return mask[:].rearrange("p (u c d) -> p u c d", u=2, d=2), a_sb[e][s][:].rearrange("p (u d) c -> p u c d", u=2)
+
+        def signs(e):
+            for s in range(PASSES):
+                if (e, s) in SIGN_ON_SCALAR:
+                    dst, src = mask_views(e, s)
+                    nc.scalar.activation(dst, src, ACT.Sign)
+
+        def make_mask(e, s):
+            if (e, s) in SIGN_ON_SCALAR:
+                mask = mask_of[e, s]
+                nc.vector.tensor_scalar(out=mask[:], in0=mask[:], scalar1=0.0, scalar2=None, op0=ALU.max)
+            else:
+                dst, src = mask_views(e, s)
+                nc.vector.tensor_scalar(out=dst, in0=src, scalar1=0.0, scalar2=None, op0=ALU.is_gt)
+
+        def second_product(e):
+            da = [ring.tile([P, 4 * C], BF16, name="da", align_bytes=64, bufs=4) for s in range(PASSES)]
+            for s in range(PASSES):
+                make_mask(e, s)
+            for h in range(2):
+                for s in range(PASSES):
+                    turned = psum.tile([P, 4 * P], F32, name="turned", tag="turned", bufs=3)
+                    for j in range(2):
+                        words = rounded[e, s, 2 * h + j][:].bitcast(F32)
+                        for u in range(2):
+                            at = (2 * u + j) * P
+                            nc.tensor.transpose(turned[:, at : at + P], words[:, u * P : (u + 1) * P], ident[:])
+                    mask = mask_of[e, s][:].rearrange("p (u c d) -> p c u d", u=2, d=2)
+                    nc.vector.tensor_tensor(
+                        da[s][:, 4 * h * HALF : 4 * (h + 1) * HALF].rearrange("p (c u d) -> p c u d", u=2, d=2),
+                        turned[:].bitcast(BF16).rearrange("p (u c d) -> p c u d", u=2, d=2),
+                        mask[:, h * HALF : (h + 1) * HALF],
+                        ALU.mult,
+                    )
+            acc = psum.tile([P, C], F32, name="acc", tag="acc", bufs=1)
+            for s in range(PASSES):
+                codes = ring.tile([P, C], U32, name="codes", align_bytes=64, bufs=3)
+                scales = ring.tile([P, C], U8, name="scales", align_bytes=64, bufs=3)
+                nc.vector.quantize_mx(out=codes[:].bitcast(E5M2X4), scales=scales[:], in_=da[s][:])
+                g = e * PASSES + s
+                nc.tensor.matmul_mx(
+                    out=acc[:],
+                    lhsT=w1_w[:, 2 * g * K : 2 * (g + 1) * K].bitcast(E2M1X4),
+                    lhsT_scale=w1_s[:, g * K : (g + 1) * K],
+                    rhs=codes[:].bitcast(E5M2X4),
+                    rhs_scale=scales[:],
+                    start=(s == 0),
+                    stop=(s == PASSES - 1),
+                )
+            nc.scalar.copy(dx[:, e * C : (e + 1) * C], acc[:])
+
+        gather(0)
+        first_product(0)
+        gather(1)
+        for e in range(E):
+            second_product(e)
+            if e + 1 < E:
+                signs(e + 1)
+                first_product(e + 1)
+            if e + 2 < E:
+                gather(e + 2)
+
+        nc.vector.tensor_copy(first_half[:], dx[:].indirect(pos1_sb[:]))
+        t0 = 0
+        for n, width in enumerate(OUT_PIECES):
+            piece = keep.tile([P, width], F32, name="piece%d" % n)
+            cols = pos2_sb[:, t0 // LIST_COL : (t0 + width) // LIST_COL]
+            nc.vector.tensor_tensor(piece[:], dx[:].indirect(cols), first_half[:, t0 : t0 + width], ALU.add)
+            nc.sync.dma_start(out[:, t0 : t0 + width], piece[:])
+            t0 = t0 + width

@@ -25,7 +25,7 @@ PASSES = H // PASS
 BLOCKS = C // P
 HALF = C // 2
 LIST_COL = 16
-SIGN_ON_SCALAR = ((1, 1), (2, 1), (3, 1))
+SIGN_ON_SCALAR = ((1, 1), (2, 1), (3, 1), (4, 1))
 OUT_PIECES = (512, 512, 256, 256)
 
 
@@ -43,11 +43,13 @@ def tile_moe_bdx_mlp_relu_kernel(
         pos2_sb = keep.tile([P, T // LIST_COL], U16, name="pos2_sb")
         dy_w = keep.tile([P, T], I32, name="dy_w", align_bytes=64)
         dy_s = keep.tile([P, T], U8, name="dy_s", align_bytes=64)
-        w2_s = keep.tile([P, E * H], U8, name="w2_s", align_bytes=64)
+        w2_s_first = keep.tile([P, H], U8, name="w2_s_first", align_bytes=64)
+        w2_s_rest = keep.tile([P, (E - 1) * H], U8, name="w2_s_rest", align_bytes=64)
+        w2_s = [w2_s_first[:]] + [w2_s_rest[:, e * H : (e + 1) * H] for e in range(E - 1)]
         w1_s = keep.tile([P, E * PASSES * K], U8, name="w1_s", align_bytes=64)
         w1_w = keep.tile([P, E * PASSES * 2 * K], U8, name="w1_w", align_bytes=64)
         w2_w = [keep.tile([P, 2 * H], U8, name="w2_w%d" % e, align_bytes=64) for e in range(E)]
-        a_sb = [[keep.tile([P, 4, C], F32, name="a%d_%d" % (e, s)) for s in range(PASSES)] for e in range(E)]
+        a_sb = {}
         ident = keep.tile([P, P], F32, name="ident")
         gate_rows = keep.tile([P, P], F32, name="gate_rows")
         gate_col = keep.tile([P, S // P], F32, name="gate_col")
@@ -55,29 +57,37 @@ def tile_moe_bdx_mlp_relu_kernel(
         first_half = keep.tile([P, T], F32, name="first_half")
 
         nc.gpsimd.memset(dy_s[:].bitcast(I32), 0)
-        nc.vector.memset(w2_s[:].bitcast(I32), 0)
-        nc.gpsimd.memset(gate_rows[:], 0.0)
-        nc.gpsimd.dma_start(gate_rows[0 : S // P, :], gate[0].rearrange("(b m) -> b m", m=P))
         make_identity(nc, ident[:])
-        nc.gpsimd.memset(w1_s[:].bitcast(I32), 0)
 
-        def load_a(e):
-            for s in range(PASSES):
-                rows = a[s * PASS : (s + 1) * PASS, e * C : (e + 1) * C]
-                nc.sync.dma_start(a_sb[e][s][:], rows.rearrange("(p t) c -> p t c", t=4))
+        def load_a(e, s):
+            rows = a[s * PASS : (s + 1) * PASS, e * C : (e + 1) * C]
+            a_sb[e, s] = ring.tile([P, 4, C], F32, name="a_sb", bufs=8)
+            nc.sync.dma_start(a_sb[e, s][:], rows.rearrange("(p t) c -> p t c", t=4))
+
+        def load_w2(e):
+            nc.sync.dma_start(w2_w[e][:].bitcast(I32), w2_words[e, 0].bitcast(I32))
+
+        def load_w2_scales(plane, e0, e1):
+            for r in range(4):
+                nc.sync.dma_start(
+                    plane[r:P:32, :].bitcast(I32).rearrange("q (e i) -> q e i", i=H // 4),
+                    w2_scales[e0:e1, 0, r:16:4, :].bitcast(I32).rearrange("e q i -> q e i"),
+                )
 
         nc.sync.dma_start(offs_sb[:], offs)
+        for r in range(4):
+            nc.sync.dma_start(dy_s[r:P:32, :].bitcast(I32), dy_scales[0, r:16:4, :].bitcast(I32))
         nc.sync.dma_start(dy_w[:], dy_words[0].rearrange("p t d -> p (t d)").bitcast(I32))
-        for r in range(4):
-            nc.scalar.dma_start(dy_s[r:P:32, :].bitcast(I32), dy_scales[0, r:16:4, :].bitcast(I32))
-        nc.sync.dma_start(w2_w[0][:].bitcast(I32), w2_words[0, 0].bitcast(I32))
-        for r in range(4):
-            nc.sync.dma_start(
-                w2_s[r:P:32, :].bitcast(I32).rearrange("q (e i) -> q e i", e=E),
-                w2_scales[:, 0, r:16:4, :].bitcast(I32).rearrange("e q i -> q e i"),
-            )
-        load_a(0)
-        nc.sync.dma_start(w2_w[1][:].bitcast(I32), w2_words[1, 0].bitcast(I32))
+        load_w2(0)
+        nc.sync.dma_start(gate_rows[:], gate.rearrange("h (b m) -> (h b) m", m=P)[0:P, :])
+        load_w2_scales(w2_s_first, 0, 1)
+        load_a(0, 0)
+        load_w2(1)
+        load_w2_scales(w2_s_rest, 1, E)
+        load_a(0, 1)
+        load_a(1, 1)
+        load_a(1, 0)
+        load_w2(2)
         for r in range(4):
             nc.sync.dma_start(
                 w1_s[r:P:32, :].bitcast(I32).rearrange("q (g k) -> q g k", g=E * PASSES),
@@ -87,99 +97,116 @@ def tile_moe_bdx_mlp_relu_kernel(
             w1_w[:].bitcast(I32).rearrange("p (g k) -> p g k", g=E * PASSES),
             w1_words.rearrange("e s p k -> p (e s) k").bitcast(I32),
         )
-        for e in range(1, E):
+        for e in range(2, E):
+            load_a(e, 1)
+            load_a(e, 0)
             if e + 1 < E:
-                nc.sync.dma_start(w2_w[e + 1][:].bitcast(I32), w2_words[e + 1, 0].bitcast(I32))
-            load_a(e)
+                load_w2(e + 1)
         nc.sync.dma_start(pos1_sb[:], pos1)
         nc.sync.dma_start(pos2_sb[:], pos2)
 
-        gate_ps = psum.tile([P, 4 * P], F32, name="gate_ps", tag="turned", bufs=3)
+        gate_ps = psum.tile([P, 4 * P], F32, name="gate_ps", tag="turned", bufs=4)
         nc.tensor.transpose(gate_ps[:, 0:P], gate_rows[:], ident[:])
         nc.scalar.activation(gate_col[:], gate_ps[:, 0 : S // P], ACT.Copy)
 
-        gathered = {}
+        g_w = {}
+        g_s = {}
         rounded = {}
+        sign_of = {}
         mask_of = {}
+        turned_of = {}
+        da_of = {}
+        quantised = {}
 
-        def gather(e):
-            cols = offs_sb[:, e * C // LIST_COL : (e + 1) * C // LIST_COL]
-            g_w = ring.tile([P, C], U32, name="g_w", align_bytes=64, bufs=3)
-            g_s = ring.tile([P, C], U8, name="g_s", align_bytes=64, bufs=3)
-            nc.vector.tensor_copy(g_s[:], dy_s[:].indirect(cols))
+        def made_on_vector(columns, dtype, name):
+            return ring.tile([P, columns], dtype, name=name, tag="made_on_vector", align_bytes=64, bufs=20)
+
+        def slots(e, c0, c1):
+            return offs_sb[:, (e * C + c0) // LIST_COL : (e * C + c1) // LIST_COL]
+
+        def gather_bytes(e):
+            g_s[e] = made_on_vector(C, U8, "g_s")
+            nc.vector.tensor_copy(g_s[e][:], dy_s[:].indirect(slots(e, 0, C)))
+
+        def gather_words(e):
+            g_w[e] = made_on_vector(C, U32, "g_w")
             width = HALF if e == 0 else C
             for c0 in range(0, C, width):
-                part = cols[:, c0 // LIST_COL : (c0 + width) // LIST_COL]
-                nc.vector.tensor_copy(g_w[:, c0 : c0 + width], dy_w[:].bitcast(U32).indirect(part))
-            gathered[e] = (g_w, g_s)
+                nc.vector.tensor_copy(g_w[e][:, c0 : c0 + width], dy_w[:].bitcast(U32).indirect(slots(e, c0, c0 + width)))
 
         def first_product(e):
-            g_w, g_s = gathered[e]
-            for h in range(2):
-                for s in range(PASSES):
-                    for b in (2 * h, 2 * h + 1):
-                        dh = psum.tile([P, PASS], F32, name="dh", tag="dh", bufs=4)
-                        nc.tensor.matmul_mx(
-                            out=dh[:],
-                            lhsT=g_w[:, b * P : (b + 1) * P].bitcast(E5M2X4),
-                            lhsT_scale=g_s[:, b * P : (b + 1) * P],
-                            rhs=w2_w[e][:, 2 * s * PASS : 2 * (s + 1) * PASS].bitcast(E2M1X4),
-                            rhs_scale=w2_s[:, e * H + s * PASS : e * H + (s + 1) * PASS],
-                            start=True,
-                            stop=True,
-                        )
-                        x = ring.tile([P, PASS], BF16, name="x", bufs=16)
-                        nc.scalar.activation(
-                            x[:].rearrange("m (u p d) -> m u p d", u=2, d=2),
-                            dh[:].rearrange("m (p u d) -> m u p d", u=2, d=2),
-                            ACT.Copy,
-                            scale=gate_col[:, e * BLOCKS + b : e * BLOCKS + b + 1],
-                        )
-                        rounded[e, s, b] = x
+            for s in range(PASSES):
+                for b in range(BLOCKS):
+                    dh = psum.tile([P, PASS], F32, name="dh", tag="sums", bufs=4)
+                    nc.tensor.matmul_mx(
+                        out=dh[:],
+                        lhsT=g_w[e][:, b * P : (b + 1) * P].bitcast(E5M2X4),
+                        lhsT_scale=g_s[e][:, b * P : (b + 1) * P],
+                        rhs=w2_w[e][:, 2 * s * PASS : 2 * (s + 1) * PASS].bitcast(E2M1X4),
+                        rhs_scale=w2_s[e][:, s * PASS : (s + 1) * PASS],
+                        start=True,
+                        stop=True,
+                    )
+                    x = ring.tile([P, PASS], BF16, name="x", bufs=16)
+                    nc.scalar.activation(
+                        x[:].rearrange("m (u p d) -> m u p d", u=2, d=2),
+                        dh[:].rearrange("m (p u d) -> m u p d", u=2, d=2),
+                        ACT.Copy,
+                        scale=gate_col[:, e * BLOCKS + b : e * BLOCKS + b + 1],
+                    )
+                    rounded[e, s, b] = x
+                    if b % 2 == 1:
+                        turn(e, s, b // 2)
 
-        def mask_views(e, s):
-            mask = ring.tile([P, 4 * C], BF16, name="mask", bufs=4)
-            mask_of[e, s] = mask
-            return mask[:].rearrange("p (u c d) -> p u c d", u=2, d=2), a_sb[e][s][:].rearrange("p (u d) c -> p u c d", u=2)
+        def paired(tile):
+            return tile[:].rearrange("p (u c d) -> p u c d", u=2, d=2)
+
+        def saved(e, s):
+            return a_sb[e, s][:].rearrange("p (u d) c -> p u c d", u=2)
 
         def signs(e):
             for s in range(PASSES):
                 if (e, s) in SIGN_ON_SCALAR:
-                    dst, src = mask_views(e, s)
-                    nc.scalar.activation(dst, src, ACT.Sign)
+                    sign_of[e, s] = ring.tile([P, 4 * C], BF16, name="sign", bufs=2)
+                    nc.scalar.activation(paired(sign_of[e, s]), saved(e, s), ACT.Sign)
 
         def make_mask(e, s):
+            mask_of[e, s] = made_on_vector(4 * C, BF16, "mask")
             if (e, s) in SIGN_ON_SCALAR:
-                mask = mask_of[e, s]
-                nc.vector.tensor_scalar(out=mask[:], in0=mask[:], scalar1=0.0, scalar2=None, op0=ALU.max)
+                nc.vector.tensor_scalar(out=mask_of[e, s][:], in0=sign_of[e, s][:], scalar1=0.0, scalar2=None, op0=ALU.max)
             else:
-                dst, src = mask_views(e, s)
-                nc.vector.tensor_scalar(out=dst, in0=src, scalar1=0.0, scalar2=None, op0=ALU.is_gt)
+                nc.vector.tensor_scalar(out=paired(mask_of[e, s]), in0=saved(e, s), scalar1=0.0, scalar2=None, op0=ALU.is_gt)
+
+        def turn(e, s, h):
+            turned = psum.tile([P, 4 * P], F32, name="turned", tag="turned", bufs=4)
+            for j in range(2):
+                words = rounded[e, s, 2 * h + j][:].bitcast(F32)
+                for u in range(2):
+                    at = (2 * u + j) * P
+                    nc.tensor.transpose(turned[:, at : at + P], words[:, u * P : (u + 1) * P], ident[:])
+            turned_of[e, s, h] = turned
+
+        def masked(e, s, h):
+            if h == 0:
+                da_of[e, s] = made_on_vector(4 * C, BF16, "da")
+            mask = mask_of[e, s][:].rearrange("p (u c d) -> p c u d", u=2, d=2)
+            nc.vector.tensor_tensor(
+                da_of[e, s][:, 4 * h * HALF : 4 * (h + 1) * HALF].rearrange("p (c u d) -> p c u d", u=2, d=2),
+                turned_of[e, s, h][:].bitcast(BF16).rearrange("p (u c d) -> p c u d", u=2, d=2),
+                mask[:, h * HALF : (h + 1) * HALF],
+                ALU.mult,
+            )
+
+        def quantise(e, s):
+            codes = made_on_vector(C, U32, "codes")
+            scales = ring.tile([P, C], U8, name="scales", align_bytes=64, bufs=4)
+            nc.vector.quantize_mx(out=codes[:].bitcast(E5M2X4), scales=scales[:], in_=da_of[e, s][:])
+            quantised[e, s] = (codes, scales)
 
         def second_product(e):
-            da = [ring.tile([P, 4 * C], BF16, name="da", align_bytes=64, bufs=4) for s in range(PASSES)]
+            acc = psum.tile([P, C], F32, name="acc", tag="sums", bufs=4)
             for s in range(PASSES):
-                make_mask(e, s)
-            for h in range(2):
-                for s in range(PASSES):
-                    turned = psum.tile([P, 4 * P], F32, name="turned", tag="turned", bufs=3)
-                    for j in range(2):
-                        words = rounded[e, s, 2 * h + j][:].bitcast(F32)
-                        for u in range(2):
-                            at = (2 * u + j) * P
-                            nc.tensor.transpose(turned[:, at : at + P], words[:, u * P : (u + 1) * P], ident[:])
-                    mask = mask_of[e, s][:].rearrange("p (u c d) -> p c u d", u=2, d=2)
-                    nc.vector.tensor_tensor(
-                        da[s][:, 4 * h * HALF : 4 * (h + 1) * HALF].rearrange("p (c u d) -> p c u d", u=2, d=2),
-                        turned[:].bitcast(BF16).rearrange("p (u c d) -> p c u d", u=2, d=2),
-                        mask[:, h * HALF : (h + 1) * HALF],
-                        ALU.mult,
-                    )
-            acc = psum.tile([P, C], F32, name="acc", tag="acc", bufs=1)
-            for s in range(PASSES):
-                codes = ring.tile([P, C], U32, name="codes", align_bytes=64, bufs=3)
-                scales = ring.tile([P, C], U8, name="scales", align_bytes=64, bufs=3)
-                nc.vector.quantize_mx(out=codes[:].bitcast(E5M2X4), scales=scales[:], in_=da[s][:])
+                codes, scales = quantised[e, s]
                 g = e * PASSES + s
                 nc.tensor.matmul_mx(
                     out=acc[:],
@@ -190,18 +217,35 @@ def tile_moe_bdx_mlp_relu_kernel(
                     start=(s == 0),
                     stop=(s == PASSES - 1),
                 )
-            nc.scalar.copy(dx[:, e * C : (e + 1) * C], acc[:])
-
-        gather(0)
-        first_product(0)
-        gather(1)
-        for e in range(E):
-            second_product(e)
             if e + 1 < E:
-                signs(e + 1)
-                first_product(e + 1)
+                nc.scalar.copy(dx[:, e * C : (e + 1) * C], acc[:])
+            else:
+                nc.vector.tensor_copy(dx[:, e * C : (e + 1) * C], acc[:])
+
+        gather_bytes(0)
+        gather_bytes(1)
+        gather_words(0)
+        first_product(0)
+        gather_words(1)
+        gather_bytes(2)
+        make_mask(0, 0)
+        for e in range(E):
             if e + 2 < E:
-                gather(e + 2)
+                gather_words(e + 2)
+            masked(e, 0, 0)
+            masked(e, 0, 1)
+            make_mask(e, 1)
+            quantise(e, 0)
+            masked(e, 1, 0)
+            masked(e, 1, 1)
+            if e + 3 < E:
+                gather_bytes(e + 3)
+            if e + 1 < E:
+                first_product(e + 1)
+                signs(e + 1)
+                make_mask(e + 1, 0)
+            quantise(e, 1)
+            second_product(e)
 
         nc.vector.tensor_copy(first_half[:], dx[:].indirect(pos1_sb[:]))
         t0 = 0

@@ -25,7 +25,8 @@ PASSES = H // PASS
 BLOCKS = C // P
 HALF = C // 2
 LIST_COL = 16
-SIGN_ON_SCALAR = ((1, 1), (2, 1), (3, 1), (4, 1))
+LAST = PASSES - 1
+SIGN_ON_SCALAR = (1, 2, 3)
 OUT_PIECES = (512, 512, 256, 256)
 
 
@@ -157,6 +158,7 @@ def tile_moe_bdx_mlp_relu_kernel(
                     rounded[e, s, b] = x
                     if b % 2 == 1:
                         turn(e, s, b // 2)
+                        sign_quarter(e, s, b // 2)
 
         def paired(tile):
             return tile[:].rearrange("p (u c d) -> p u c d", u=2, d=2)
@@ -164,16 +166,17 @@ def tile_moe_bdx_mlp_relu_kernel(
         def saved(e, s):
             return a_sb[e, s][:].rearrange("p (u d) c -> p u c d", u=2)
 
-        def signs(e):
-            for s in range(PASSES):
-                if (e, s) in SIGN_ON_SCALAR:
-                    sign_of[e, s] = ring.tile([P, 4 * C], BF16, name="sign", bufs=2)
-                    nc.scalar.activation(paired(sign_of[e, s]), saved(e, s), ACT.Sign)
+        def sign_quarter(e, u, h):
+            if e in SIGN_ON_SCALAR:
+                if (u, h) == (0, 0):
+                    sign_of[e] = ring.tile([P, 4 * C], BF16, name="sign", bufs=2)
+                cols = slice(h * HALF, (h + 1) * HALF)
+                nc.scalar.activation(paired(sign_of[e])[:, u, cols, :], saved(e, LAST)[:, u, cols, :], ACT.Sign)
 
         def make_mask(e, s):
             mask_of[e, s] = made_on_vector(4 * C, BF16, "mask")
-            if (e, s) in SIGN_ON_SCALAR:
-                nc.vector.tensor_scalar(out=mask_of[e, s][:], in0=sign_of[e, s][:], scalar1=0.0, scalar2=None, op0=ALU.max)
+            if s == LAST and e in SIGN_ON_SCALAR:
+                nc.vector.tensor_scalar(out=mask_of[e, s][:], in0=sign_of[e][:], scalar1=0.0, scalar2=None, op0=ALU.max)
             else:
                 nc.vector.tensor_scalar(out=paired(mask_of[e, s]), in0=saved(e, s), scalar1=0.0, scalar2=None, op0=ALU.is_gt)
 
@@ -242,7 +245,6 @@ def tile_moe_bdx_mlp_relu_kernel(
                 gather_bytes(e + 3)
             if e + 1 < E:
                 first_product(e + 1)
-                signs(e + 1)
                 make_mask(e + 1, 0)
             quantise(e, 1)
             second_product(e)

@@ -26,7 +26,8 @@ BLOCKS = C // P
 HALF = C // 2
 LIST_COL = 16
 LAST = PASSES - 1
-SIGN_ON_SCALAR = (1, 2, 3)
+EARLY = 2
+SIGN_ON_SCALAR = (1, 2, 3, 4)
 OUT_PIECES = (512, 512, 256, 256)
 
 
@@ -44,9 +45,10 @@ def tile_moe_bdx_mlp_relu_kernel(
         pos2_sb = keep.tile([P, T // LIST_COL], U16, name="pos2_sb")
         dy_w = keep.tile([P, T], I32, name="dy_w", align_bytes=64)
         dy_s = keep.tile([P, T], U8, name="dy_s", align_bytes=64)
-        w2_s_first = keep.tile([P, H], U8, name="w2_s_first", align_bytes=64)
-        w2_s_rest = keep.tile([P, (E - 1) * H], U8, name="w2_s_rest", align_bytes=64)
-        w2_s = [w2_s_first[:]] + [w2_s_rest[:, e * H : (e + 1) * H] for e in range(E - 1)]
+        w2_s_first = keep.tile([P, EARLY * H], U8, name="w2_s_first", align_bytes=64)
+        w2_s_rest = keep.tile([P, (E - EARLY) * H], U8, name="w2_s_rest", align_bytes=64)
+        w2_s = [w2_s_first[:, e * H : (e + 1) * H] for e in range(EARLY)]
+        w2_s = w2_s + [w2_s_rest[:, e * H : (e + 1) * H] for e in range(E - EARLY)]
         w1_s = keep.tile([P, E * PASSES * K], U8, name="w1_s", align_bytes=64)
         w1_w = keep.tile([P, E * PASSES * 2 * K], U8, name="w1_w", align_bytes=64)
         w2_w = [keep.tile([P, 2 * H], U8, name="w2_w%d" % e, align_bytes=64) for e in range(E)]
@@ -55,14 +57,13 @@ def tile_moe_bdx_mlp_relu_kernel(
         gate_rows = keep.tile([P, P], F32, name="gate_rows")
         gate_col = keep.tile([P, S // P], F32, name="gate_col")
         dx = keep.tile([P, S], F32, name="dx")
-        first_half = keep.tile([P, T], F32, name="first_half")
 
         nc.gpsimd.memset(dy_s[:].bitcast(I32), 0)
         make_identity(nc, ident[:])
 
         def load_a(e, s):
             rows = a[s * PASS : (s + 1) * PASS, e * C : (e + 1) * C]
-            a_sb[e, s] = ring.tile([P, 4, C], F32, name="a_sb", bufs=8)
+            a_sb[e, s] = ring.tile([P, 4, C], F32, name="a_sb", bufs=6)
             nc.sync.dma_start(a_sb[e, s][:], rows.rearrange("(p t) c -> p t c", t=4))
 
         def load_w2(e):
@@ -81,14 +82,22 @@ def tile_moe_bdx_mlp_relu_kernel(
         nc.sync.dma_start(dy_w[:], dy_words[0].rearrange("p t d -> p (t d)").bitcast(I32))
         load_w2(0)
         nc.sync.dma_start(gate_rows[:], gate.rearrange("h (b m) -> (h b) m", m=P)[0:P, :])
-        load_w2_scales(w2_s_first, 0, 1)
+        load_w2_scales(w2_s_first, 0, EARLY)
         load_a(0, 0)
         load_w2(1)
-        load_w2_scales(w2_s_rest, 1, E)
         load_a(0, 1)
         load_a(1, 1)
         load_a(1, 0)
         load_w2(2)
+        load_w2_scales(w2_s_rest, EARLY, E)
+        load_a(2, 1)
+        load_a(2, 0)
+        load_w2(3)
+        for e in range(3, E):
+            load_a(e, 1)
+            load_a(e, 0)
+            if e + 1 < E:
+                load_w2(e + 1)
         for r in range(4):
             nc.sync.dma_start(
                 w1_s[r:P:32, :].bitcast(I32).rearrange("q (g k) -> q g k", g=E * PASSES),
@@ -98,11 +107,6 @@ def tile_moe_bdx_mlp_relu_kernel(
             w1_w[:].bitcast(I32).rearrange("p (g k) -> p g k", g=E * PASSES),
             w1_words.rearrange("e s p k -> p (e s) k").bitcast(I32),
         )
-        for e in range(2, E):
-            load_a(e, 1)
-            load_a(e, 0)
-            if e + 1 < E:
-                load_w2(e + 1)
         nc.sync.dma_start(pos1_sb[:], pos1)
         nc.sync.dma_start(pos2_sb[:], pos2)
 
@@ -120,7 +124,7 @@ def tile_moe_bdx_mlp_relu_kernel(
         quantised = {}
 
         def made_on_vector(columns, dtype, name):
-            return ring.tile([P, columns], dtype, name=name, tag="made_on_vector", align_bytes=64, bufs=20)
+            return ring.tile([P, columns], dtype, name=name, tag="made_on_vector", align_bytes=64, bufs=26)
 
         def slots(e, c0, c1):
             return offs_sb[:, (e * C + c0) // LIST_COL : (e * C + c1) // LIST_COL]
@@ -202,7 +206,7 @@ def tile_moe_bdx_mlp_relu_kernel(
 
         def quantise(e, s):
             codes = made_on_vector(C, U32, "codes")
-            scales = ring.tile([P, C], U8, name="scales", align_bytes=64, bufs=4)
+            scales = ring.tile([P, C], U8, name="scales", align_bytes=64, bufs=E * PASSES)
             nc.vector.quantize_mx(out=codes[:].bitcast(E5M2X4), scales=scales[:], in_=da_of[e, s][:])
             quantised[e, s] = (codes, scales)
 
@@ -247,8 +251,10 @@ def tile_moe_bdx_mlp_relu_kernel(
                 first_product(e + 1)
                 make_mask(e + 1, 0)
             quantise(e, 1)
+        for e in range(E):
             second_product(e)
 
+        first_half = ring.tile([P, T], F32, name="first_half", tag="a_sb", bufs=6)
         nc.vector.tensor_copy(first_half[:], dx[:].indirect(pos1_sb[:]))
         t0 = 0
         for n, width in enumerate(OUT_PIECES):

@@ -28,7 +28,7 @@ LIST_COL = 16
 LAST = PASSES - 1
 EARLY = 2
 SIGN_ON_SCALAR = (1, 2, 3, 4)
-OUT_PIECES = (512, 512, 256, 256)
+OUT_PIECES = (512, 512, 384, 128)
 
 
 def tile_moe_bdx_mlp_relu_kernel(
@@ -110,7 +110,7 @@ def tile_moe_bdx_mlp_relu_kernel(
         nc.sync.dma_start(pos1_sb[:], pos1)
         nc.sync.dma_start(pos2_sb[:], pos2)
 
-        gate_ps = psum.tile([P, 4 * P], F32, name="gate_ps", tag="turned", bufs=4)
+        gate_ps = psum.tile([P, 4 * P], F32, name="gate_ps", tag="bank", bufs=8)
         nc.tensor.transpose(gate_ps[:, 0:P], gate_rows[:], ident[:])
         nc.scalar.activation(gate_col[:], gate_ps[:, 0 : S // P], ACT.Copy)
 
@@ -139,30 +139,32 @@ def tile_moe_bdx_mlp_relu_kernel(
             for c0 in range(0, C, width):
                 nc.vector.tensor_copy(g_w[e][:, c0 : c0 + width], dy_w[:].bitcast(U32).indirect(slots(e, c0, c0 + width)))
 
-        def first_product(e):
-            for s in range(PASSES):
-                for b in range(BLOCKS):
-                    dh = psum.tile([P, PASS], F32, name="dh", tag="sums", bufs=4)
-                    nc.tensor.matmul_mx(
-                        out=dh[:],
-                        lhsT=g_w[e][:, b * P : (b + 1) * P].bitcast(E5M2X4),
-                        lhsT_scale=g_s[e][:, b * P : (b + 1) * P],
-                        rhs=w2_w[e][:, 2 * s * PASS : 2 * (s + 1) * PASS].bitcast(E2M1X4),
-                        rhs_scale=w2_s[e][:, s * PASS : (s + 1) * PASS],
-                        start=True,
-                        stop=True,
-                    )
-                    x = ring.tile([P, PASS], BF16, name="x", bufs=16)
-                    nc.scalar.activation(
-                        x[:].rearrange("m (u p d) -> m u p d", u=2, d=2),
-                        dh[:].rearrange("m (p u d) -> m u p d", u=2, d=2),
-                        ACT.Copy,
-                        scale=gate_col[:, e * BLOCKS + b : e * BLOCKS + b + 1],
-                    )
-                    rounded[e, s, b] = x
-                    if b % 2 == 1:
-                        turn(e, s, b // 2)
-                        sign_quarter(e, s, b // 2)
+        def first_product(e, s):
+            for b in range(BLOCKS):
+                dh = psum.tile([P, PASS], F32, name="dh", tag="bank", bufs=8)
+                nc.tensor.matmul_mx(
+                    out=dh[:],
+                    lhsT=g_w[e][:, b * P : (b + 1) * P].bitcast(E5M2X4),
+                    lhsT_scale=g_s[e][:, b * P : (b + 1) * P],
+                    rhs=w2_w[e][:, 2 * s * PASS : 2 * (s + 1) * PASS].bitcast(E2M1X4),
+                    rhs_scale=w2_s[e][:, s * PASS : (s + 1) * PASS],
+                    start=True,
+                    stop=True,
+                )
+                x = ring.tile([P, PASS], BF16, name="x", bufs=16)
+                nc.scalar.activation(
+                    x[:].rearrange("m (u p d) -> m u p d", u=2, d=2),
+                    dh[:].rearrange("m (p u d) -> m u p d", u=2, d=2),
+                    ACT.Copy,
+                    scale=gate_col[:, e * BLOCKS + b : e * BLOCKS + b + 1],
+                )
+                rounded[e, s, b] = x
+                if b % 2 == 1:
+                    sign_quarter(e, s, b // 2)
+                if b == 2 and (e, s) != (0, 0):
+                    before = divmod(e * PASSES + s - 1, PASSES)
+                    turn(before[0], before[1], 0)
+                    turn(before[0], before[1], 1)
 
         def paired(tile):
             return tile[:].rearrange("p (u c d) -> p u c d", u=2, d=2)
@@ -185,7 +187,7 @@ def tile_moe_bdx_mlp_relu_kernel(
                 nc.vector.tensor_scalar(out=paired(mask_of[e, s]), in0=saved(e, s), scalar1=0.0, scalar2=None, op0=ALU.is_gt)
 
         def turn(e, s, h):
-            turned = psum.tile([P, 4 * P], F32, name="turned", tag="turned", bufs=4)
+            turned = psum.tile([P, 4 * P], F32, name="turned", tag="bank", bufs=8)
             for j in range(2):
                 words = rounded[e, s, 2 * h + j][:].bitcast(F32)
                 for u in range(2):
@@ -211,7 +213,7 @@ def tile_moe_bdx_mlp_relu_kernel(
             quantised[e, s] = (codes, scales)
 
         def second_product(e):
-            acc = psum.tile([P, C], F32, name="acc", tag="sums", bufs=4)
+            acc = psum.tile([P, C], F32, name="acc", tag="bank", bufs=8)
             for s in range(PASSES):
                 codes, scales = quantised[e, s]
                 g = e * PASSES + s
@@ -232,23 +234,30 @@ def tile_moe_bdx_mlp_relu_kernel(
         gather_bytes(0)
         gather_bytes(1)
         gather_words(0)
-        first_product(0)
+        first_product(0, 0)
+        first_product(0, 1)
         gather_words(1)
         gather_bytes(2)
+        gather_words(2)
         make_mask(0, 0)
         for e in range(E):
-            if e + 2 < E:
-                gather_words(e + 2)
+            if e + 3 < E:
+                gather_bytes(e + 3)
             masked(e, 0, 0)
             masked(e, 0, 1)
             make_mask(e, 1)
             quantise(e, 0)
+            if e + 1 < E:
+                first_product(e + 1, 0)
+            else:
+                turn(e, 1, 0)
+                turn(e, 1, 1)
             masked(e, 1, 0)
             masked(e, 1, 1)
             if e + 3 < E:
-                gather_bytes(e + 3)
+                gather_words(e + 3)
             if e + 1 < E:
-                first_product(e + 1)
+                first_product(e + 1, 1)
                 make_mask(e + 1, 0)
             quantise(e, 1)
         for e in range(E):

@@ -122,6 +122,7 @@ def tile_moe_bdx_mlp_relu_kernel(
         turned_of = {}
         da_of = {}
         quantised = {}
+        acc_of = {}
 
         def made_on_vector(columns, dtype, name):
             return ring.tile([P, columns], dtype, name=name, tag="made_on_vector", align_bytes=64, bufs=26)
@@ -213,12 +214,12 @@ def tile_moe_bdx_mlp_relu_kernel(
             quantised[e, s] = (codes, scales)
 
         def second_product(e):
-            acc = psum.tile([P, C], F32, name="acc", tag="bank", bufs=8)
+            acc_of[e] = psum.tile([P, C], F32, name="acc", tag="bank", bufs=8)
             for s in range(PASSES):
                 codes, scales = quantised[e, s]
                 g = e * PASSES + s
                 nc.tensor.matmul_mx(
-                    out=acc[:],
+                    out=acc_of[e][:],
                     lhsT=w1_w[:, 2 * g * K : 2 * (g + 1) * K].bitcast(E2M1X4),
                     lhsT_scale=w1_s[:, g * K : (g + 1) * K],
                     rhs=codes[:].bitcast(E5M2X4),
@@ -226,10 +227,12 @@ def tile_moe_bdx_mlp_relu_kernel(
                     start=(s == 0),
                     stop=(s == PASSES - 1),
                 )
-            if e + 1 < E:
-                nc.scalar.copy(dx[:, e * C : (e + 1) * C], acc[:])
+
+        def copy_out(e):
+            if e < E - 1:
+                nc.scalar.copy(dx[:, e * C : (e + 1) * C], acc_of[e][:])
             else:
-                nc.vector.tensor_copy(dx[:, e * C : (e + 1) * C], acc[:])
+                nc.vector.tensor_copy(dx[:, e * C : (e + 1) * C], acc_of[e][:])
 
         gather_bytes(0)
         gather_bytes(1)
@@ -240,28 +243,38 @@ def tile_moe_bdx_mlp_relu_kernel(
         gather_bytes(2)
         gather_words(2)
         make_mask(0, 0)
-        for e in range(E):
+        for e in range(E - 1):
             if e + 3 < E:
                 gather_bytes(e + 3)
             masked(e, 0, 0)
             masked(e, 0, 1)
             make_mask(e, 1)
             quantise(e, 0)
-            if e + 1 < E:
-                first_product(e + 1, 0)
-            else:
-                turn(e, 1, 0)
-                turn(e, 1, 1)
+            first_product(e + 1, 0)
             masked(e, 1, 0)
             masked(e, 1, 1)
             if e + 3 < E:
                 gather_words(e + 3)
-            if e + 1 < E:
-                first_product(e + 1, 1)
-                make_mask(e + 1, 0)
+            if e + 2 == E:
+                second_product(0)
+                second_product(1)
+            first_product(e + 1, 1)
+            make_mask(e + 1, 0)
+            if e + 2 == E:
+                make_mask(e + 1, 1)
             quantise(e, 1)
-        for e in range(E):
+        last = E - 1
+        turn(last, 1, 0)
+        turn(last, 1, 1)
+        for s in range(PASSES):
+            masked(last, s, 0)
+            masked(last, s, 1)
+        for s in range(PASSES):
+            quantise(last, s)
+        for e in range(2, E):
             second_product(e)
+        for e in range(E):
+            copy_out(e)
 
         first_half = ring.tile([P, T], F32, name="first_half", tag="a_sb", bufs=6)
         nc.vector.tensor_copy(first_half[:], dx[:].indirect(pos1_sb[:]))

@@ -26,8 +26,13 @@ BLOCKS = C // P
 HALF = C // 2
 LIST_COL = 16
 LAST = PASSES - 1
-EARLY = 2
 SIGN_ON_SCALAR = (1, 2, 3, 4)
+SECOND_FIRST = (2, 3, 4)
+SIGN_FIRST = 15
+SIGN_NEXT = 18
+SIGN_SPREAD = 7
+LIFT_WIDTH = {1: C, 2: C, 3: 3 * C // 4}
+LIFT = 2.0**23
 OUT_PIECES = (512, 512, 384, 128)
 
 
@@ -45,13 +50,13 @@ def tile_moe_bdx_mlp_relu_kernel(
         pos2_sb = keep.tile([P, T // LIST_COL], U16, name="pos2_sb")
         dy_w = keep.tile([P, T], I32, name="dy_w", align_bytes=64)
         dy_s = keep.tile([P, T], U8, name="dy_s", align_bytes=64)
-        w2_s_first = keep.tile([P, EARLY * H], U8, name="w2_s_first", align_bytes=64)
-        w2_s_rest = keep.tile([P, (E - EARLY) * H], U8, name="w2_s_rest", align_bytes=64)
-        w2_s = [w2_s_first[:, e * H : (e + 1) * H] for e in range(EARLY)]
-        w2_s = w2_s + [w2_s_rest[:, e * H : (e + 1) * H] for e in range(E - EARLY)]
+        w2_s_pair = [keep.tile([P, 2 * H], U8, name="w2_s%d" % n, align_bytes=64) for n in range(E // 2)]
+        w2_s = [w2_s_pair[e // 2][:, (e % 2) * H : (e % 2 + 1) * H] for e in range(E)]
         w1_s = keep.tile([P, E * PASSES * K], U8, name="w1_s", align_bytes=64)
         w1_w = keep.tile([P, E * PASSES * 2 * K], U8, name="w1_w", align_bytes=64)
         w2_w = [keep.tile([P, 2 * H], U8, name="w2_w%d" % e, align_bytes=64) for e in range(E)]
+        g_s = {}
+        g_w = {}
         a_sb = {}
         ident = keep.tile([P, P], F32, name="ident")
         gate_rows = keep.tile([P, P], F32, name="gate_rows")
@@ -69,44 +74,50 @@ def tile_moe_bdx_mlp_relu_kernel(
         def load_w2(e):
             nc.sync.dma_start(w2_w[e][:].bitcast(I32), w2_words[e, 0].bitcast(I32))
 
-        def load_w2_scales(plane, e0, e1):
+        def load_w2_scales(e0):
+            plane = w2_s_pair[e0 // 2]
+            e1 = e0 + 2
             for r in range(4):
                 nc.sync.dma_start(
                     plane[r:P:32, :].bitcast(I32).rearrange("q (e i) -> q e i", i=H // 4),
                     w2_scales[e0:e1, 0, r:16:4, :].bitcast(I32).rearrange("e q i -> q e i"),
                 )
 
+        def load_w1():
+            for r in range(4):
+                nc.sync.dma_start(
+                    w1_s[r:P:32, :].bitcast(I32).rearrange("q (g k) -> q g k", g=E * PASSES),
+                    w1_scales.rearrange("e s f k -> (e s) f k")[:, r:16:4, :].bitcast(I32).rearrange("g q k -> q g k"),
+                )
+            nc.sync.dma_start(
+                w1_w[:].bitcast(I32).rearrange("p (g k) -> p g k", g=E * PASSES),
+                w1_words.rearrange("e s p k -> p (e s) k").bitcast(I32),
+            )
+
         nc.sync.dma_start(offs_sb[:], offs)
+        load_w2(0)
         for r in range(4):
             nc.sync.dma_start(dy_s[r:P:32, :].bitcast(I32), dy_scales[0, r:16:4, :].bitcast(I32))
         nc.sync.dma_start(dy_w[:], dy_words[0].rearrange("p t d -> p (t d)").bitcast(I32))
-        load_w2(0)
         nc.sync.dma_start(gate_rows[:], gate.rearrange("h (b m) -> (h b) m", m=P)[0:P, :])
-        load_w2_scales(w2_s_first, 0, EARLY)
+        load_w2_scales(0)
         load_a(0, 0)
         load_w2(1)
         load_a(0, 1)
-        load_a(1, 1)
         load_a(1, 0)
+        load_a(1, 1)
         load_w2(2)
-        load_w2_scales(w2_s_rest, EARLY, E)
-        load_a(2, 1)
-        load_a(2, 0)
-        load_w2(3)
-        for e in range(3, E):
-            load_a(e, 1)
-            load_a(e, 0)
+        load_w2_scales(2)
+        for e in range(2, E):
+            first = 1 if e in SECOND_FIRST else 0
+            load_a(e, first)
+            if e + 1 == E:
+                load_w1()
+            load_a(e, 1 - first)
             if e + 1 < E:
                 load_w2(e + 1)
-        for r in range(4):
-            nc.sync.dma_start(
-                w1_s[r:P:32, :].bitcast(I32).rearrange("q (g k) -> q g k", g=E * PASSES),
-                w1_scales.rearrange("e s f k -> (e s) f k")[:, r:16:4, :].bitcast(I32).rearrange("g q k -> q g k"),
-            )
-        nc.sync.dma_start(
-            w1_w[:].bitcast(I32).rearrange("p (g k) -> p g k", g=E * PASSES),
-            w1_words.rearrange("e s p k -> p (e s) k").bitcast(I32),
-        )
+            if e + 1 == 4:
+                load_w2_scales(4)
         nc.sync.dma_start(pos1_sb[:], pos1)
         nc.sync.dma_start(pos2_sb[:], pos2)
 
@@ -114,31 +125,40 @@ def tile_moe_bdx_mlp_relu_kernel(
         nc.tensor.transpose(gate_ps[:, 0:P], gate_rows[:], ident[:])
         nc.scalar.activation(gate_col[:], gate_ps[:, 0 : S // P], ACT.Copy)
 
-        g_w = {}
-        g_s = {}
         rounded = {}
-        sign_of = {}
+        signed = {}
+        signed_width = {}
         mask_of = {}
         turned_of = {}
         da_of = {}
-        quantised = {}
+        codes_of = {}
+        scales_of = {}
         acc_of = {}
 
         def made_on_vector(columns, dtype, name):
             return ring.tile([P, columns], dtype, name=name, tag="made_on_vector", align_bytes=64, bufs=26)
 
+        def made_on_scalar(name):
+            return ring.tile([P, 4 * C], BF16, name=name, tag="made_on_scalar", bufs=8)
+
         def slots(e, c0, c1):
             return offs_sb[:, (e * C + c0) // LIST_COL : (e * C + c1) // LIST_COL]
 
-        def gather_bytes(e):
-            g_s[e] = made_on_vector(C, U8, "g_s")
-            nc.vector.tensor_copy(g_s[e][:], dy_s[:].indirect(slots(e, 0, C)))
+        def gather_bytes(e, c0, c1):
+            if c0 == 0:
+                g_s[e] = made_on_vector(C, U8, "g_s")
+            nc.vector.tensor_copy(g_s[e][:, c0:c1], dy_s[:].indirect(slots(e, c0, c1)))
 
-        def gather_words(e):
-            g_w[e] = made_on_vector(C, U32, "g_w")
-            width = HALF if e == 0 else C
-            for c0 in range(0, C, width):
-                nc.vector.tensor_copy(g_w[e][:, c0 : c0 + width], dy_w[:].bitcast(U32).indirect(slots(e, c0, c0 + width)))
+        def gather_words(e, c0, c1):
+            if c0 == 0:
+                g_w[e] = made_on_vector(C, U32, "g_w")
+            nc.vector.tensor_copy(g_w[e][:, c0:c1], dy_w[:].bitcast(U32).indirect(slots(e, c0, c1)))
+
+        later_gathers = [(gather_words, 3), (gather_bytes, 4), (gather_words, 4), (gather_bytes, 5), (gather_words, 5)]
+
+        def gather(n):
+            if n < len(later_gathers):
+                later_gathers[n][0](later_gathers[n][1], 0, C)
 
         def first_product(e, s):
             for b in range(BLOCKS):
@@ -152,135 +172,161 @@ def tile_moe_bdx_mlp_relu_kernel(
                     start=True,
                     stop=True,
                 )
-                x = ring.tile([P, PASS], BF16, name="x", bufs=16)
+                if b == 0:
+                    unit_rounded = made_on_scalar("x")
+                x = unit_rounded[:, b * PASS : (b + 1) * PASS]
                 nc.scalar.activation(
-                    x[:].rearrange("m (u p d) -> m u p d", u=2, d=2),
+                    x.rearrange("m (u p d) -> m u p d", u=2, d=2),
                     dh[:].rearrange("m (p u d) -> m u p d", u=2, d=2),
                     ACT.Copy,
                     scale=gate_col[:, e * BLOCKS + b : e * BLOCKS + b + 1],
                 )
                 rounded[e, s, b] = x
-                if b % 2 == 1:
-                    sign_quarter(e, s, b // 2)
+                for n in range(4 * len(SIGN_ON_SCALAR)):
+                    if sign_place(n) == BLOCKS * (PASSES * e + s) + b:
+                        sign_quarter(SIGN_ON_SCALAR[n // 4], LAST, n % 4 // 2, n % 2)
                 if b == 2 and (e, s) != (0, 0):
                     before = divmod(e * PASSES + s - 1, PASSES)
                     turn(before[0], before[1], 0)
                     turn(before[0], before[1], 1)
 
         def paired(tile):
-            return tile[:].rearrange("p (u c d) -> p u c d", u=2, d=2)
+            return tile.rearrange("p (u c d) -> p u c d", u=2, d=2)
 
         def saved(e, s):
             return a_sb[e, s][:].rearrange("p (u d) c -> p u c d", u=2)
 
-        def sign_quarter(e, u, h):
-            if e in SIGN_ON_SCALAR:
-                if (u, h) == (0, 0):
-                    sign_of[e] = ring.tile([P, 4 * C], BF16, name="sign", bufs=2)
-                cols = slice(h * HALF, (h + 1) * HALF)
-                nc.scalar.activation(paired(sign_of[e])[:, u, cols, :], saved(e, LAST)[:, u, cols, :], ACT.Sign)
+        def sign_place(n):
+            return SIGN_FIRST if n < 4 else SIGN_NEXT + (n - 4) * SIGN_SPREAD // 4
+
+        def sign_quarter(e, s, u, h):
+            if (u, h) == (0, 0):
+                signed[e, s] = made_on_scalar("sign")[:]
+                signed_width[e, s] = C
+            cols = slice(h * HALF, (h + 1) * HALF)
+            nc.scalar.activation(paired(signed[e, s])[:, u, cols, :], saved(e, s)[:, u, cols, :], ACT.Sign)
+
+        def lift(e, s, tile, width):
+            signed[e, s] = tile
+            signed_width[e, s] = width
+            nc.gpsimd.tensor_scalar(
+                out=paired(tile)[:, :, 0:width, :], in0=saved(e, s)[:, :, 0:width, :], scalar1=LIFT, scalar2=0.0, op0=ALU.mult, op1=ALU.add
+            )
 
         def make_mask(e, s):
             mask_of[e, s] = made_on_vector(4 * C, BF16, "mask")
-            if s == LAST and e in SIGN_ON_SCALAR:
-                nc.vector.tensor_scalar(out=mask_of[e, s][:], in0=sign_of[e][:], scalar1=0.0, scalar2=None, op0=ALU.max)
-            else:
-                nc.vector.tensor_scalar(out=paired(mask_of[e, s]), in0=saved(e, s), scalar1=0.0, scalar2=None, op0=ALU.is_gt)
+            mask = paired(mask_of[e, s][:])
+            width = signed_width.get((e, s), 0)
+            if width < C:
+                nc.vector.tensor_scalar(out=mask[:, :, width:C, :], in0=saved(e, s)[:, :, width:C, :], scalar1=0.0, scalar2=None, op0=ALU.is_gt)
+            if width > 0:
+                nc.vector.tensor_scalar(
+                    out=mask[:, :, 0:width, :], in0=paired(signed[e, s])[:, :, 0:width, :], scalar1=0.0, scalar2=None, op0=ALU.is_gt
+                )
 
         def turn(e, s, h):
             turned = psum.tile([P, 4 * P], F32, name="turned", tag="bank", bufs=8)
             for j in range(2):
-                words = rounded[e, s, 2 * h + j][:].bitcast(F32)
+                words = rounded[e, s, 2 * h + j].bitcast(F32)
                 for u in range(2):
                     at = (2 * u + j) * P
                     nc.tensor.transpose(turned[:, at : at + P], words[:, u * P : (u + 1) * P], ident[:])
             turned_of[e, s, h] = turned
 
-        def masked(e, s, h):
-            if h == 0:
-                da_of[e, s] = made_on_vector(4 * C, BF16, "da")
+        def masked(e, s, apart=False):
             mask = mask_of[e, s][:].rearrange("p (u c d) -> p c u d", u=2, d=2)
-            nc.vector.tensor_tensor(
-                da_of[e, s][:, 4 * h * HALF : 4 * (h + 1) * HALF].rearrange("p (c u d) -> p c u d", u=2, d=2),
-                turned_of[e, s, h][:].bitcast(BF16).rearrange("p (u c d) -> p c u d", u=2, d=2),
-                mask[:, h * HALF : (h + 1) * HALF],
-                ALU.mult,
-            )
+            for h in range(2):
+                if apart:
+                    da_of[e, s, h] = made_on_vector(4 * HALF, BF16, "da")[:]
+                elif h == 0:
+                    da_of[e, s] = made_on_vector(4 * C, BF16, "da")[:]
+                if not apart:
+                    da_of[e, s, h] = da_of[e, s][:, 4 * h * HALF : 4 * (h + 1) * HALF]
+                nc.vector.tensor_tensor(
+                    da_of[e, s, h].rearrange("p (c u d) -> p c u d", u=2, d=2),
+                    turned_of[e, s, h][:].bitcast(BF16).rearrange("p (u c d) -> p c u d", u=2, d=2),
+                    mask[:, h * HALF : (h + 1) * HALF],
+                    ALU.mult,
+                )
 
-        def quantise(e, s):
-            codes = made_on_vector(C, U32, "codes")
-            scales = ring.tile([P, C], U8, name="scales", align_bytes=64, bufs=E * PASSES)
-            nc.vector.quantize_mx(out=codes[:].bitcast(E5M2X4), scales=scales[:], in_=da_of[e, s][:])
-            quantised[e, s] = (codes, scales)
+        def quantise(e, s, apart=False):
+            codes_of[e, s] = made_on_vector(C, U32, "codes")
+            scales_of[e, s] = ring.tile([P, C], U8, name="scales", align_bytes=64, bufs=E * PASSES)
+            if apart:
+                for h in range(2):
+                    cols = slice(h * HALF, (h + 1) * HALF)
+                    nc.vector.quantize_mx(out=codes_of[e, s][:, cols].bitcast(E5M2X4), scales=scales_of[e, s][:, cols], in_=da_of[e, s, h])
+            else:
+                nc.vector.quantize_mx(out=codes_of[e, s][:].bitcast(E5M2X4), scales=scales_of[e, s][:], in_=da_of[e, s])
 
         def second_product(e):
             acc_of[e] = psum.tile([P, C], F32, name="acc", tag="bank", bufs=8)
             for s in range(PASSES):
-                codes, scales = quantised[e, s]
                 g = e * PASSES + s
                 nc.tensor.matmul_mx(
                     out=acc_of[e][:],
                     lhsT=w1_w[:, 2 * g * K : 2 * (g + 1) * K].bitcast(E2M1X4),
                     lhsT_scale=w1_s[:, g * K : (g + 1) * K],
-                    rhs=codes[:].bitcast(E5M2X4),
-                    rhs_scale=scales[:],
+                    rhs=codes_of[e, s][:].bitcast(E5M2X4),
+                    rhs_scale=scales_of[e, s][:],
                     start=(s == 0),
                     stop=(s == PASSES - 1),
                 )
 
         def copy_out(e):
-            if e < E - 1:
-                nc.scalar.copy(dx[:, e * C : (e + 1) * C], acc_of[e][:])
-            else:
-                nc.vector.tensor_copy(dx[:, e * C : (e + 1) * C], acc_of[e][:])
+            nc.scalar.copy(dx[:, e * C : (e + 1) * C], acc_of[e][:])
 
-        gather_bytes(0)
-        gather_bytes(1)
-        gather_words(0)
+        gather_bytes(0, 0, C)
+        gather_bytes(1, 0, HALF)
+        gather_words(0, 0, HALF)
+        gather_words(0, HALF, C)
+        gather_bytes(1, HALF, C)
+        gather_words(1, 0, C)
+        gather_bytes(2, 0, C)
+        gather_words(2, 0, C)
+        gather_bytes(3, 0, C)
+        lift(0, 0, keep.tile([P, 4 * C], BF16, name="lifted")[:], C)
         first_product(0, 0)
         first_product(0, 1)
-        gather_words(1)
-        gather_bytes(2)
-        gather_words(2)
         make_mask(0, 0)
-        for e in range(E - 1):
-            if e + 3 < E:
-                gather_bytes(e + 3)
-            masked(e, 0, 0)
-            masked(e, 0, 1)
-            make_mask(e, 1)
-            quantise(e, 0)
-            first_product(e + 1, 0)
-            masked(e, 1, 0)
-            masked(e, 1, 1)
-            if e + 3 < E:
-                gather_words(e + 3)
-            if e + 2 == E:
+        last = E - 1
+        for e in range(E):
+            if e < last:
+                first_product(e + 1, 0)
+            else:
                 second_product(0)
                 second_product(1)
-            first_product(e + 1, 1)
-            make_mask(e + 1, 0)
-            if e + 2 == E:
-                make_mask(e + 1, 1)
-            quantise(e, 1)
-        last = E - 1
-        turn(last, 1, 0)
-        turn(last, 1, 1)
-        for s in range(PASSES):
-            masked(last, s, 0)
-            masked(last, s, 1)
-        for s in range(PASSES):
-            quantise(last, s)
-        for e in range(2, E):
+                turn(last, 1, 0)
+                second_product(2)
+                turn(last, 1, 1)
+            masked(e, 0)
+            make_mask(e, 1)
+            quantise(e, 0)
+            if e + 1 in LIFT_WIDTH:
+                if (e, 1) in signed:
+                    lift(e + 1, 0, signed[e, 1], LIFT_WIDTH[e + 1])
+                else:
+                    lift(e + 1, 0, a_sb[e, 1][:, 0:2, :].rearrange("p t c -> p (t c)").bitcast(BF16), LIFT_WIDTH[e + 1])
+            gather(2 * e)
+            gather(2 * e + 1)
+            if e < last:
+                first_product(e + 1, 1)
+            masked(e, 1, e == last)
+            if e < last:
+                make_mask(e + 1, 0)
+            quantise(e, 1, e == last)
+        for e in range(3, E):
             second_product(e)
         for e in range(E):
             copy_out(e)
 
         first_half = ring.tile([P, T], F32, name="first_half", tag="a_sb", bufs=6)
-        nc.vector.tensor_copy(first_half[:], dx[:].indirect(pos1_sb[:]))
+        for t0 in range(0, T, T // 2):
+            cols = pos1_sb[:, t0 // LIST_COL : (t0 + T // 2) // LIST_COL]
+            nc.vector.tensor_copy(first_half[:, t0 : t0 + T // 2], dx[:].indirect(cols))
         t0 = 0
-        for n, width in enumerate(OUT_PIECES):
-            piece = keep.tile([P, width], F32, name="piece%d" % n)
+        for width in OUT_PIECES:
+            piece = ring.tile([P, width], F32, name="piece", tag="made_on_scalar", bufs=8)
             cols = pos2_sb[:, t0 // LIST_COL : (t0 + width) // LIST_COL]
             nc.vector.tensor_tensor(piece[:], dx[:].indirect(cols), first_half[:, t0 : t0 + width], ALU.add)
             nc.sync.dma_start(out[:, t0 : t0 + width], piece[:])

@@ -26,12 +26,10 @@ BLOCKS = C // P
 HALF = C // 2
 LIST_COL = 16
 LAST = PASSES - 1
-SIGN_ON_SCALAR = (1, 2, 3, 4)
+SIGN_PLACES = {(1, 1): (14, 14, 15, 15), (2, 1): (17, 18, 19, 20), (3, 1): (25, 26, 27, 28), (4, 1): (33, 34, 35, 36)}
 SECOND_FIRST = (2, 3, 4)
-SIGN_FIRST = 15
-SIGN_NEXT = 18
-SIGN_SPREAD = 7
-LIFT_WIDTH = {1: C, 2: C, 3: 3 * C // 4}
+LIFT_WIDTH = {2: C, 3: 3 * C // 4}
+A_ROOMS = 6
 LIFT = 2.0**23
 OUT_PIECES = (512, 512, 384, 128)
 
@@ -68,7 +66,7 @@ def tile_moe_bdx_mlp_relu_kernel(
 
         def load_a(e, s):
             rows = a[s * PASS : (s + 1) * PASS, e * C : (e + 1) * C]
-            a_sb[e, s] = ring.tile([P, 4, C], F32, name="a_sb", bufs=6)
+            a_sb[e, s] = keep.tile([P, 4, C], F32, name="a_sb", tag="a_room%d" % (len(a_sb) % A_ROOMS))
             nc.sync.dma_start(a_sb[e, s][:], rows.rearrange("(p t) c -> p t c", t=4))
 
         def load_w2(e):
@@ -145,14 +143,16 @@ def tile_moe_bdx_mlp_relu_kernel(
             return offs_sb[:, (e * C + c0) // LIST_COL : (e * C + c1) // LIST_COL]
 
         def gather_bytes(e, c0, c1):
-            if c0 == 0:
-                g_s[e] = made_on_vector(C, U8, "g_s")
-            nc.vector.tensor_copy(g_s[e][:, c0:c1], dy_s[:].indirect(slots(e, c0, c1)))
+            gathered = made_on_vector(c1 - c0, U8, "g_s")
+            nc.vector.tensor_copy(gathered[:], dy_s[:].indirect(slots(e, c0, c1)))
+            for c in range(c0, c1, P):
+                g_s[e, c // P] = gathered[:, c - c0 : c - c0 + P]
 
         def gather_words(e, c0, c1):
-            if c0 == 0:
-                g_w[e] = made_on_vector(C, U32, "g_w")
-            nc.vector.tensor_copy(g_w[e][:, c0:c1], dy_w[:].bitcast(U32).indirect(slots(e, c0, c1)))
+            gathered = made_on_vector(c1 - c0, U32, "g_w")
+            nc.vector.tensor_copy(gathered[:], dy_w[:].bitcast(U32).indirect(slots(e, c0, c1)))
+            for c in range(c0, c1, P):
+                g_w[e, c // P] = gathered[:, c - c0 : c - c0 + P]
 
         later_gathers = [(gather_words, 3), (gather_bytes, 4), (gather_words, 4), (gather_bytes, 5), (gather_words, 5)]
 
@@ -165,8 +165,8 @@ def tile_moe_bdx_mlp_relu_kernel(
                 dh = psum.tile([P, PASS], F32, name="dh", tag="bank", bufs=8)
                 nc.tensor.matmul_mx(
                     out=dh[:],
-                    lhsT=g_w[e][:, b * P : (b + 1) * P].bitcast(E5M2X4),
-                    lhsT_scale=g_s[e][:, b * P : (b + 1) * P],
+                    lhsT=g_w[e, b].bitcast(E5M2X4),
+                    lhsT_scale=g_s[e, b],
                     rhs=w2_w[e][:, 2 * s * PASS : 2 * (s + 1) * PASS].bitcast(E2M1X4),
                     rhs_scale=w2_s[e][:, s * PASS : (s + 1) * PASS],
                     start=True,
@@ -182,9 +182,10 @@ def tile_moe_bdx_mlp_relu_kernel(
                     scale=gate_col[:, e * BLOCKS + b : e * BLOCKS + b + 1],
                 )
                 rounded[e, s, b] = x
-                for n in range(4 * len(SIGN_ON_SCALAR)):
-                    if sign_place(n) == BLOCKS * (PASSES * e + s) + b:
-                        sign_quarter(SIGN_ON_SCALAR[n // 4], LAST, n % 4 // 2, n % 2)
+                for unit, places in SIGN_PLACES.items():
+                    for n, place in enumerate(places):
+                        if place == BLOCKS * (PASSES * e + s) + b:
+                            sign_quarter(unit[0], unit[1], n % 2, n // 2)
                 if b == 2 and (e, s) != (0, 0):
                     before = divmod(e * PASSES + s - 1, PASSES)
                     turn(before[0], before[1], 0)
@@ -196,13 +197,10 @@ def tile_moe_bdx_mlp_relu_kernel(
         def saved(e, s):
             return a_sb[e, s][:].rearrange("p (u d) c -> p u c d", u=2)
 
-        def sign_place(n):
-            return SIGN_FIRST if n < 4 else SIGN_NEXT + (n - 4) * SIGN_SPREAD // 4
-
         def sign_quarter(e, s, u, h):
             if (u, h) == (0, 0):
                 signed[e, s] = made_on_scalar("sign")[:]
-                signed_width[e, s] = C
+                signed_width[e, s] = HALF * len(SIGN_PLACES[e, s]) // 2
             cols = slice(h * HALF, (h + 1) * HALF)
             nc.scalar.activation(paired(signed[e, s])[:, u, cols, :], saved(e, s)[:, u, cols, :], ACT.Sign)
 
@@ -285,12 +283,24 @@ def tile_moe_bdx_mlp_relu_kernel(
         gather_bytes(2, 0, C)
         gather_words(2, 0, C)
         gather_bytes(3, 0, C)
-        lift(0, 0, keep.tile([P, 4 * C], BF16, name="lifted")[:], C)
+        lifted = keep.tile([P, 4 * C], BF16, name="lifted")[:]
+        lift(0, 0, lifted, C)
         first_product(0, 0)
         first_product(0, 1)
         make_mask(0, 0)
+        make_mask(0, 1)
+        lift(1, 0, lifted, C)
+        first_product(1, 0)
+        masked(0, 0)
+        masked(0, 1)
+        gather(0)
+        gather(1)
+        first_product(1, 1)
+        make_mask(1, 0)
+        quantise(0, 0)
+        quantise(0, 1)
         last = E - 1
-        for e in range(E):
+        for e in range(1, E):
             if e < last:
                 first_product(e + 1, 0)
             else:
@@ -303,16 +313,12 @@ def tile_moe_bdx_mlp_relu_kernel(
             make_mask(e, 1)
             quantise(e, 0)
             if e + 1 in LIFT_WIDTH:
-                if (e, 1) in signed:
-                    lift(e + 1, 0, signed[e, 1], LIFT_WIDTH[e + 1])
-                else:
-                    lift(e + 1, 0, a_sb[e, 1][:, 0:2, :].rearrange("p t c -> p (t c)").bitcast(BF16), LIFT_WIDTH[e + 1])
+                lift(e + 1, 0, signed[e, 1], LIFT_WIDTH[e + 1])
+            masked(e, 1, e == last)
             gather(2 * e)
             gather(2 * e + 1)
             if e < last:
                 first_product(e + 1, 1)
-            masked(e, 1, e == last)
-            if e < last:
                 make_mask(e + 1, 0)
             quantise(e, 1, e == last)
         for e in range(3, E):
@@ -320,7 +326,7 @@ def tile_moe_bdx_mlp_relu_kernel(
         for e in range(E):
             copy_out(e)
 
-        first_half = ring.tile([P, T], F32, name="first_half", tag="a_sb", bufs=6)
+        first_half = keep.tile([P, T], F32, name="first_half", tag="a_room0")
         for t0 in range(0, T, T // 2):
             cols = pos1_sb[:, t0 // LIST_COL : (t0 + T // 2) // LIST_COL]
             nc.vector.tensor_copy(first_half[:, t0 : t0 + T // 2], dx[:].indirect(cols))

@@ -26,9 +26,11 @@ BLOCKS = C // P
 HALF = C // 2
 LIST_COL = 16
 LAST = PASSES - 1
-SIGN_PLACES = {(1, 1): (14, 14, 15, 15), (2, 1): (17, 18, 19, 20), (3, 1): (25, 26, 27, 28), (4, 1): (33, 34, 35, 36)}
-SECOND_FIRST = (2, 3, 4)
-LIFT_WIDTH = {2: C, 3: 3 * C // 4}
+SIGN_PLACES = {(1, 1): (14, 14, 15, 15), (2, 1): (17, 18, 19, 20), (3, 1): (24, 25, 26, 27), (5, 1): (43, 44, 45, 46)}
+SECOND_FIRST = (2, 3)
+LIFT_WIDTH = {3: C, 4: C, 5: 3 * C // 4}
+TURN_LAG = {0: 9, 1: 8}
+TURN_LAG_LATER = 7
 A_ROOMS = 6
 LIFT = 2.0**23
 OUT_PIECES = (512, 512, 384, 128)
@@ -109,9 +111,9 @@ def tile_moe_bdx_mlp_relu_kernel(
         for e in range(2, E):
             first = 1 if e in SECOND_FIRST else 0
             load_a(e, first)
+            load_a(e, 1 - first)
             if e + 1 == E:
                 load_w1()
-            load_a(e, 1 - first)
             if e + 1 < E:
                 load_w2(e + 1)
             if e + 1 == 4:
@@ -154,12 +156,6 @@ def tile_moe_bdx_mlp_relu_kernel(
             for c in range(c0, c1, P):
                 g_w[e, c // P] = gathered[:, c - c0 : c - c0 + P]
 
-        later_gathers = [(gather_words, 3), (gather_bytes, 4), (gather_words, 4), (gather_bytes, 5), (gather_words, 5)]
-
-        def gather(n):
-            if n < len(later_gathers):
-                later_gathers[n][0](later_gathers[n][1], 0, C)
-
         def first_product(e, s):
             for b in range(BLOCKS):
                 dh = psum.tile([P, PASS], F32, name="dh", tag="bank", bufs=8)
@@ -186,10 +182,10 @@ def tile_moe_bdx_mlp_relu_kernel(
                     for n, place in enumerate(places):
                         if place == BLOCKS * (PASSES * e + s) + b:
                             sign_quarter(unit[0], unit[1], n % 2, n // 2)
-                if b == 2 and (e, s) != (0, 0):
-                    before = divmod(e * PASSES + s - 1, PASSES)
-                    turn(before[0], before[1], 0)
-                    turn(before[0], before[1], 1)
+                for unit in range(E * PASSES - 1):
+                    if BLOCKS * unit + TURN_LAG.get(unit, TURN_LAG_LATER) == BLOCKS * (PASSES * e + s) + b:
+                        turn(unit // PASSES, unit % PASSES, 0)
+                        turn(unit // PASSES, unit % PASSES, 1)
 
         def paired(tile):
             return tile.rearrange("p (u c d) -> p u c d", u=2, d=2)
@@ -291,36 +287,53 @@ def tile_moe_bdx_mlp_relu_kernel(
         make_mask(0, 1)
         lift(1, 0, lifted, C)
         first_product(1, 0)
+        first_product(1, 1)
         masked(0, 0)
         masked(0, 1)
-        gather(0)
-        gather(1)
-        first_product(1, 1)
+        gather_words(3, 0, C)
         make_mask(1, 0)
         quantise(0, 0)
         quantise(0, 1)
         last = E - 1
-        for e in range(1, E):
-            if e < last:
-                first_product(e + 1, 0)
-            else:
-                second_product(0)
-                second_product(1)
-                turn(last, 1, 0)
-                second_product(2)
-                turn(last, 1, 1)
+        first_product(2, 0)
+        first_product(2, 1)
+        masked(1, 0)
+        make_mask(1, 1)
+        quantise(1, 0)
+        lift(2, 0, signed[1, 1], C)
+        masked(1, 1)
+        gather_bytes(4, 0, C)
+        gather_words(4, 0, C)
+        make_mask(2, 1)
+        make_mask(2, 0)
+        quantise(1, 1)
+        room = signed[2, 0]
+        for e in range(2, last):
+            first_product(e + 1, 0)
+            first_product(e + 1, 1)
+            lift(e + 1, 0, room, LIFT_WIDTH[e + 1])
             masked(e, 0)
-            make_mask(e, 1)
+            masked(e, 1)
+            if e == 2:
+                gather_bytes(5, 0, C)
+            if e == 3:
+                gather_words(5, 0, C)
+            if e + 1 < last:
+                make_mask(e + 1, 1)
+            make_mask(e + 1, 0)
             quantise(e, 0)
-            if e + 1 in LIFT_WIDTH:
-                lift(e + 1, 0, signed[e, 1], LIFT_WIDTH[e + 1])
-            masked(e, 1, e == last)
-            gather(2 * e)
-            gather(2 * e + 1)
-            if e < last:
-                first_product(e + 1, 1)
-                make_mask(e + 1, 0)
-            quantise(e, 1, e == last)
+            quantise(e, 1)
+            room = da_of[e, 0]
+        second_product(0)
+        second_product(1)
+        turn(last, 1, 0)
+        second_product(2)
+        turn(last, 1, 1)
+        masked(last, 0)
+        make_mask(last, 1)
+        quantise(last, 0)
+        masked(last, 1, True)
+        quantise(last, 1, True)
         for e in range(3, E):
             second_product(e)
         for e in range(E):

@@ -25,15 +25,17 @@ PASSES = H // PASS
 BLOCKS = C // P
 HALF = C // 2
 LIST_COL = 16
-LAST = PASSES - 1
-SIGN_PLACES = {(1, 1): (14, 14, 15, 15), (2, 1): (17, 18, 19, 20), (3, 1): (24, 25, 26, 27), (5, 1): (43, 44, 45, 46)}
-SECOND_FIRST = (2, 3)
-LIFT_WIDTH = {3: C, 4: C, 5: 3 * C // 4}
-TURN_LAG = {0: 9, 1: 8}
-TURN_LAG_LATER = 7
 A_ROOMS = 6
 LIFT = 2.0**23
-OUT_PIECES = (512, 512, 384, 128)
+SIGN_FIRST_BLOCK = 14
+SIGN_DISTANCE = 7
+SIGN_QUARTERS = 3
+LAST_SIGN_QUARTERS = 2
+FIRST_PIECE = 128
+TURN_LAG = 7
+LAST_LIFT_WIDTH = 3 * C // 4
+OWN_PIECE = 192
+OUT_PIECES = (160, 352, 352, 352, 128)
 
 
 def tile_moe_bdx_mlp_relu_kernel(
@@ -55,13 +57,12 @@ def tile_moe_bdx_mlp_relu_kernel(
         w1_s = keep.tile([P, E * PASSES * K], U8, name="w1_s", align_bytes=64)
         w1_w = keep.tile([P, E * PASSES * 2 * K], U8, name="w1_w", align_bytes=64)
         w2_w = [keep.tile([P, 2 * H], U8, name="w2_w%d" % e, align_bytes=64) for e in range(E)]
-        g_s = {}
-        g_w = {}
-        a_sb = {}
         ident = keep.tile([P, P], F32, name="ident")
         gate_rows = keep.tile([P, P], F32, name="gate_rows")
         gate_col = keep.tile([P, S // P], F32, name="gate_col")
-        dx = keep.tile([P, S], F32, name="dx")
+        lifted_second = keep.tile([P, 4 * C], BF16, name="lifted_second", tag="dx")
+        lifted = keep.tile([P, 4 * C], BF16, name="lifted")
+        a_sb = {}
 
         nc.gpsimd.memset(dy_s[:].bitcast(I32), 0)
         make_identity(nc, ident[:])
@@ -76,11 +77,10 @@ def tile_moe_bdx_mlp_relu_kernel(
 
         def load_w2_scales(e0):
             plane = w2_s_pair[e0 // 2]
-            e1 = e0 + 2
             for r in range(4):
                 nc.sync.dma_start(
                     plane[r:P:32, :].bitcast(I32).rearrange("q (e i) -> q e i", i=H // 4),
-                    w2_scales[e0:e1, 0, r:16:4, :].bitcast(I32).rearrange("e q i -> q e i"),
+                    w2_scales[e0 : e0 + 2, 0, r:16:4, :].bitcast(I32).rearrange("e q i -> q e i"),
                 )
 
         def load_w1():
@@ -95,97 +95,55 @@ def tile_moe_bdx_mlp_relu_kernel(
             )
 
         nc.sync.dma_start(offs_sb[:], offs)
-        load_w2(0)
+        nc.sync.dma_start(gate_rows[:], gate.rearrange("h (b m) -> (h b) m", m=P)[0:P, :])
         for r in range(4):
             nc.sync.dma_start(dy_s[r:P:32, :].bitcast(I32), dy_scales[0, r:16:4, :].bitcast(I32))
         nc.sync.dma_start(dy_w[:], dy_words[0].rearrange("p t d -> p (t d)").bitcast(I32))
-        nc.sync.dma_start(gate_rows[:], gate.rearrange("h (b m) -> (h b) m", m=P)[0:P, :])
+        load_w2(0)
         load_w2_scales(0)
-        load_a(0, 0)
-        load_w2(1)
-        load_a(0, 1)
-        load_a(1, 0)
-        load_a(1, 1)
-        load_w2(2)
-        load_w2_scales(2)
-        for e in range(2, E):
-            first = 1 if e in SECOND_FIRST else 0
-            load_a(e, first)
-            load_a(e, 1 - first)
-            if e + 1 == E:
-                load_w1()
-            if e + 1 < E:
+        for e in range(E):
+            load_a(e, 0)
+            if e == 0:
+                load_w2(1)
+            load_a(e, 1)
+            if 0 < e < E - 1:
                 load_w2(e + 1)
-            if e + 1 == 4:
-                load_w2_scales(4)
+            if e % 2 == 1 and e < E - 1:
+                load_w2_scales(e + 1)
+        load_w1()
         nc.sync.dma_start(pos1_sb[:], pos1)
         nc.sync.dma_start(pos2_sb[:], pos2)
 
-        gate_ps = psum.tile([P, 4 * P], F32, name="gate_ps", tag="bank", bufs=8)
-        nc.tensor.transpose(gate_ps[:, 0:P], gate_rows[:], ident[:])
-        nc.scalar.activation(gate_col[:], gate_ps[:, 0 : S // P], ACT.Copy)
-
-        rounded = {}
-        signed = {}
-        signed_width = {}
-        mask_of = {}
-        turned_of = {}
-        da_of = {}
-        codes_of = {}
-        scales_of = {}
-        acc_of = {}
+        def bank(name):
+            return psum.tile([P, PASS], F32, name=name, tag="bank", bufs=4)
 
         def made_on_vector(columns, dtype, name):
             return ring.tile([P, columns], dtype, name=name, tag="made_on_vector", align_bytes=64, bufs=26)
 
-        def made_on_scalar(name):
-            return ring.tile([P, 4 * C], BF16, name=name, tag="made_on_scalar", bufs=8)
+        def made_on_scalar(columns, dtype, name):
+            return ring.tile([P, columns], dtype, name=name, tag="made_on_scalar", bufs=8)
+
+        gate_ps = bank("gate_ps")
+        nc.tensor.transpose(gate_ps[:, 0:P], gate_rows[:], ident[:])
+        nc.scalar.activation(gate_col[:], gate_ps[:, 0 : S // P], ACT.Copy)
+
+        g_s, g_w, rounded, signed, mask_of, turned_of, da_of, codes_of, scales_of = {}, {}, {}, {}, {}, {}, {}, {}, {}
+        blocks_done = []
 
         def slots(e, c0, c1):
             return offs_sb[:, (e * C + c0) // LIST_COL : (e * C + c1) // LIST_COL]
 
-        def gather_bytes(e, c0, c1):
+        def gather_bytes(e, c0=0, c1=C):
             gathered = made_on_vector(c1 - c0, U8, "g_s")
             nc.vector.tensor_copy(gathered[:], dy_s[:].indirect(slots(e, c0, c1)))
             for c in range(c0, c1, P):
                 g_s[e, c // P] = gathered[:, c - c0 : c - c0 + P]
 
-        def gather_words(e, c0, c1):
+        def gather_words(e, c0=0, c1=C):
             gathered = made_on_vector(c1 - c0, U32, "g_w")
             nc.vector.tensor_copy(gathered[:], dy_w[:].bitcast(U32).indirect(slots(e, c0, c1)))
             for c in range(c0, c1, P):
                 g_w[e, c // P] = gathered[:, c - c0 : c - c0 + P]
-
-        def first_product(e, s):
-            for b in range(BLOCKS):
-                dh = psum.tile([P, PASS], F32, name="dh", tag="bank", bufs=8)
-                nc.tensor.matmul_mx(
-                    out=dh[:],
-                    lhsT=g_w[e, b].bitcast(E5M2X4),
-                    lhsT_scale=g_s[e, b],
-                    rhs=w2_w[e][:, 2 * s * PASS : 2 * (s + 1) * PASS].bitcast(E2M1X4),
-                    rhs_scale=w2_s[e][:, s * PASS : (s + 1) * PASS],
-                    start=True,
-                    stop=True,
-                )
-                if b == 0:
-                    unit_rounded = made_on_scalar("x")
-                x = unit_rounded[:, b * PASS : (b + 1) * PASS]
-                nc.scalar.activation(
-                    x.rearrange("m (u p d) -> m u p d", u=2, d=2),
-                    dh[:].rearrange("m (p u d) -> m u p d", u=2, d=2),
-                    ACT.Copy,
-                    scale=gate_col[:, e * BLOCKS + b : e * BLOCKS + b + 1],
-                )
-                rounded[e, s, b] = x
-                for unit, places in SIGN_PLACES.items():
-                    for n, place in enumerate(places):
-                        if place == BLOCKS * (PASSES * e + s) + b:
-                            sign_quarter(unit[0], unit[1], n % 2, n // 2)
-                for unit in range(E * PASSES - 1):
-                    if BLOCKS * unit + TURN_LAG.get(unit, TURN_LAG_LATER) == BLOCKS * (PASSES * e + s) + b:
-                        turn(unit // PASSES, unit % PASSES, 0)
-                        turn(unit // PASSES, unit % PASSES, 1)
 
         def paired(tile):
             return tile.rearrange("p (u c d) -> p u c d", u=2, d=2)
@@ -193,160 +151,177 @@ def tile_moe_bdx_mlp_relu_kernel(
         def saved(e, s):
             return a_sb[e, s][:].rearrange("p (u d) c -> p u c d", u=2)
 
-        def sign_quarter(e, s, u, h):
-            if (u, h) == (0, 0):
-                signed[e, s] = made_on_scalar("sign")[:]
-                signed_width[e, s] = HALF * len(SIGN_PLACES[e, s]) // 2
-            cols = slice(h * HALF, (h + 1) * HALF)
-            nc.scalar.activation(paired(signed[e, s])[:, u, cols, :], saved(e, s)[:, u, cols, :], ACT.Sign)
+        def sign_quarter(e, quarter):
+            if quarter == 0:
+                signed[e] = made_on_scalar(4 * C, BF16, "sign")
+            cols = slice(quarter * P, (quarter + 1) * P)
+            nc.scalar.activation(paired(signed[e][:])[:, :, cols, :], saved(e, 1)[:, :, cols, :], ACT.Sign)
 
-        def lift(e, s, tile, width):
-            signed[e, s] = tile
-            signed_width[e, s] = width
+        def sign_count(e):
+            return LAST_SIGN_QUARTERS if e == E - 1 else SIGN_QUARTERS
+
+        def first_sign_block(e):
+            return SIGN_FIRST_BLOCK + SIGN_DISTANCE * (e - 1)
+
+        def turn(e, s, order):
+            turned = psum.tile([P, 2 * PASS], F32, name="turned", bufs=2)
+            for b in order:
+                words = rounded[e, s][:, b * PASS : (b + 1) * PASS].bitcast(F32)
+                for u in range(2):
+                    at = (b // 2) * PASS + (2 * u + b % 2) * P
+                    nc.tensor.transpose(turned[:, at : at + P], words[:, u * P : (u + 1) * P], ident[:])
+            for h in range(2):
+                turned_of[e, s, h] = turned[:, h * PASS : (h + 1) * PASS]
+
+        def next_block():
+            k = len(blocks_done)
+            blocks_done.append(k)
+            e, s, b = k // (PASSES * BLOCKS), k // BLOCKS % PASSES, k % BLOCKS
+            dh = bank("dh")
+            nc.tensor.matmul_mx(
+                out=dh[:],
+                lhsT=g_w[e, b].bitcast(E5M2X4),
+                lhsT_scale=g_s[e, b],
+                rhs=w2_w[e][:, 2 * s * PASS : 2 * (s + 1) * PASS].bitcast(E2M1X4),
+                rhs_scale=w2_s[e][:, s * PASS : (s + 1) * PASS],
+                start=True,
+                stop=True,
+            )
+            if b == 0:
+                rounded[e, s] = made_on_scalar(4 * C, BF16, "x")
+            nc.scalar.activation(
+                rounded[e, s][:, b * PASS : (b + 1) * PASS].rearrange("m (u p d) -> m u p d", u=2, d=2),
+                dh[:].rearrange("m (p u d) -> m u p d", u=2, d=2),
+                ACT.Copy,
+                scale=gate_col[:, e * BLOCKS + b : e * BLOCKS + b + 1],
+            )
+            for signed_e in range(1, E):
+                if 0 <= k - first_sign_block(signed_e) < sign_count(signed_e):
+                    sign_quarter(signed_e, k - first_sign_block(signed_e))
+            if k >= TURN_LAG and (k - TURN_LAG) % BLOCKS == 0:
+                unit = (k - TURN_LAG) // BLOCKS
+                turn(unit // PASSES, unit % PASSES, reversed(range(BLOCKS)))
+
+        def blocks_through(k):
+            while len(blocks_done) <= k:
+                next_block()
+
+        def lift(e, s, tile, c0, c1):
             nc.gpsimd.tensor_scalar(
-                out=paired(tile)[:, :, 0:width, :], in0=saved(e, s)[:, :, 0:width, :], scalar1=LIFT, scalar2=0.0, op0=ALU.mult, op1=ALU.add
+                out=paired(tile[:])[:, :, c0:c1, :], in0=saved(e, s)[:, :, c0:c1, :], scalar1=LIFT, scalar2=0.0, op0=ALU.mult, op1=ALU.add
             )
 
-        def make_mask(e, s):
+        def make_mask(e, s, source=None, width=0):
             mask_of[e, s] = made_on_vector(4 * C, BF16, "mask")
             mask = paired(mask_of[e, s][:])
-            width = signed_width.get((e, s), 0)
             if width < C:
                 nc.vector.tensor_scalar(out=mask[:, :, width:C, :], in0=saved(e, s)[:, :, width:C, :], scalar1=0.0, scalar2=None, op0=ALU.is_gt)
             if width > 0:
-                nc.vector.tensor_scalar(
-                    out=mask[:, :, 0:width, :], in0=paired(signed[e, s])[:, :, 0:width, :], scalar1=0.0, scalar2=None, op0=ALU.is_gt
-                )
+                nc.vector.tensor_scalar(out=mask[:, :, 0:width, :], in0=paired(source[:])[:, :, 0:width, :], scalar1=0.0, scalar2=None, op0=ALU.is_gt)
 
-        def turn(e, s, h):
-            turned = psum.tile([P, 4 * P], F32, name="turned", tag="bank", bufs=8)
-            for j in range(2):
-                words = rounded[e, s, 2 * h + j].bitcast(F32)
-                for u in range(2):
-                    at = (2 * u + j) * P
-                    nc.tensor.transpose(turned[:, at : at + P], words[:, u * P : (u + 1) * P], ident[:])
-            turned_of[e, s, h] = turned
-
-        def masked(e, s, apart=False):
+        def masked_half(e, s, h, da):
             mask = mask_of[e, s][:].rearrange("p (u c d) -> p c u d", u=2, d=2)
-            for h in range(2):
-                if apart:
-                    da_of[e, s, h] = made_on_vector(4 * HALF, BF16, "da")[:]
-                elif h == 0:
-                    da_of[e, s] = made_on_vector(4 * C, BF16, "da")[:]
-                if not apart:
-                    da_of[e, s, h] = da_of[e, s][:, 4 * h * HALF : 4 * (h + 1) * HALF]
-                nc.vector.tensor_tensor(
-                    da_of[e, s, h].rearrange("p (c u d) -> p c u d", u=2, d=2),
-                    turned_of[e, s, h][:].bitcast(BF16).rearrange("p (u c d) -> p c u d", u=2, d=2),
-                    mask[:, h * HALF : (h + 1) * HALF],
-                    ALU.mult,
-                )
+            nc.vector.tensor_tensor(
+                da.rearrange("p (c u d) -> p c u d", u=2, d=2),
+                turned_of[e, s, h].bitcast(BF16).rearrange("p (u c d) -> p c u d", u=2, d=2),
+                mask[:, h * HALF : (h + 1) * HALF],
+                ALU.mult,
+            )
 
-        def quantise(e, s, apart=False):
-            codes_of[e, s] = made_on_vector(C, U32, "codes")
-            scales_of[e, s] = ring.tile([P, C], U8, name="scales", align_bytes=64, bufs=E * PASSES)
-            if apart:
-                for h in range(2):
-                    cols = slice(h * HALF, (h + 1) * HALF)
-                    nc.vector.quantize_mx(out=codes_of[e, s][:, cols].bitcast(E5M2X4), scales=scales_of[e, s][:, cols], in_=da_of[e, s, h])
-            else:
-                nc.vector.quantize_mx(out=codes_of[e, s][:].bitcast(E5M2X4), scales=scales_of[e, s][:], in_=da_of[e, s])
+        def masked(e, s):
+            blocks_through(BLOCKS * (PASSES * e + s) + TURN_LAG)
+            da_of[e, s] = made_on_vector(4 * C, BF16, "da")
+            for h in range(2):
+                masked_half(e, s, h, da_of[e, s][:, 4 * h * HALF : 4 * (h + 1) * HALF])
+
+        def quantise(key, da, width):
+            codes_of[key] = made_on_vector(width, U32, "codes")
+            scales_of[key] = ring.tile([P, width], U8, name="scales", align_bytes=64, bufs=E * PASSES + 1)
+            nc.vector.quantize_mx(out=codes_of[key][:].bitcast(E5M2X4), scales=scales_of[key][:], in_=da)
+
+        def second_pass(acc, e, s, codes, scales):
+            g = e * PASSES + s
+            nc.tensor.matmul_mx(
+                out=acc,
+                lhsT=w1_w[:, 2 * g * K : 2 * (g + 1) * K].bitcast(E2M1X4),
+                lhsT_scale=w1_s[:, g * K : (g + 1) * K],
+                rhs=codes.bitcast(E5M2X4),
+                rhs_scale=scales,
+                start=(s == 0),
+                stop=(s == PASSES - 1),
+            )
 
         def second_product(e):
-            acc_of[e] = psum.tile([P, C], F32, name="acc", tag="bank", bufs=8)
+            acc = bank("acc")
             for s in range(PASSES):
-                g = e * PASSES + s
-                nc.tensor.matmul_mx(
-                    out=acc_of[e][:],
-                    lhsT=w1_w[:, 2 * g * K : 2 * (g + 1) * K].bitcast(E2M1X4),
-                    lhsT_scale=w1_s[:, g * K : (g + 1) * K],
-                    rhs=codes_of[e, s][:].bitcast(E5M2X4),
-                    rhs_scale=scales_of[e, s][:],
-                    start=(s == 0),
-                    stop=(s == PASSES - 1),
-                )
+                second_pass(acc[:], e, s, codes_of[e, s][:], scales_of[e, s][:])
+            nc.scalar.copy(dx[:, e * C : (e + 1) * C], acc[:])
 
-        def copy_out(e):
-            nc.scalar.copy(dx[:, e * C : (e + 1) * C], acc_of[e][:])
-
-        gather_bytes(0, 0, C)
-        gather_bytes(1, 0, HALF)
-        gather_words(0, 0, HALF)
-        gather_words(0, HALF, C)
-        gather_bytes(1, HALF, C)
-        gather_words(1, 0, C)
-        gather_bytes(2, 0, C)
-        gather_words(2, 0, C)
-        gather_bytes(3, 0, C)
-        lifted = keep.tile([P, 4 * C], BF16, name="lifted")[:]
-        lift(0, 0, lifted, C)
-        first_product(0, 0)
-        first_product(0, 1)
-        make_mask(0, 0)
-        make_mask(0, 1)
-        lift(1, 0, lifted, C)
-        first_product(1, 0)
-        first_product(1, 1)
-        masked(0, 0)
-        masked(0, 1)
-        gather_words(3, 0, C)
-        make_mask(1, 0)
-        quantise(0, 0)
-        quantise(0, 1)
         last = E - 1
-        first_product(2, 0)
-        first_product(2, 1)
-        masked(1, 0)
-        make_mask(1, 1)
-        quantise(1, 0)
-        lift(2, 0, signed[1, 1], C)
-        masked(1, 1)
-        gather_bytes(4, 0, C)
-        gather_words(4, 0, C)
-        make_mask(2, 1)
-        make_mask(2, 0)
-        quantise(1, 1)
-        room = signed[2, 0]
-        for e in range(2, last):
-            first_product(e + 1, 0)
-            first_product(e + 1, 1)
-            lift(e + 1, 0, room, LIFT_WIDTH[e + 1])
+        gather_bytes(0)
+        gather_words(0, 0, FIRST_PIECE)
+        gather_words(0, FIRST_PIECE, C)
+        for e in range(1, 4):
+            gather_bytes(e)
+            gather_words(e)
+        lift(0, 0, lifted, 0, C)
+        lift(0, 1, lifted_second, 0, C)
+        make_mask(0, 0, lifted, C)
+        make_mask(0, 1, lifted_second, C)
+        dx = keep.tile([P, S], F32, name="dx", tag="dx")
+        for e in range(last):
+            width = LAST_LIFT_WIDTH if e + 1 == last else C
+            lift(e + 1, 0, lifted, 0, width)
             masked(e, 0)
             masked(e, 1)
-            if e == 2:
-                gather_bytes(5, 0, C)
-            if e == 3:
-                gather_words(5, 0, C)
             if e + 1 < last:
-                make_mask(e + 1, 1)
-            make_mask(e + 1, 0)
-            quantise(e, 0)
-            quantise(e, 1)
-            room = da_of[e, 0]
-        second_product(0)
-        second_product(1)
-        turn(last, 1, 0)
-        second_product(2)
-        turn(last, 1, 1)
-        masked(last, 0)
-        make_mask(last, 1)
-        quantise(last, 0)
-        masked(last, 1, True)
-        quantise(last, 1, True)
-        for e in range(3, E):
-            second_product(e)
-        for e in range(E):
-            copy_out(e)
+                blocks_through(first_sign_block(e + 1))
+                lift(e + 1, 1, signed[e + 1], SIGN_QUARTERS * P, C)
+                if e % 2 == 0:
+                    gather_bytes(4 + e // 2)
+                else:
+                    gather_words(4 + e // 2)
+            quantise((e, 0), da_of[e, 0][:], C)
+            quantise((e, 1), da_of[e, 1][:], C)
+            make_mask(e + 1, 0, lifted, width)
+            blocks_through(first_sign_block(e + 1) + sign_count(e + 1) - 1)
+            make_mask(e + 1, 1, signed[e + 1], C if e + 1 < last else LAST_SIGN_QUARTERS * P)
 
-        first_half = keep.tile([P, T], F32, name="first_half", tag="a_room0")
-        for t0 in range(0, T, T // 2):
-            cols = pos1_sb[:, t0 // LIST_COL : (t0 + T // 2) // LIST_COL]
-            nc.vector.tensor_copy(first_half[:, t0 : t0 + T // 2], dx[:].indirect(cols))
-        t0 = 0
-        for width in OUT_PIECES:
-            piece = ring.tile([P, width], F32, name="piece", tag="made_on_scalar", bufs=8)
-            cols = pos2_sb[:, t0 // LIST_COL : (t0 + width) // LIST_COL]
-            nc.vector.tensor_tensor(piece[:], dx[:].indirect(cols), first_half[:, t0 : t0 + width], ALU.add)
+        masked(last, 0)
+        turn(last, 1, range(BLOCKS))
+        for e in range(last):
+            second_product(e)
+        halves = [made_on_vector(4 * HALF, BF16, "da")]
+        masked_half(last, 1, 0, halves[0][:])
+        quantise((last, 0), da_of[last, 0][:], C)
+        halves.append(made_on_vector(4 * HALF, BF16, "da"))
+        masked_half(last, 1, 1, halves[1][:])
+        accs = []
+        for h in range(2):
+            accs.append(bank("acc"))
+            cols = slice(h * HALF, (h + 1) * HALF)
+            second_pass(accs[h][:, 0:HALF], last, 0, codes_of[last, 0][:, cols], scales_of[last, 0][:, cols])
+        for h in range(2):
+            quantise((last, 1, h), halves[h][:], HALF)
+            second_pass(accs[h][:, 0:HALF], last, 1, codes_of[last, 1, h][:], scales_of[last, 1, h][:])
+        nc.scalar.copy(dx[:, last * C : last * C + HALF], accs[0][:, 0:HALF])
+        nc.vector.tensor_copy(dx[:, last * C + HALF : S], accs[1][:, 0:HALF])
+
+        def list_columns(t0, width):
+            return slice(t0 // LIST_COL, (t0 + width) // LIST_COL)
+
+        def add_second_and_store(t0, width, by_first):
+            piece = made_on_vector(width, F32, "piece")
+            nc.vector.tensor_tensor(piece[:], dx[:].indirect(pos2_sb[:, list_columns(t0, width)]), by_first[:], ALU.add)
             nc.sync.dma_start(out[:, t0 : t0 + width], piece[:])
+
+        own_first = made_on_vector(OWN_PIECE, F32, "own_first")
+        nc.vector.tensor_copy(own_first[:], dx[:].indirect(pos1_sb[:, list_columns(0, OWN_PIECE)]))
+        t0 = OWN_PIECE
+        for n, width in enumerate(OUT_PIECES):
+            by_first = made_on_scalar(width, F32, "by_first")
+            nc.scalar.activation(by_first[:], dx[:].indirect(pos1_sb[:, list_columns(t0, width)]), ACT.Copy)
+            add_second_and_store(t0, width, by_first)
+            if n == 0:
+                add_second_and_store(0, OWN_PIECE, own_first)
             t0 = t0 + width

@@ -27,13 +27,10 @@ HALF = C // 2
 LIST_COL = 16
 A_ROOMS = 6
 LIFT = 2.0**23
-SIGN_FIRST_BLOCK = 14
-SIGN_DISTANCE = 7
-SIGN_QUARTERS = 3
-LAST_SIGN_QUARTERS = 2
+SIGN_AFTER = {1: (15, 15, 15, 15), 2: (20, 20, 21, 21), 3: (26, 26, 27, 27), 5: (41, 42, 43)}
 FIRST_PIECE = 128
 TURN_LAG = 7
-LAST_LIFT_WIDTH = 3 * C // 4
+LIFT_WIDTH = (C, C, 7 * C // 8, 7 * C // 8, 7 * C // 8, C // 2)
 OWN_PIECE = 192
 OUT_PIECES = (160, 352, 352, 352, 128)
 
@@ -60,7 +57,7 @@ def tile_moe_bdx_mlp_relu_kernel(
         ident = keep.tile([P, P], F32, name="ident")
         gate_rows = keep.tile([P, P], F32, name="gate_rows")
         gate_col = keep.tile([P, S // P], F32, name="gate_col")
-        lifted_second = keep.tile([P, 4 * C], BF16, name="lifted_second", tag="dx")
+        dx = keep.tile([P, S], F32, name="dx")
         lifted = keep.tile([P, 4 * C], BF16, name="lifted")
         a_sb = {}
 
@@ -70,7 +67,9 @@ def tile_moe_bdx_mlp_relu_kernel(
         def load_a(e, s):
             rows = a[s * PASS : (s + 1) * PASS, e * C : (e + 1) * C]
             a_sb[e, s] = keep.tile([P, 4, C], F32, name="a_sb", tag="a_room%d" % (len(a_sb) % A_ROOMS))
-            nc.sync.dma_start(a_sb[e, s][:], rows.rearrange("(p t) c -> p t c", t=4))
+            step = 2 if (e, s) == (0, 0) else 4
+            for t in range(0, 4, step):
+                nc.sync.dma_start(a_sb[e, s][:, t : t + step, :], rows.rearrange("(p t) c -> p t c", t=4)[:, t : t + step, :])
 
         def load_w2(e):
             nc.sync.dma_start(w2_w[e][:].bitcast(I32), w2_words[e, 0].bitcast(I32))
@@ -157,12 +156,6 @@ def tile_moe_bdx_mlp_relu_kernel(
             cols = slice(quarter * P, (quarter + 1) * P)
             nc.scalar.activation(paired(signed[e][:])[:, :, cols, :], saved(e, 1)[:, :, cols, :], ACT.Sign)
 
-        def sign_count(e):
-            return LAST_SIGN_QUARTERS if e == E - 1 else SIGN_QUARTERS
-
-        def first_sign_block(e):
-            return SIGN_FIRST_BLOCK + SIGN_DISTANCE * (e - 1)
-
         def turn(e, s, order):
             turned = psum.tile([P, 2 * PASS], F32, name="turned", bufs=2)
             for b in order:
@@ -195,9 +188,10 @@ def tile_moe_bdx_mlp_relu_kernel(
                 ACT.Copy,
                 scale=gate_col[:, e * BLOCKS + b : e * BLOCKS + b + 1],
             )
-            for signed_e in range(1, E):
-                if 0 <= k - first_sign_block(signed_e) < sign_count(signed_e):
-                    sign_quarter(signed_e, k - first_sign_block(signed_e))
+            for signed_e, places in SIGN_AFTER.items():
+                for quarter, place in enumerate(places):
+                    if place == k:
+                        sign_quarter(signed_e, quarter)
             if k >= TURN_LAG and (k - TURN_LAG) % BLOCKS == 0:
                 unit = (k - TURN_LAG) // BLOCKS
                 turn(unit // PASSES, unit % PASSES, reversed(range(BLOCKS)))
@@ -259,36 +253,49 @@ def tile_moe_bdx_mlp_relu_kernel(
 
         last = E - 1
         gather_bytes(0)
+        gather_bytes(1, 0, HALF)
         gather_words(0, 0, FIRST_PIECE)
         gather_words(0, FIRST_PIECE, C)
-        for e in range(1, 4):
-            gather_bytes(e)
-            gather_words(e)
-        lift(0, 0, lifted, 0, C)
-        lift(0, 1, lifted_second, 0, C)
-        make_mask(0, 0, lifted, C)
-        make_mask(0, 1, lifted_second, C)
-        dx = keep.tile([P, S], F32, name="dx", tag="dx")
+        gather_bytes(1, HALF, C)
+        gather_words(1)
+        gather_bytes(2)
+        gather_words(2)
+        gather_bytes(3)
+        in_window = {0: [(gather_words, 3), (gather_bytes, 4)], 1: [(gather_words, 4)], 2: [(gather_bytes, 5)], 3: [(gather_words, 5)], 4: []}
+        scaled = lifted
+        for u in range(2):
+            nc.gpsimd.tensor_scalar(
+                out=paired(scaled[:])[:, u], in0=saved(0, 0)[:, u], scalar1=LIFT, scalar2=0.0, op0=ALU.mult, op1=ALU.add
+            )
+        make_mask(0, 0, scaled, C)
+        make_mask(0, 1)
+        room = lifted
         for e in range(last):
-            width = LAST_LIFT_WIDTH if e + 1 == last else C
-            lift(e + 1, 0, lifted, 0, width)
+            scaled = room
+            lift(e + 1, 0, scaled, 0, LIFT_WIDTH[e + 1])
+            between = 0 if e == 0 else 1
             masked(e, 0)
+            for gather, of in in_window[e][:between]:
+                gather(of)
             masked(e, 1)
-            if e + 1 < last:
-                blocks_through(first_sign_block(e + 1))
-                lift(e + 1, 1, signed[e + 1], SIGN_QUARTERS * P, C)
-                if e % 2 == 0:
-                    gather_bytes(4 + e // 2)
-                else:
-                    gather_words(4 + e // 2)
-            quantise((e, 0), da_of[e, 0][:], C)
+            for gather, of in in_window[e][between:]:
+                gather(of)
+            if e + 1 in SIGN_AFTER:
+                quantise((e, 0), da_of[e, 0][:], C)
+                make_mask(e + 1, 0, scaled, LIFT_WIDTH[e + 1])
+                blocks_through(SIGN_AFTER[e + 1][-1])
+                make_mask(e + 1, 1, signed[e + 1], P * len(SIGN_AFTER[e + 1]))
+                room = signed[e + 1]
+            else:
+                make_mask(e + 1, 1)
+                make_mask(e + 1, 0, scaled, LIFT_WIDTH[e + 1])
+                quantise((e, 0), da_of[e, 0][:], C)
+                room = da_of[e, 0]
             quantise((e, 1), da_of[e, 1][:], C)
-            make_mask(e + 1, 0, lifted, width)
-            blocks_through(first_sign_block(e + 1) + sign_count(e + 1) - 1)
-            make_mask(e + 1, 1, signed[e + 1], C if e + 1 < last else LAST_SIGN_QUARTERS * P)
 
         masked(last, 0)
-        turn(last, 1, range(BLOCKS))
+        blocks_through(E * PASSES * BLOCKS - 1)
+        turn(last, 1, (1, 0, 3, 2))
         for e in range(last):
             second_product(e)
         halves = [made_on_vector(4 * HALF, BF16, "da")]

@@ -27,10 +27,12 @@ HALF = C // 2
 LIST_COL = 16
 A_ROOMS = 6
 LIFT = 2.0**23
-SIGN_AFTER = {1: (15, 15, 15, 15), 2: (20, 20, 21, 21), 3: (26, 26, 27, 27), 5: (41, 42, 43)}
+SIGN_AFTER = {(1, 1): 15, (2, 1): 22, (5, 0): 42}
 FIRST_PIECE = 128
-TURN_LAG = 7
-LIFT_WIDTH = (C, C, 7 * C // 8, 7 * C // 8, 7 * C // 8, C // 2)
+TURN_AFTER = (13, 15, 23, 23, 28, 28, 36, 37, 43, 43, 43)
+EARLY_PRODUCT_AFTER = (45, 47)
+LIFT_WIDTH = {3: 3 * C // 4, 4: C // 2}
+W1_PIECES = 3
 OWN_PIECE = 192
 OUT_PIECES = (160, 352, 352, 352, 128)
 
@@ -52,7 +54,7 @@ def tile_moe_bdx_mlp_relu_kernel(
         w2_s_pair = [keep.tile([P, 2 * H], U8, name="w2_s%d" % n, align_bytes=64) for n in range(E // 2)]
         w2_s = [w2_s_pair[e // 2][:, (e % 2) * H : (e % 2 + 1) * H] for e in range(E)]
         w1_s = keep.tile([P, E * PASSES * K], U8, name="w1_s", align_bytes=64)
-        w1_w = keep.tile([P, E * PASSES * 2 * K], U8, name="w1_w", align_bytes=64)
+        w1_w = [keep.tile([P, E // W1_PIECES * PASSES * 2 * K], U8, name="w1_w%d" % n, align_bytes=64) for n in range(W1_PIECES)]
         w2_w = [keep.tile([P, 2 * H], U8, name="w2_w%d" % e, align_bytes=64) for e in range(E)]
         ident = keep.tile([P, P], F32, name="ident")
         gate_rows = keep.tile([P, P], F32, name="gate_rows")
@@ -82,15 +84,18 @@ def tile_moe_bdx_mlp_relu_kernel(
                     w2_scales[e0 : e0 + 2, 0, r:16:4, :].bitcast(I32).rearrange("e q i -> q e i"),
                 )
 
-        def load_w1():
+        def load_w1_scales():
             for r in range(4):
                 nc.sync.dma_start(
                     w1_s[r:P:32, :].bitcast(I32).rearrange("q (g k) -> q g k", g=E * PASSES),
                     w1_scales.rearrange("e s f k -> (e s) f k")[:, r:16:4, :].bitcast(I32).rearrange("g q k -> q g k"),
                 )
+
+        def load_w1(n):
+            step = E // W1_PIECES
             nc.sync.dma_start(
-                w1_w[:].bitcast(I32).rearrange("p (g k) -> p g k", g=E * PASSES),
-                w1_words.rearrange("e s p k -> p (e s) k").bitcast(I32),
+                w1_w[n][:].bitcast(I32).rearrange("p (g k) -> p g k", g=step * PASSES),
+                w1_words[n * step : (n + 1) * step].rearrange("e s p k -> p (e s) k").bitcast(I32),
             )
 
         nc.sync.dma_start(offs_sb[:], offs)
@@ -104,17 +109,23 @@ def tile_moe_bdx_mlp_relu_kernel(
             load_a(e, 0)
             if e == 0:
                 load_w2(1)
+            if e == E - 2:
+                load_w2(E - 1)
+            if e == E - 1:
+                load_w1_scales()
+                load_w1(0)
             load_a(e, 1)
-            if 0 < e < E - 1:
+            if 0 < e < E - 2:
                 load_w2(e + 1)
             if e % 2 == 1 and e < E - 1:
                 load_w2_scales(e + 1)
-        load_w1()
+        for n in range(1, W1_PIECES):
+            load_w1(n)
         nc.sync.dma_start(pos1_sb[:], pos1)
         nc.sync.dma_start(pos2_sb[:], pos2)
 
         def bank(name):
-            return psum.tile([P, PASS], F32, name=name, tag="bank", bufs=4)
+            return psum.tile([P, PASS], F32, name=name, tag="bank", bufs=8)
 
         def made_on_vector(columns, dtype, name):
             return ring.tile([P, columns], dtype, name=name, tag="made_on_vector", align_bytes=64, bufs=26)
@@ -150,21 +161,18 @@ def tile_moe_bdx_mlp_relu_kernel(
         def saved(e, s):
             return a_sb[e, s][:].rearrange("p (u d) c -> p u c d", u=2)
 
-        def sign_quarter(e, quarter):
-            if quarter == 0:
-                signed[e] = made_on_scalar(4 * C, BF16, "sign")
-            cols = slice(quarter * P, (quarter + 1) * P)
-            nc.scalar.activation(paired(signed[e][:])[:, :, cols, :], saved(e, 1)[:, :, cols, :], ACT.Sign)
+        def sign(e, s):
+            signed[e, s] = made_on_scalar(4 * C, BF16, "sign")
+            nc.scalar.activation(paired(signed[e, s][:]), saved(e, s), ACT.Sign)
 
-        def turn(e, s, order):
-            turned = psum.tile([P, 2 * PASS], F32, name="turned", bufs=2)
-            for b in order:
-                words = rounded[e, s][:, b * PASS : (b + 1) * PASS].bitcast(F32)
+        def turn(e, s, h):
+            turned = bank("turned")
+            for j in range(2):
+                words = rounded[e, s][:, (2 * h + j) * PASS : (2 * h + j + 1) * PASS].bitcast(F32)
                 for u in range(2):
-                    at = (b // 2) * PASS + (2 * u + b % 2) * P
+                    at = (2 * u + j) * P
                     nc.tensor.transpose(turned[:, at : at + P], words[:, u * P : (u + 1) * P], ident[:])
-            for h in range(2):
-                turned_of[e, s, h] = turned[:, h * PASS : (h + 1) * PASS]
+            turned_of[e, s, h] = turned[:]
 
         def next_block():
             k = len(blocks_done)
@@ -188,13 +196,15 @@ def tile_moe_bdx_mlp_relu_kernel(
                 ACT.Copy,
                 scale=gate_col[:, e * BLOCKS + b : e * BLOCKS + b + 1],
             )
-            for signed_e, places in SIGN_AFTER.items():
-                for quarter, place in enumerate(places):
-                    if place == k:
-                        sign_quarter(signed_e, quarter)
-            if k >= TURN_LAG and (k - TURN_LAG) % BLOCKS == 0:
-                unit = (k - TURN_LAG) // BLOCKS
-                turn(unit // PASSES, unit % PASSES, reversed(range(BLOCKS)))
+            for unit, place in SIGN_AFTER.items():
+                if place == k:
+                    sign(*unit)
+            for unit, after in enumerate(TURN_AFTER):
+                if after == k:
+                    turn(unit // PASSES, unit % PASSES, 0)
+                    turn(unit // PASSES, unit % PASSES, 1)
+            if k in EARLY_PRODUCT_AFTER:
+                second_product(EARLY_PRODUCT_AFTER.index(k))
 
         def blocks_through(k):
             while len(blocks_done) <= k:
@@ -223,7 +233,7 @@ def tile_moe_bdx_mlp_relu_kernel(
             )
 
         def masked(e, s):
-            blocks_through(BLOCKS * (PASSES * e + s) + TURN_LAG)
+            blocks_through(TURN_AFTER[PASSES * e + s])
             da_of[e, s] = made_on_vector(4 * C, BF16, "da")
             for h in range(2):
                 masked_half(e, s, h, da_of[e, s][:, 4 * h * HALF : 4 * (h + 1) * HALF])
@@ -235,9 +245,10 @@ def tile_moe_bdx_mlp_relu_kernel(
 
         def second_pass(acc, e, s, codes, scales):
             g = e * PASSES + s
+            in_piece = g % (E // W1_PIECES * PASSES)
             nc.tensor.matmul_mx(
                 out=acc,
-                lhsT=w1_w[:, 2 * g * K : 2 * (g + 1) * K].bitcast(E2M1X4),
+                lhsT=w1_w[e // (E // W1_PIECES)][:, 2 * in_piece * K : 2 * (in_piece + 1) * K].bitcast(E2M1X4),
                 lhsT_scale=w1_s[:, g * K : (g + 1) * K],
                 rhs=codes.bitcast(E5M2X4),
                 rhs_scale=scales,
@@ -261,48 +272,72 @@ def tile_moe_bdx_mlp_relu_kernel(
         gather_bytes(2)
         gather_words(2)
         gather_bytes(3)
-        in_window = {0: [(gather_words, 3), (gather_bytes, 4)], 1: [(gather_words, 4)], 2: [(gather_bytes, 5)], 3: [(gather_words, 5)], 4: []}
-        scaled = lifted
         for u in range(2):
             nc.gpsimd.tensor_scalar(
-                out=paired(scaled[:])[:, u], in0=saved(0, 0)[:, u], scalar1=LIFT, scalar2=0.0, op0=ALU.mult, op1=ALU.add
+                out=paired(lifted[:])[:, u], in0=saved(0, 0)[:, u], scalar1=LIFT, scalar2=0.0, op0=ALU.mult, op1=ALU.add
             )
-        make_mask(0, 0, scaled, C)
-        make_mask(0, 1)
-        room = lifted
-        for e in range(last):
-            scaled = room
-            lift(e + 1, 0, scaled, 0, LIFT_WIDTH[e + 1])
-            between = 0 if e == 0 else 1
-            masked(e, 0)
-            for gather, of in in_window[e][:between]:
-                gather(of)
-            masked(e, 1)
-            for gather, of in in_window[e][between:]:
-                gather(of)
-            if e + 1 in SIGN_AFTER:
-                quantise((e, 0), da_of[e, 0][:], C)
-                make_mask(e + 1, 0, scaled, LIFT_WIDTH[e + 1])
-                blocks_through(SIGN_AFTER[e + 1][-1])
-                make_mask(e + 1, 1, signed[e + 1], P * len(SIGN_AFTER[e + 1]))
-                room = signed[e + 1]
-            else:
-                make_mask(e + 1, 1)
-                make_mask(e + 1, 0, scaled, LIFT_WIDTH[e + 1])
-                quantise((e, 0), da_of[e, 0][:], C)
-                room = da_of[e, 0]
-            quantise((e, 1), da_of[e, 1][:], C)
+        make_mask(0, 0, lifted, C)
+        lift(0, 1, lifted, 0, C)
+        gather_words(3)
+        masked(0, 0)
+        gather_bytes(4)
+        make_mask(0, 1, lifted, C)
+        lift(1, 0, lifted, 0, C)
+        quantise((0, 0), da_of[0, 0][:], C)
+        masked(0, 1)
+        gather_words(4)
+        gather_bytes(5)
+        quantise((0, 1), da_of[0, 1][:], C)
+        blocks_through(SIGN_AFTER[1, 1])
+        make_mask(1, 1, signed[1, 1], C)
+        make_mask(1, 0, lifted, C)
+        lift(2, 0, signed[1, 1], 0, C)
+        gather_words(5)
+
+        masked(1, 0)
+        masked(1, 1)
+        quantise((1, 0), da_of[1, 0][:], C)
+        make_mask(2, 0, signed[1, 1], C)
+        blocks_through(SIGN_AFTER[2, 1])
+        make_mask(2, 1, signed[2, 1], C)
+        lift(3, 0, signed[2, 1], 0, LIFT_WIDTH[3])
+        quantise((1, 1), da_of[1, 1][:], C)
+
+        masked(2, 0)
+        masked(2, 1)
+        make_mask(3, 1)
+        make_mask(3, 0, signed[2, 1], LIFT_WIDTH[3])
+        quantise((2, 0), da_of[2, 0][:], C)
+        lift(4, 0, da_of[2, 0], 0, LIFT_WIDTH[4])
+        quantise((2, 1), da_of[2, 1][:], C)
+
+        masked(3, 0)
+        masked(3, 1)
+        quantise((3, 0), da_of[3, 0][:], C)
+        make_mask(4, 0, da_of[2, 0], LIFT_WIDTH[4])
+        make_mask(4, 1)
+        quantise((3, 1), da_of[3, 1][:], C)
+
+        masked(4, 0)
+        masked(4, 1)
+        quantise((4, 0), da_of[4, 0][:], C)
+        blocks_through(SIGN_AFTER[last, 0])
+        make_mask(last, 0, signed[last, 0], C)
+        quantise((4, 1), da_of[4, 1][:], C)
 
         masked(last, 0)
+        make_mask(last, 1)
         blocks_through(E * PASSES * BLOCKS - 1)
-        turn(last, 1, (1, 0, 3, 2))
-        for e in range(last):
-            second_product(e)
-        halves = [made_on_vector(4 * HALF, BF16, "da")]
-        masked_half(last, 1, 0, halves[0][:])
+        turn(last, 1, 0)
+        second_product(2)
+        turn(last, 1, 1)
+        second_product(3)
+        second_product(4)
         quantise((last, 0), da_of[last, 0][:], C)
-        halves.append(made_on_vector(4 * HALF, BF16, "da"))
-        masked_half(last, 1, 1, halves[1][:])
+        halves = []
+        for h in range(2):
+            halves.append(made_on_vector(4 * HALF, BF16, "da"))
+            masked_half(last, 1, h, halves[h][:])
         accs = []
         for h in range(2):
             accs.append(bank("acc"))

@@ -33,8 +33,9 @@ TURN_AFTER = (13, 15, 23, 23, 28, 28, 36, 37, 43, 43, 43)
 EARLY_PRODUCT_AFTER = (45, 47)
 LIFT_WIDTH = {3: 3 * C // 4, 4: C // 2}
 W1_PIECES = 3
-OWN_PIECE = 192
-OUT_PIECES = (160, 352, 352, 352, 128)
+OWN_PIECE = 320
+OUT_PIECES = (192, 384, 288, 224, 128)
+LAST_PIECES = ((0, HALF), (HALF, P), (HALF + P, P))
 
 
 def tile_moe_bdx_mlp_relu_kernel(
@@ -223,12 +224,13 @@ def tile_moe_bdx_mlp_relu_kernel(
             if width > 0:
                 nc.vector.tensor_scalar(out=mask[:, :, 0:width, :], in0=paired(source[:])[:, :, 0:width, :], scalar1=0.0, scalar2=None, op0=ALU.is_gt)
 
-        def masked_half(e, s, h, da):
+        def masked_slots(e, s, c0, width, da):
             mask = mask_of[e, s][:].rearrange("p (u c d) -> p c u d", u=2, d=2)
+            turned = turned_of[e, s, c0 // HALF].bitcast(BF16).rearrange("p (u c d) -> p c u d", u=2, d=2)
             nc.vector.tensor_tensor(
                 da.rearrange("p (c u d) -> p c u d", u=2, d=2),
-                turned_of[e, s, h].bitcast(BF16).rearrange("p (u c d) -> p c u d", u=2, d=2),
-                mask[:, h * HALF : (h + 1) * HALF],
+                turned[:, c0 % HALF : c0 % HALF + width],
+                mask[:, c0 : c0 + width],
                 ALU.mult,
             )
 
@@ -236,11 +238,11 @@ def tile_moe_bdx_mlp_relu_kernel(
             blocks_through(TURN_AFTER[PASSES * e + s])
             da_of[e, s] = made_on_vector(4 * C, BF16, "da")
             for h in range(2):
-                masked_half(e, s, h, da_of[e, s][:, 4 * h * HALF : 4 * (h + 1) * HALF])
+                masked_slots(e, s, h * HALF, HALF, da_of[e, s][:, 4 * h * HALF : 4 * (h + 1) * HALF])
 
         def quantise(key, da, width):
             codes_of[key] = made_on_vector(width, U32, "codes")
-            scales_of[key] = ring.tile([P, width], U8, name="scales", align_bytes=64, bufs=E * PASSES + 1)
+            scales_of[key] = ring.tile([P, width], U8, name="scales", align_bytes=64, bufs=E * PASSES + 2)
             nc.vector.quantize_mx(out=codes_of[key][:].bitcast(E5M2X4), scales=scales_of[key][:], in_=da)
 
         def second_pass(acc, e, s, codes, scales):
@@ -334,20 +336,28 @@ def tile_moe_bdx_mlp_relu_kernel(
         second_product(3)
         second_product(4)
         quantise((last, 0), da_of[last, 0][:], C)
-        halves = []
-        for h in range(2):
-            halves.append(made_on_vector(4 * HALF, BF16, "da"))
-            masked_half(last, 1, h, halves[h][:])
-        accs = []
-        for h in range(2):
+        accs, pieces = [], []
+        for c0, width in LAST_PIECES:
             accs.append(bank("acc"))
-            cols = slice(h * HALF, (h + 1) * HALF)
-            second_pass(accs[h][:, 0:HALF], last, 0, codes_of[last, 0][:, cols], scales_of[last, 0][:, cols])
-        for h in range(2):
-            quantise((last, 1, h), halves[h][:], HALF)
-            second_pass(accs[h][:, 0:HALF], last, 1, codes_of[last, 1, h][:], scales_of[last, 1, h][:])
-        nc.scalar.copy(dx[:, last * C : last * C + HALF], accs[0][:, 0:HALF])
-        nc.vector.tensor_copy(dx[:, last * C + HALF : S], accs[1][:, 0:HALF])
+            second_pass(accs[-1][:, 0:width], last, 0, codes_of[last, 0][:, c0 : c0 + width], scales_of[last, 0][:, c0 : c0 + width])
+
+        def last_masked(n):
+            c0, width = LAST_PIECES[n]
+            pieces.append(made_on_vector(4 * width, BF16, "da"))
+            masked_slots(last, 1, c0, width, pieces[n][:])
+
+        def last_product(n):
+            c0, width = LAST_PIECES[n]
+            quantise((last, 1, n), pieces[n][:], width)
+            second_pass(accs[n][:, 0:width], last, 1, codes_of[last, 1, n][:], scales_of[last, 1, n][:])
+            copy = nc.vector.tensor_copy if n + 1 == len(LAST_PIECES) else nc.scalar.copy
+            copy(dx[:, last * C + c0 : last * C + c0 + width], accs[n][:, 0:width])
+
+        last_masked(0)
+        for n in range(1, len(LAST_PIECES)):
+            last_masked(n)
+            last_product(n - 1)
+        last_product(len(LAST_PIECES) - 1)
 
         def list_columns(t0, width):
             return slice(t0 // LIST_COL, (t0 + width) // LIST_COL)

@@ -27,14 +27,15 @@ HALF = C // 2
 LIST_COL = 16
 A_ROOMS = 6
 LIFT = 2.0**23
-SIGN_AFTER = {(1, 1): 15, (2, 1): 22, (5, 0): 42}
+SIGN_AFTER = {(1, 1): 17, (2, 1): 22, (3, 0): 25, (4, 0): 35, (5, 0): 41}
 FIRST_PIECE = 128
-TURN_AFTER = (13, 15, 23, 23, 28, 28, 36, 37, 43, 43, 43)
+TURN_AFTER = (13, 15, 23, 23, 28, 28, 36, 37, 43, 43, 45)
 EARLY_PRODUCT_AFTER = (45, 47)
-LIFT_WIDTH = {3: 3 * C // 4, 4: C // 2}
+LIFT_WIDTH = {3: 3 * C // 4, 4: C // 2, 5: 3 * C // 8}
 W1_PIECES = 3
+SCALE_GROUPS = {0: 1, 1: 1, 2: 2, 4: 2}
 OWN_PIECE = 320
-OUT_PIECES = (192, 384, 288, 224, 128)
+OUT_PIECES = (160, 384, 320, 224, 128)
 LAST_PIECES = ((0, HALF), (HALF, P), (HALF + P, P))
 
 
@@ -52,8 +53,8 @@ def tile_moe_bdx_mlp_relu_kernel(
         pos2_sb = keep.tile([P, T // LIST_COL], U16, name="pos2_sb")
         dy_w = keep.tile([P, T], I32, name="dy_w", align_bytes=64)
         dy_s = keep.tile([P, T], U8, name="dy_s", align_bytes=64)
-        w2_s_pair = [keep.tile([P, 2 * H], U8, name="w2_s%d" % n, align_bytes=64) for n in range(E // 2)]
-        w2_s = [w2_s_pair[e // 2][:, (e % 2) * H : (e % 2 + 1) * H] for e in range(E)]
+        w2_s_group = {e0: keep.tile([P, n * H], U8, name="w2_s%d" % e0, align_bytes=64) for e0, n in SCALE_GROUPS.items()}
+        w2_s = [w2_s_group[e0][:, j * H : (j + 1) * H] for e0, n in SCALE_GROUPS.items() for j in range(n)]
         w1_s = keep.tile([P, E * PASSES * K], U8, name="w1_s", align_bytes=64)
         w1_w = [keep.tile([P, E // W1_PIECES * PASSES * 2 * K], U8, name="w1_w%d" % n, align_bytes=64) for n in range(W1_PIECES)]
         w2_w = [keep.tile([P, 2 * H], U8, name="w2_w%d" % e, align_bytes=64) for e in range(E)]
@@ -78,11 +79,11 @@ def tile_moe_bdx_mlp_relu_kernel(
             nc.sync.dma_start(w2_w[e][:].bitcast(I32), w2_words[e, 0].bitcast(I32))
 
         def load_w2_scales(e0):
-            plane = w2_s_pair[e0 // 2]
+            plane = w2_s_group[e0]
             for r in range(4):
                 nc.sync.dma_start(
                     plane[r:P:32, :].bitcast(I32).rearrange("q (e i) -> q e i", i=H // 4),
-                    w2_scales[e0 : e0 + 2, 0, r:16:4, :].bitcast(I32).rearrange("e q i -> q e i"),
+                    w2_scales[e0 : e0 + SCALE_GROUPS[e0], 0, r:16:4, :].bitcast(I32).rearrange("e q i -> q e i"),
                 )
 
         def load_w1_scales():
@@ -110,15 +111,19 @@ def tile_moe_bdx_mlp_relu_kernel(
             load_a(e, 0)
             if e == 0:
                 load_w2(1)
+                load_w2_scales(1)
+            if e == 1:
+                load_w2(2)
+                load_w2_scales(2)
             if e == E - 2:
                 load_w2(E - 1)
             if e == E - 1:
                 load_w1_scales()
                 load_w1(0)
             load_a(e, 1)
-            if 0 < e < E - 2:
+            if 1 < e < E - 2:
                 load_w2(e + 1)
-            if e % 2 == 1 and e < E - 1:
+            if e == 3:
                 load_w2_scales(e + 1)
         for n in range(1, W1_PIECES):
             load_w1(n)
@@ -163,8 +168,10 @@ def tile_moe_bdx_mlp_relu_kernel(
             return a_sb[e, s][:].rearrange("p (u d) c -> p u c d", u=2)
 
         def sign(e, s):
-            signed[e, s] = made_on_scalar(4 * C, BF16, "sign")
-            nc.scalar.activation(paired(signed[e, s][:]), saved(e, s), ACT.Sign)
+            if s == 1:
+                signed[e, s] = made_on_scalar(4 * C, BF16, "sign")
+            c0 = 0 if s == 1 else LIFT_WIDTH[e]
+            nc.scalar.activation(paired(signed[e, s][:])[:, :, c0:C, :], saved(e, s)[:, :, c0:C, :], ACT.Sign)
 
         def turn(e, s, h):
             turned = bank("turned")
@@ -258,11 +265,14 @@ def tile_moe_bdx_mlp_relu_kernel(
                 stop=(s == PASSES - 1),
             )
 
-        def second_product(e):
+        def second_sums(e):
             acc = bank("acc")
             for s in range(PASSES):
                 second_pass(acc[:], e, s, codes_of[e, s][:], scales_of[e, s][:])
-            nc.scalar.copy(dx[:, e * C : (e + 1) * C], acc[:])
+            return acc
+
+        def second_product(e):
+            nc.scalar.copy(dx[:, e * C : (e + 1) * C], second_sums(e)[:])
 
         last = E - 1
         gather_bytes(0)
@@ -302,23 +312,27 @@ def tile_moe_bdx_mlp_relu_kernel(
         make_mask(2, 0, signed[1, 1], C)
         blocks_through(SIGN_AFTER[2, 1])
         make_mask(2, 1, signed[2, 1], C)
-        lift(3, 0, signed[2, 1], 0, LIFT_WIDTH[3])
+        signed[3, 0] = signed[2, 1]
+        lift(3, 0, signed[3, 0], 0, LIFT_WIDTH[3])
         quantise((1, 1), da_of[1, 1][:], C)
 
         masked(2, 0)
         masked(2, 1)
         make_mask(3, 1)
-        make_mask(3, 0, signed[2, 1], LIFT_WIDTH[3])
+        make_mask(3, 0, signed[3, 0], C)
         quantise((2, 0), da_of[2, 0][:], C)
-        lift(4, 0, da_of[2, 0], 0, LIFT_WIDTH[4])
+        signed[4, 0] = da_of[2, 0]
+        lift(4, 0, signed[4, 0], 0, LIFT_WIDTH[4])
         quantise((2, 1), da_of[2, 1][:], C)
 
         masked(3, 0)
         masked(3, 1)
         quantise((3, 0), da_of[3, 0][:], C)
-        make_mask(4, 0, da_of[2, 0], LIFT_WIDTH[4])
-        make_mask(4, 1)
+        make_mask(4, 0, signed[4, 0], C)
         quantise((3, 1), da_of[3, 1][:], C)
+        signed[5, 0] = da_of[3, 1]
+        lift(5, 0, signed[5, 0], 0, LIFT_WIDTH[5])
+        make_mask(4, 1)
 
         masked(4, 0)
         masked(4, 1)
@@ -334,7 +348,7 @@ def tile_moe_bdx_mlp_relu_kernel(
         second_product(2)
         turn(last, 1, 1)
         second_product(3)
-        second_product(4)
+        waiting = second_sums(last - 1)
         quantise((last, 0), da_of[last, 0][:], C)
         accs, pieces = [], []
         for c0, width in LAST_PIECES:
@@ -350,14 +364,14 @@ def tile_moe_bdx_mlp_relu_kernel(
             c0, width = LAST_PIECES[n]
             quantise((last, 1, n), pieces[n][:], width)
             second_pass(accs[n][:, 0:width], last, 1, codes_of[last, 1, n][:], scales_of[last, 1, n][:])
-            copy = nc.vector.tensor_copy if n + 1 == len(LAST_PIECES) else nc.scalar.copy
-            copy(dx[:, last * C + c0 : last * C + c0 + width], accs[n][:, 0:width])
+            if n + 1 == len(LAST_PIECES):
+                nc.vector.tensor_copy(dx[:, (last - 1) * C : last * C], waiting[:])
+            nc.scalar.copy(dx[:, last * C + c0 : last * C + c0 + width], accs[n][:, 0:width])
 
-        last_masked(0)
-        for n in range(1, len(LAST_PIECES)):
+        for n in range(len(LAST_PIECES)):
             last_masked(n)
-            last_product(n - 1)
-        last_product(len(LAST_PIECES) - 1)
+        for n in range(len(LAST_PIECES)):
+            last_product(n)
 
         def list_columns(t0, width):
             return slice(t0 // LIST_COL, (t0 + width) // LIST_COL)

@@ -27,11 +27,10 @@ HALF = C // 2
 LIST_COL = 16
 A_ROOMS = 6
 LIFT = 2.0**23
-SIGN_AFTER = {(1, 1): 17, (2, 1): 22, (3, 0): 25, (4, 0): 35, (5, 0): 41}
+SIGN_AFTER = {(1, 1): 17, (2, 1): 22, (3, 0): 26, (4, 0): 35, (5, 0): 41}
 FIRST_PIECE = 128
-TURN_AFTER = (13, 15, 23, 23, 28, 28, 36, 37, 43, 43, 45)
-EARLY_PRODUCT_AFTER = (45, 47)
-LIFT_WIDTH = {3: 3 * C // 4, 4: C // 2, 5: 3 * C // 8}
+TURN_AFTER = (13, 15, 23, 23, 28, 28, 36, 37, 41, 43)
+LIFT_WIDTH = {3: 5 * C // 8, 4: C // 2, 5: 3 * C // 8}
 W1_PIECES = 3
 SCALE_GROUPS = {0: 1, 1: 1, 2: 2, 4: 2}
 OWN_PIECE = 320
@@ -153,7 +152,7 @@ def tile_moe_bdx_mlp_relu_kernel(
             gathered = made_on_vector(c1 - c0, U8, "g_s")
             nc.vector.tensor_copy(gathered[:], dy_s[:].indirect(slots(e, c0, c1)))
             for c in range(c0, c1, P):
-                g_s[e, c // P] = gathered[:, c - c0 : c - c0 + P]
+                g_s[e + c // C, c % C // P] = gathered[:, c - c0 : c - c0 + P]
 
         def gather_words(e, c0=0, c1=C):
             gathered = made_on_vector(c1 - c0, U32, "g_w")
@@ -175,7 +174,7 @@ def tile_moe_bdx_mlp_relu_kernel(
 
         def turn(e, s, h):
             turned = bank("turned")
-            for j in range(2):
+            for j in (1, 0):
                 words = rounded[e, s][:, (2 * h + j) * PASS : (2 * h + j + 1) * PASS].bitcast(F32)
                 for u in range(2):
                     at = (2 * u + j) * P
@@ -211,8 +210,6 @@ def tile_moe_bdx_mlp_relu_kernel(
                 if after == k:
                     turn(unit // PASSES, unit % PASSES, 0)
                     turn(unit // PASSES, unit % PASSES, 1)
-            if k in EARLY_PRODUCT_AFTER:
-                second_product(EARLY_PRODUCT_AFTER.index(k))
 
         def blocks_through(k):
             while len(blocks_done) <= k:
@@ -242,7 +239,8 @@ def tile_moe_bdx_mlp_relu_kernel(
             )
 
         def masked(e, s):
-            blocks_through(TURN_AFTER[PASSES * e + s])
+            if e < E - 1:
+                blocks_through(TURN_AFTER[PASSES * e + s])
             da_of[e, s] = made_on_vector(4 * C, BF16, "da")
             for h in range(2):
                 masked_slots(e, s, h * HALF, HALF, da_of[e, s][:, 4 * h * HALF : 4 * (h + 1) * HALF])
@@ -281,9 +279,8 @@ def tile_moe_bdx_mlp_relu_kernel(
         gather_words(0, FIRST_PIECE, C)
         gather_bytes(1, HALF, C)
         gather_words(1)
-        gather_bytes(2)
+        gather_bytes(2, 0, 2 * C)
         gather_words(2)
-        gather_bytes(3)
         for u in range(2):
             nc.gpsimd.tensor_scalar(
                 out=paired(lifted[:])[:, u], in0=saved(0, 0)[:, u], scalar1=LIFT, scalar2=0.0, op0=ALU.mult, op1=ALU.add
@@ -292,13 +289,12 @@ def tile_moe_bdx_mlp_relu_kernel(
         lift(0, 1, lifted, 0, C)
         gather_words(3)
         masked(0, 0)
-        gather_bytes(4)
+        gather_words(4)
         make_mask(0, 1, lifted, C)
         lift(1, 0, lifted, 0, C)
         quantise((0, 0), da_of[0, 0][:], C)
         masked(0, 1)
-        gather_words(4)
-        gather_bytes(5)
+        gather_bytes(4, 0, 2 * C)
         quantise((0, 1), da_of[0, 1][:], C)
         blocks_through(SIGN_AFTER[1, 1])
         make_mask(1, 1, signed[1, 1], C)
@@ -341,9 +337,14 @@ def tile_moe_bdx_mlp_relu_kernel(
         make_mask(last, 0, signed[last, 0], C)
         quantise((4, 1), da_of[4, 1][:], C)
 
+        blocks_through(E * PASSES * BLOCKS - 3)
+        turn(last, 0, 0)
+        blocks_through(E * PASSES * BLOCKS - 1)
+        turn(last, 0, 1)
+        second_product(0)
         masked(last, 0)
         make_mask(last, 1)
-        blocks_through(E * PASSES * BLOCKS - 1)
+        second_product(1)
         turn(last, 1, 0)
         second_product(2)
         turn(last, 1, 1)
@@ -366,7 +367,8 @@ def tile_moe_bdx_mlp_relu_kernel(
             second_pass(accs[n][:, 0:width], last, 1, codes_of[last, 1, n][:], scales_of[last, 1, n][:])
             if n + 1 == len(LAST_PIECES):
                 nc.vector.tensor_copy(dx[:, (last - 1) * C : last * C], waiting[:])
-            nc.scalar.copy(dx[:, last * C + c0 : last * C + c0 + width], accs[n][:, 0:width])
+            copy = nc.vector.tensor_copy if n + 1 == len(LAST_PIECES) else nc.scalar.copy
+            copy(dx[:, last * C + c0 : last * C + c0 + width], accs[n][:, 0:width])
 
         for n in range(len(LAST_PIECES)):
             last_masked(n)

@@ -23,19 +23,25 @@ P = 128
 PASS = 512
 PASSES = H // PASS
 BLOCKS = C // P
+LAST_BLOCK = E * PASSES * BLOCKS - 1
 HALF = C // 2
 LIST_COL = 16
+SCALE_ROWS = 4
+BANKS = 8
 A_ROOMS = 6
+VECTOR_TILES = 26
+SCALAR_TILES = 8
 LIFT = 2.0**23
-SIGN_AFTER = {(1, 1): 17, (2, 1): 22, (3, 0): 26, (4, 0): 35, (5, 0): 41}
-FIRST_PIECE = 128
-TURN_AFTER = (13, 15, 23, 23, 28, 28, 36, 37, 41, 43)
+SIGNED = ((1, 1), (2, 1), (3, 0), (4, 0), (5, 0))
 LIFT_WIDTH = {3: 5 * C // 8, 4: C // 2, 5: 3 * C // 8}
-W1_PIECES = 3
+EARLY_EXPERTS = 2
+FIRST_PIECE = P
 SCALE_GROUPS = {0: 1, 1: 1, 2: 2, 4: 2}
+W1_PIECES = 3
+W1_EXPERTS = E // W1_PIECES
+LAST_PIECES = ((0, HALF), (HALF, P), (HALF + P, P))
 OWN_PIECE = 320
 OUT_PIECES = (160, 384, 320, 224, 128)
-LAST_PIECES = ((0, HALF), (HALF, P), (HALF + P, P))
 
 
 def tile_moe_bdx_mlp_relu_kernel(
@@ -55,7 +61,7 @@ def tile_moe_bdx_mlp_relu_kernel(
         w2_s_group = {e0: keep.tile([P, n * H], U8, name="w2_s%d" % e0, align_bytes=64) for e0, n in SCALE_GROUPS.items()}
         w2_s = [w2_s_group[e0][:, j * H : (j + 1) * H] for e0, n in SCALE_GROUPS.items() for j in range(n)]
         w1_s = keep.tile([P, E * PASSES * K], U8, name="w1_s", align_bytes=64)
-        w1_w = [keep.tile([P, E // W1_PIECES * PASSES * 2 * K], U8, name="w1_w%d" % n, align_bytes=64) for n in range(W1_PIECES)]
+        w1_w = [keep.tile([P, W1_EXPERTS * PASSES * 2 * K], U8, name="w1_w%d" % n, align_bytes=64) for n in range(W1_PIECES)]
         w2_w = [keep.tile([P, 2 * H], U8, name="w2_w%d" % e, align_bytes=64) for e in range(E)]
         ident = keep.tile([P, P], F32, name="ident")
         gate_rows = keep.tile([P, P], F32, name="gate_rows")
@@ -78,65 +84,61 @@ def tile_moe_bdx_mlp_relu_kernel(
             nc.sync.dma_start(w2_w[e][:].bitcast(I32), w2_words[e, 0].bitcast(I32))
 
         def load_w2_scales(e0):
-            plane = w2_s_group[e0]
-            for r in range(4):
+            group = w2_s_group[e0]
+            for r in range(SCALE_ROWS):
                 nc.sync.dma_start(
-                    plane[r:P:32, :].bitcast(I32).rearrange("q (e i) -> q e i", i=H // 4),
+                    group[r:P:32, :].bitcast(I32).rearrange("q (e i) -> q e i", i=H // 4),
                     w2_scales[e0 : e0 + SCALE_GROUPS[e0], 0, r:16:4, :].bitcast(I32).rearrange("e q i -> q e i"),
                 )
 
         def load_w1_scales():
-            for r in range(4):
+            for r in range(SCALE_ROWS):
                 nc.sync.dma_start(
                     w1_s[r:P:32, :].bitcast(I32).rearrange("q (g k) -> q g k", g=E * PASSES),
                     w1_scales.rearrange("e s f k -> (e s) f k")[:, r:16:4, :].bitcast(I32).rearrange("g q k -> q g k"),
                 )
 
         def load_w1(n):
-            step = E // W1_PIECES
             nc.sync.dma_start(
-                w1_w[n][:].bitcast(I32).rearrange("p (g k) -> p g k", g=step * PASSES),
-                w1_words[n * step : (n + 1) * step].rearrange("e s p k -> p (e s) k").bitcast(I32),
+                w1_w[n][:].bitcast(I32).rearrange("p (g k) -> p g k", g=W1_EXPERTS * PASSES),
+                w1_words[n * W1_EXPERTS : (n + 1) * W1_EXPERTS].rearrange("e s p k -> p (e s) k").bitcast(I32),
             )
 
         nc.sync.dma_start(offs_sb[:], offs)
         nc.sync.dma_start(gate_rows[:], gate.rearrange("h (b m) -> (h b) m", m=P)[0:P, :])
-        for r in range(4):
+        for r in range(SCALE_ROWS):
             nc.sync.dma_start(dy_s[r:P:32, :].bitcast(I32), dy_scales[0, r:16:4, :].bitcast(I32))
         nc.sync.dma_start(dy_w[:], dy_words[0].rearrange("p t d -> p (t d)").bitcast(I32))
         load_w2(0)
         load_w2_scales(0)
-        for e in range(E):
+        last = E - 1
+        for e in range(last):
+            between = e in (0, last - 1)
             load_a(e, 0)
-            if e == 0:
-                load_w2(1)
-                load_w2_scales(1)
-            if e == 1:
-                load_w2(2)
-                load_w2_scales(2)
-            if e == E - 2:
-                load_w2(E - 1)
-            if e == E - 1:
-                load_w1_scales()
-                load_w1(0)
-            load_a(e, 1)
-            if 1 < e < E - 2:
-                load_w2(e + 1)
-            if e == 3:
+            if not between:
+                load_a(e, 1)
+            load_w2(e + 1)
+            if e + 1 in SCALE_GROUPS:
                 load_w2_scales(e + 1)
+            if between:
+                load_a(e, 1)
+        load_a(last, 0)
+        load_w1_scales()
+        load_w1(0)
+        load_a(last, 1)
         for n in range(1, W1_PIECES):
             load_w1(n)
         nc.sync.dma_start(pos1_sb[:], pos1)
         nc.sync.dma_start(pos2_sb[:], pos2)
 
         def bank(name):
-            return psum.tile([P, PASS], F32, name=name, tag="bank", bufs=8)
+            return psum.tile([P, PASS], F32, name=name, tag="bank", bufs=BANKS)
 
         def made_on_vector(columns, dtype, name):
-            return ring.tile([P, columns], dtype, name=name, tag="made_on_vector", align_bytes=64, bufs=26)
+            return ring.tile([P, columns], dtype, name=name, tag="made_on_vector", align_bytes=64, bufs=VECTOR_TILES)
 
         def made_on_scalar(columns, dtype, name):
-            return ring.tile([P, columns], dtype, name=name, tag="made_on_scalar", bufs=8)
+            return ring.tile([P, columns], dtype, name=name, tag="made_on_scalar", bufs=SCALAR_TILES)
 
         gate_ps = bank("gate_ps")
         nc.tensor.transpose(gate_ps[:, 0:P], gate_rows[:], ident[:])
@@ -181,6 +183,10 @@ def tile_moe_bdx_mlp_relu_kernel(
                     nc.tensor.transpose(turned[:, at : at + P], words[:, u * P : (u + 1) * P], ident[:])
             turned_of[e, s, h] = turned[:]
 
+        def turn_block(e):
+            first_of_next = (e + 1) * PASSES * BLOCKS
+            return first_of_next + (PASSES * BLOCKS - 1 if e < EARLY_EXPERTS else BLOCKS)
+
         def next_block():
             k = len(blocks_done)
             blocks_done.append(k)
@@ -203,30 +209,31 @@ def tile_moe_bdx_mlp_relu_kernel(
                 ACT.Copy,
                 scale=gate_col[:, e * BLOCKS + b : e * BLOCKS + b + 1],
             )
-            for unit, place in SIGN_AFTER.items():
-                if place == k:
-                    sign(*unit)
-            for unit, after in enumerate(TURN_AFTER):
-                if after == k:
-                    turn(unit // PASSES, unit % PASSES, 0)
-                    turn(unit // PASSES, unit % PASSES, 1)
+            if b == BLOCKS - 1 and (e, s) in SIGNED:
+                sign(e, s)
+            if e > 0 and k == turn_block(e - 1):
+                for turned_s in range(PASSES):
+                    for h in range(2):
+                        turn(e - 1, turned_s, h)
 
         def blocks_through(k):
             while len(blocks_done) <= k:
                 next_block()
 
-        def lift(e, s, tile, c0, c1):
-            nc.gpsimd.tensor_scalar(
-                out=paired(tile[:])[:, :, c0:c1, :], in0=saved(e, s)[:, :, c0:c1, :], scalar1=LIFT, scalar2=0.0, op0=ALU.mult, op1=ALU.add
-            )
+        def blocks_through_pass(e, s):
+            blocks_through((e * PASSES + s + 1) * BLOCKS - 1)
 
-        def make_mask(e, s, source=None, width=0):
+        def scale_up(target, source):
+            nc.gpsimd.tensor_scalar(out=target, in0=source, scalar1=LIFT, scalar2=0.0, op0=ALU.mult, op1=ALU.add)
+
+        def lift(e, s, tile, width=C):
+            signed[e, s] = tile
+            scale_up(paired(tile[:])[:, :, 0:width, :], saved(e, s)[:, :, 0:width, :])
+
+        def make_mask(e, s):
             mask_of[e, s] = made_on_vector(4 * C, BF16, "mask")
-            mask = paired(mask_of[e, s][:])
-            if width < C:
-                nc.vector.tensor_scalar(out=mask[:, :, width:C, :], in0=saved(e, s)[:, :, width:C, :], scalar1=0.0, scalar2=None, op0=ALU.is_gt)
-            if width > 0:
-                nc.vector.tensor_scalar(out=mask[:, :, 0:width, :], in0=paired(source[:])[:, :, 0:width, :], scalar1=0.0, scalar2=None, op0=ALU.is_gt)
+            source = paired(signed[e, s][:]) if (e, s) in signed else saved(e, s)
+            nc.vector.tensor_scalar(out=paired(mask_of[e, s][:]), in0=source, scalar1=0.0, scalar2=None, op0=ALU.is_gt)
 
         def masked_slots(e, s, c0, width, da):
             mask = mask_of[e, s][:].rearrange("p (u c d) -> p c u d", u=2, d=2)
@@ -239,23 +246,26 @@ def tile_moe_bdx_mlp_relu_kernel(
             )
 
         def masked(e, s):
-            if e < E - 1:
-                blocks_through(TURN_AFTER[PASSES * e + s])
+            if e < last:
+                blocks_through(turn_block(e))
             da_of[e, s] = made_on_vector(4 * C, BF16, "da")
             for h in range(2):
                 masked_slots(e, s, h * HALF, HALF, da_of[e, s][:, 4 * h * HALF : 4 * (h + 1) * HALF])
 
         def quantise(key, da, width):
             codes_of[key] = made_on_vector(width, U32, "codes")
-            scales_of[key] = ring.tile([P, width], U8, name="scales", align_bytes=64, bufs=E * PASSES + 2)
+            scales_of[key] = ring.tile([P, width], U8, name="scales", align_bytes=64, bufs=E * PASSES - 1 + len(LAST_PIECES))
             nc.vector.quantize_mx(out=codes_of[key][:].bitcast(E5M2X4), scales=scales_of[key][:], in_=da)
+
+        def quantise_pass(e, s):
+            quantise((e, s), da_of[e, s][:], C)
 
         def second_pass(acc, e, s, codes, scales):
             g = e * PASSES + s
-            in_piece = g % (E // W1_PIECES * PASSES)
+            in_piece = g % (W1_EXPERTS * PASSES)
             nc.tensor.matmul_mx(
                 out=acc,
-                lhsT=w1_w[e // (E // W1_PIECES)][:, 2 * in_piece * K : 2 * (in_piece + 1) * K].bitcast(E2M1X4),
+                lhsT=w1_w[e // W1_EXPERTS][:, 2 * in_piece * K : 2 * (in_piece + 1) * K].bitcast(E2M1X4),
                 lhsT_scale=w1_s[:, g * K : (g + 1) * K],
                 rhs=codes.bitcast(E5M2X4),
                 rhs_scale=scales,
@@ -272,7 +282,6 @@ def tile_moe_bdx_mlp_relu_kernel(
         def second_product(e):
             nc.scalar.copy(dx[:, e * C : (e + 1) * C], second_sums(e)[:])
 
-        last = E - 1
         gather_bytes(0)
         gather_bytes(1, 0, HALF)
         gather_words(0, 0, FIRST_PIECE)
@@ -281,65 +290,61 @@ def tile_moe_bdx_mlp_relu_kernel(
         gather_words(1)
         gather_bytes(2, 0, 2 * C)
         gather_words(2)
+        signed[0, 0] = lifted
         for u in range(2):
-            nc.gpsimd.tensor_scalar(
-                out=paired(lifted[:])[:, u], in0=saved(0, 0)[:, u], scalar1=LIFT, scalar2=0.0, op0=ALU.mult, op1=ALU.add
-            )
-        make_mask(0, 0, lifted, C)
-        lift(0, 1, lifted, 0, C)
+            scale_up(paired(lifted[:])[:, u], saved(0, 0)[:, u])
+
+        make_mask(0, 0)
+        lift(0, 1, lifted)
         gather_words(3)
         masked(0, 0)
         gather_words(4)
-        make_mask(0, 1, lifted, C)
-        lift(1, 0, lifted, 0, C)
-        quantise((0, 0), da_of[0, 0][:], C)
+        make_mask(0, 1)
+        lift(1, 0, lifted)
+        quantise_pass(0, 0)
         masked(0, 1)
         gather_bytes(4, 0, 2 * C)
-        quantise((0, 1), da_of[0, 1][:], C)
-        blocks_through(SIGN_AFTER[1, 1])
-        make_mask(1, 1, signed[1, 1], C)
-        make_mask(1, 0, lifted, C)
-        lift(2, 0, signed[1, 1], 0, C)
+        quantise_pass(0, 1)
+        blocks_through_pass(1, 1)
+        make_mask(1, 1)
+        make_mask(1, 0)
+        lift(2, 0, signed[1, 1])
         gather_words(5)
 
         masked(1, 0)
         masked(1, 1)
-        quantise((1, 0), da_of[1, 0][:], C)
-        make_mask(2, 0, signed[1, 1], C)
-        blocks_through(SIGN_AFTER[2, 1])
-        make_mask(2, 1, signed[2, 1], C)
-        signed[3, 0] = signed[2, 1]
-        lift(3, 0, signed[3, 0], 0, LIFT_WIDTH[3])
-        quantise((1, 1), da_of[1, 1][:], C)
+        quantise_pass(1, 0)
+        make_mask(2, 0)
+        blocks_through_pass(2, 1)
+        make_mask(2, 1)
+        lift(3, 0, signed[2, 1], LIFT_WIDTH[3])
+        quantise_pass(1, 1)
 
         masked(2, 0)
         masked(2, 1)
         make_mask(3, 1)
-        make_mask(3, 0, signed[3, 0], C)
-        quantise((2, 0), da_of[2, 0][:], C)
-        signed[4, 0] = da_of[2, 0]
-        lift(4, 0, signed[4, 0], 0, LIFT_WIDTH[4])
-        quantise((2, 1), da_of[2, 1][:], C)
+        make_mask(3, 0)
+        quantise_pass(2, 0)
+        lift(4, 0, da_of[2, 0], LIFT_WIDTH[4])
+        quantise_pass(2, 1)
 
         masked(3, 0)
         masked(3, 1)
-        quantise((3, 0), da_of[3, 0][:], C)
-        make_mask(4, 0, signed[4, 0], C)
-        quantise((3, 1), da_of[3, 1][:], C)
-        signed[5, 0] = da_of[3, 1]
-        lift(5, 0, signed[5, 0], 0, LIFT_WIDTH[5])
+        quantise_pass(3, 0)
+        make_mask(4, 0)
+        quantise_pass(3, 1)
+        lift(5, 0, da_of[3, 1], LIFT_WIDTH[5])
         make_mask(4, 1)
 
         masked(4, 0)
         masked(4, 1)
-        quantise((4, 0), da_of[4, 0][:], C)
-        blocks_through(SIGN_AFTER[last, 0])
-        make_mask(last, 0, signed[last, 0], C)
-        quantise((4, 1), da_of[4, 1][:], C)
+        quantise_pass(4, 0)
+        make_mask(last, 0)
+        quantise_pass(4, 1)
 
-        blocks_through(E * PASSES * BLOCKS - 3)
+        blocks_through(LAST_BLOCK - 2)
         turn(last, 0, 0)
-        blocks_through(E * PASSES * BLOCKS - 1)
+        blocks_through(LAST_BLOCK)
         turn(last, 0, 1)
         second_product(0)
         masked(last, 0)
@@ -349,8 +354,8 @@ def tile_moe_bdx_mlp_relu_kernel(
         second_product(2)
         turn(last, 1, 1)
         second_product(3)
-        waiting = second_sums(last - 1)
-        quantise((last, 0), da_of[last, 0][:], C)
+        sums_for_vector = second_sums(last - 1)
+        quantise_pass(last, 0)
         accs, pieces = [], []
         for c0, width in LAST_PIECES:
             accs.append(bank("acc"))
@@ -365,10 +370,12 @@ def tile_moe_bdx_mlp_relu_kernel(
             c0, width = LAST_PIECES[n]
             quantise((last, 1, n), pieces[n][:], width)
             second_pass(accs[n][:, 0:width], last, 1, codes_of[last, 1, n][:], scales_of[last, 1, n][:])
-            if n + 1 == len(LAST_PIECES):
-                nc.vector.tensor_copy(dx[:, (last - 1) * C : last * C], waiting[:])
-            copy = nc.vector.tensor_copy if n + 1 == len(LAST_PIECES) else nc.scalar.copy
-            copy(dx[:, last * C + c0 : last * C + c0 + width], accs[n][:, 0:width])
+            target = dx[:, last * C + c0 : last * C + c0 + width]
+            if n + 1 < len(LAST_PIECES):
+                nc.scalar.copy(target, accs[n][:, 0:width])
+            else:
+                nc.vector.tensor_copy(dx[:, (last - 1) * C : last * C], sums_for_vector[:])
+                nc.vector.tensor_copy(target, accs[n][:, 0:width])
 
         for n in range(len(LAST_PIECES)):
             last_masked(n)

@@ -33,6 +33,8 @@ VECTOR_TILES = 26
 SCALAR_TILES = 8
 LIFT = 2.0**23
 SIGNED = ((1, 1), (2, 1), (3, 0), (4, 0), (5, 0))
+SIGN_BLOCK = (1, BLOCKS - 1)
+BLOCKS_AHEAD = 2
 LIFT_WIDTH = {3: 5 * C // 8, 4: C // 2, 5: 3 * C // 8}
 EARLY_EXPERTS = 2
 FIRST_PIECE = P
@@ -113,7 +115,7 @@ def tile_moe_bdx_mlp_relu_kernel(
         load_w2_scales(0)
         last = E - 1
         for e in range(last):
-            between = e in (0, last - 1)
+            between = e not in (2, 3)
             load_a(e, 0)
             if not between:
                 load_a(e, 1)
@@ -183,6 +185,9 @@ def tile_moe_bdx_mlp_relu_kernel(
                     nc.tensor.transpose(turned[:, at : at + P], words[:, u * P : (u + 1) * P], ident[:])
             turned_of[e, s, h] = turned[:]
 
+        def sign_block(e, s):
+            return (e * PASSES + s) * BLOCKS + SIGN_BLOCK[s] + (BLOCKS_AHEAD if (e, s) == (1, 1) else 0)
+
         def turn_block(e):
             first_of_next = (e + 1) * PASSES * BLOCKS
             return first_of_next + (PASSES * BLOCKS - 1 if e < EARLY_EXPERTS else BLOCKS)
@@ -209,8 +214,9 @@ def tile_moe_bdx_mlp_relu_kernel(
                 ACT.Copy,
                 scale=gate_col[:, e * BLOCKS + b : e * BLOCKS + b + 1],
             )
-            if b == BLOCKS - 1 and (e, s) in SIGNED:
-                sign(e, s)
+            for signed_e, signed_s in SIGNED:
+                if k == sign_block(signed_e, signed_s):
+                    sign(signed_e, signed_s)
             if e > 0 and k == turn_block(e - 1):
                 for turned_s in range(PASSES):
                     for h in range(2):
@@ -219,9 +225,6 @@ def tile_moe_bdx_mlp_relu_kernel(
         def blocks_through(k):
             while len(blocks_done) <= k:
                 next_block()
-
-        def blocks_through_pass(e, s):
-            blocks_through((e * PASSES + s + 1) * BLOCKS - 1)
 
         def scale_up(target, source):
             nc.gpsimd.tensor_scalar(out=target, in0=source, scalar1=LIFT, scalar2=0.0, op0=ALU.mult, op1=ALU.add)
@@ -305,7 +308,7 @@ def tile_moe_bdx_mlp_relu_kernel(
         masked(0, 1)
         gather_bytes(4, 0, 2 * C)
         quantise_pass(0, 1)
-        blocks_through_pass(1, 1)
+        blocks_through(sign_block(1, 1))
         make_mask(1, 1)
         make_mask(1, 0)
         lift(2, 0, signed[1, 1])
@@ -315,7 +318,7 @@ def tile_moe_bdx_mlp_relu_kernel(
         masked(1, 1)
         quantise_pass(1, 0)
         make_mask(2, 0)
-        blocks_through_pass(2, 1)
+        blocks_through(sign_block(2, 1))
         make_mask(2, 1)
         lift(3, 0, signed[2, 1], LIFT_WIDTH[3])
         quantise_pass(1, 1)

@@ -28,15 +28,16 @@ HALF = C // 2
 LIST_COL = 16
 SCALE_ROWS = 4
 BANKS = 8
+PAIRS = E // 2
+WIDE = 2 * C
+GROUPS = PAIRS * PASSES
 A_ROOMS = 6
 VECTOR_TILES = 26
-SCALAR_TILES = 8
+SCALAR_TILES = 6
 LIFT = 2.0**23
-SIGNED = ((1, 1), (2, 1), (3, 0), (4, 0), (5, 0))
-SIGN_BLOCK = (1, BLOCKS - 1)
-BLOCKS_AHEAD = 2
-LIFT_WIDTH = {3: 5 * C // 8, 4: C // 2, 5: 3 * C // 8}
-EARLY_EXPERTS = 2
+SIGN_AFTER = {1: 15, 2: 22, 3: 27, 4: 32, 5: 41}
+TURN_AFTER = {(0, 0): 15, (0, 1): 15, (1, 0): 22, (1, 1): 22, (2, 0): 28, (2, 1): 28, (3, 0): 31, (3, 1): 34, (4, 0): 39, (4, 1): 42}
+LIFT_WIDTH = {4: 5 * WIDE // 8, 5: 5 * WIDE // 8}
 FIRST_PIECE = P
 SCALE_GROUPS = {0: 1, 1: 1, 2: 2, 4: 2}
 W1_PIECES = 3
@@ -69,18 +70,20 @@ def tile_moe_bdx_mlp_relu_kernel(
         gate_rows = keep.tile([P, P], F32, name="gate_rows")
         gate_col = keep.tile([P, S // P], F32, name="gate_col")
         dx = keep.tile([P, S], F32, name="dx")
-        lifted = keep.tile([P, 4 * C], BF16, name="lifted")
+        signs = keep.tile([P, 2, 2 * WIDE], BF16, name="signs")
         a_sb = {}
+        last = GROUPS - 1
 
         nc.gpsimd.memset(dy_s[:].bitcast(I32), 0)
         make_identity(nc, ident[:])
 
-        def load_a(e, s):
-            rows = a[s * PASS : (s + 1) * PASS, e * C : (e + 1) * C]
-            a_sb[e, s] = keep.tile([P, 4, C], F32, name="a_sb", tag="a_room%d" % (len(a_sb) % A_ROOMS))
-            step = 2 if (e, s) == (0, 0) else 4
-            for t in range(0, 4, step):
-                nc.sync.dma_start(a_sb[e, s][:, t : t + step, :], rows.rearrange("(p t) c -> p t c", t=4)[:, t : t + step, :])
+        def load_a(g, u):
+            pair, s = divmod(g, PASSES)
+            rows = a[s * PASS : (s + 1) * PASS, pair * WIDE : (pair + 1) * WIDE].rearrange("(p u d) c -> p u d c", u=2, d=2)
+            a_sb[g, u] = keep.tile([P, 2, WIDE], F32, name="a_sb", tag="a_room%d" % (len(a_sb) % A_ROOMS))
+            step = C if (g, u) == (last, 1) else WIDE
+            for c in range(0, WIDE, step):
+                nc.sync.dma_start(a_sb[g, u][:, :, c : c + step], rows[:, u, :, c : c + step])
 
         def load_w2(e):
             nc.sync.dma_start(w2_w[e][:].bitcast(I32), w2_words[e, 0].bitcast(I32))
@@ -113,17 +116,17 @@ def tile_moe_bdx_mlp_relu_kernel(
         nc.sync.dma_start(dy_w[:], dy_words[0].rearrange("p t d -> p (t d)").bitcast(I32))
         load_w2(0)
         load_w2_scales(0)
-        last = E - 1
-        for e in range(last):
-            between = e not in (2, 3)
-            load_a(e, 0)
-            if not between:
-                load_a(e, 1)
-            load_w2(e + 1)
-            if e + 1 in SCALE_GROUPS:
-                load_w2_scales(e + 1)
-            if between:
-                load_a(e, 1)
+        load_a(0, 0)
+        load_w2(1)
+        load_w2_scales(1)
+        load_a(0, 1)
+        for g in range(1, last):
+            if g % PASSES == 0:
+                load_w2(g)
+                load_w2_scales(g)
+                load_w2(g + 1)
+            load_a(g, 0)
+            load_a(g, 1)
         load_a(last, 0)
         load_w1_scales()
         load_w1(0)
@@ -146,8 +149,11 @@ def tile_moe_bdx_mlp_relu_kernel(
         nc.tensor.transpose(gate_ps[:, 0:P], gate_rows[:], ident[:])
         nc.scalar.activation(gate_col[:], gate_ps[:, 0 : S // P], ACT.Copy)
 
-        g_s, g_w, rounded, signed, mask_of, turned_of, da_of, codes_of, scales_of = {}, {}, {}, {}, {}, {}, {}, {}, {}
+        g_s, g_w, rounded, mask_of, turned_of, da_of, codes_of, scales_of = {}, {}, {}, {}, {}, {}, {}, {}
         blocks_done = []
+
+        def expert(g, j):
+            return g // PASSES * 2 + j
 
         def slots(e, c0, c1):
             return offs_sb[:, (e * C + c0) // LIST_COL : (e * C + c1) // LIST_COL]
@@ -167,35 +173,40 @@ def tile_moe_bdx_mlp_relu_kernel(
         def paired(tile):
             return tile.rearrange("p (u c d) -> p u c d", u=2, d=2)
 
-        def saved(e, s):
-            return a_sb[e, s][:].rearrange("p (u d) c -> p u c d", u=2)
+        def saved(g, u):
+            return a_sb[g, u][:].rearrange("p d c -> p c d")
 
-        def sign(e, s):
-            if s == 1:
-                signed[e, s] = made_on_scalar(4 * C, BF16, "sign")
-            c0 = 0 if s == 1 else LIFT_WIDTH[e]
-            nc.scalar.activation(paired(signed[e, s][:])[:, :, c0:C, :], saved(e, s)[:, :, c0:C, :], ACT.Sign)
+        def signed(g, u):
+            if g == last:
+                room = a_sb[last - 1, 1][:].rearrange("p d c -> p (d c)").bitcast(BF16)[:, 0 : 2 * WIDE]
+            else:
+                room = signs[:, u, :]
+            return room.rearrange("p (c d) -> p c d", d=2)
 
-        def turn(e, s, h):
+        def sign(g):
+            u, c0 = (0, LIFT_WIDTH[g]) if g in LIFT_WIDTH else (1, 0)
+            nc.scalar.activation(signed(g, u)[:, c0:WIDE, :], saved(g, u)[:, c0:WIDE, :], ACT.Sign)
+
+        def lift(g, u=0):
+            width = LIFT_WIDTH.get(g, WIDE)
+            nc.gpsimd.tensor_scalar(
+                out=signed(g, u)[:, 0:width, :], in0=saved(g, u)[:, 0:width, :], scalar1=LIFT, scalar2=0.0, op0=ALU.mult, op1=ALU.add
+            )
+
+        def turn(g, j, h):
             turned = bank("turned")
-            for j in (1, 0):
-                words = rounded[e, s][:, (2 * h + j) * PASS : (2 * h + j + 1) * PASS].bitcast(F32)
+            for b in (1, 0):
+                words = rounded[g, j][:, (2 * h + b) * PASS : (2 * h + b + 1) * PASS].bitcast(F32)
                 for u in range(2):
-                    at = (2 * u + j) * P
+                    at = (2 * u + b) * P
                     nc.tensor.transpose(turned[:, at : at + P], words[:, u * P : (u + 1) * P], ident[:])
-            turned_of[e, s, h] = turned[:]
-
-        def sign_block(e, s):
-            return (e * PASSES + s) * BLOCKS + SIGN_BLOCK[s] + (BLOCKS_AHEAD if (e, s) == (1, 1) else 0)
-
-        def turn_block(e):
-            first_of_next = (e + 1) * PASSES * BLOCKS
-            return first_of_next + (PASSES * BLOCKS - 1 if e < EARLY_EXPERTS else BLOCKS)
+            turned_of[g, j, h] = turned[:]
 
         def next_block():
             k = len(blocks_done)
             blocks_done.append(k)
-            e, s, b = k // (PASSES * BLOCKS), k // BLOCKS % PASSES, k % BLOCKS
+            g, j, b = k // (2 * BLOCKS), k // BLOCKS % 2, k % BLOCKS
+            e, s = expert(g, j), g % PASSES
             dh = bank("dh")
             nc.tensor.matmul_mx(
                 out=dh[:],
@@ -207,40 +218,43 @@ def tile_moe_bdx_mlp_relu_kernel(
                 stop=True,
             )
             if b == 0:
-                rounded[e, s] = made_on_scalar(4 * C, BF16, "x")
+                rounded[g, j] = made_on_scalar(4 * C, BF16, "x")
             nc.scalar.activation(
-                rounded[e, s][:, b * PASS : (b + 1) * PASS].rearrange("m (u p d) -> m u p d", u=2, d=2),
+                rounded[g, j][:, b * PASS : (b + 1) * PASS].rearrange("m (u p d) -> m u p d", u=2, d=2),
                 dh[:].rearrange("m (p u d) -> m u p d", u=2, d=2),
                 ACT.Copy,
                 scale=gate_col[:, e * BLOCKS + b : e * BLOCKS + b + 1],
             )
-            for signed_e, signed_s in SIGNED:
-                if k == sign_block(signed_e, signed_s):
-                    sign(signed_e, signed_s)
-            if e > 0 and k == turn_block(e - 1):
-                for turned_s in range(PASSES):
+            for (turned_g, turned_j), at in TURN_AFTER.items():
+                if k == at:
                     for h in range(2):
-                        turn(e - 1, turned_s, h)
+                        turn(turned_g, turned_j, h)
 
         def blocks_through(k):
             while len(blocks_done) <= k:
                 next_block()
 
-        def scale_up(target, source):
-            nc.gpsimd.tensor_scalar(out=target, in0=source, scalar1=LIFT, scalar2=0.0, op0=ALU.mult, op1=ALU.add)
+        def sign_in_turn(g):
+            blocks_through(SIGN_AFTER[g])
+            sign(g)
 
-        def lift(e, s, tile, width=C):
-            signed[e, s] = tile
-            scale_up(paired(tile[:])[:, :, 0:width, :], saved(e, s)[:, :, 0:width, :])
+        def compare(target, source):
+            nc.vector.tensor_scalar(out=target, in0=source, scalar1=0.0, scalar2=None, op0=ALU.is_gt)
 
-        def make_mask(e, s):
-            mask_of[e, s] = made_on_vector(4 * C, BF16, "mask")
-            source = paired(signed[e, s][:]) if (e, s) in signed else saved(e, s)
-            nc.vector.tensor_scalar(out=paired(mask_of[e, s][:]), in0=source, scalar1=0.0, scalar2=None, op0=ALU.is_gt)
+        def make_mask(g, j):
+            mask_of[g, j] = made_on_vector(4 * C, BF16, "mask")
+            compare(paired(mask_of[g, j][:]), signs[:].rearrange("p u (c d) -> p u c d", d=2)[:, :, j * C : (j + 1) * C, :])
 
-        def masked_slots(e, s, c0, width, da):
-            mask = mask_of[e, s][:].rearrange("p (u c d) -> p c u d", u=2, d=2)
-            turned = turned_of[e, s, c0 // HALF].bitcast(BF16).rearrange("p (u c d) -> p c u d", u=2, d=2)
+        def first_half_mask(g, j):
+            mask_of[g, j] = made_on_vector(4 * C, BF16, "mask")
+            compare(paired(mask_of[g, j][:])[:, 0], signed(g, 0)[:, j * C : (j + 1) * C, :])
+
+        def second_half_mask(g, j):
+            compare(paired(mask_of[g, j][:])[:, 1], saved(g, 1)[:, j * C : (j + 1) * C, :])
+
+        def masked_slots(g, j, c0, width, da):
+            mask = mask_of[g, j][:].rearrange("p (u c d) -> p c u d", u=2, d=2)
+            turned = turned_of[g, j, c0 // HALF].bitcast(BF16).rearrange("p (u c d) -> p c u d", u=2, d=2)
             nc.vector.tensor_tensor(
                 da.rearrange("p (c u d) -> p c u d", u=2, d=2),
                 turned[:, c0 % HALF : c0 % HALF + width],
@@ -248,28 +262,28 @@ def tile_moe_bdx_mlp_relu_kernel(
                 ALU.mult,
             )
 
-        def masked(e, s):
-            if e < last:
-                blocks_through(turn_block(e))
-            da_of[e, s] = made_on_vector(4 * C, BF16, "da")
+        def masked(g, j):
+            if g < last:
+                blocks_through(TURN_AFTER[g, j])
+            da_of[g, j] = made_on_vector(4 * C, BF16, "da")
             for h in range(2):
-                masked_slots(e, s, h * HALF, HALF, da_of[e, s][:, 4 * h * HALF : 4 * (h + 1) * HALF])
+                masked_slots(g, j, h * HALF, HALF, da_of[g, j][:, 4 * h * HALF : 4 * (h + 1) * HALF])
 
         def quantise(key, da, width):
             codes_of[key] = made_on_vector(width, U32, "codes")
             scales_of[key] = ring.tile([P, width], U8, name="scales", align_bytes=64, bufs=E * PASSES - 1 + len(LAST_PIECES))
             nc.vector.quantize_mx(out=codes_of[key][:].bitcast(E5M2X4), scales=scales_of[key][:], in_=da)
 
-        def quantise_pass(e, s):
-            quantise((e, s), da_of[e, s][:], C)
+        def quantise_pass(g, j):
+            quantise((expert(g, j), g % PASSES), da_of[g, j][:], C)
 
         def second_pass(acc, e, s, codes, scales):
-            g = e * PASSES + s
-            in_piece = g % (W1_EXPERTS * PASSES)
+            n = e * PASSES + s
+            in_piece = n % (W1_EXPERTS * PASSES)
             nc.tensor.matmul_mx(
                 out=acc,
                 lhsT=w1_w[e // W1_EXPERTS][:, 2 * in_piece * K : 2 * (in_piece + 1) * K].bitcast(E2M1X4),
-                lhsT_scale=w1_s[:, g * K : (g + 1) * K],
+                lhsT_scale=w1_s[:, n * K : (n + 1) * K],
                 rhs=codes.bitcast(E5M2X4),
                 rhs_scale=scales,
                 start=(s == 0),
@@ -293,94 +307,86 @@ def tile_moe_bdx_mlp_relu_kernel(
         gather_words(1)
         gather_bytes(2, 0, 2 * C)
         gather_words(2)
-        signed[0, 0] = lifted
-        for u in range(2):
-            scale_up(paired(lifted[:])[:, u], saved(0, 0)[:, u])
-
-        make_mask(0, 0)
-        lift(0, 1, lifted)
         gather_words(3)
-        masked(0, 0)
-        gather_words(4)
-        make_mask(0, 1)
-        lift(1, 0, lifted)
-        quantise_pass(0, 0)
-        masked(0, 1)
-        gather_bytes(4, 0, 2 * C)
-        quantise_pass(0, 1)
-        blocks_through(sign_block(1, 1))
-        make_mask(1, 1)
-        make_mask(1, 0)
-        lift(2, 0, signed[1, 1])
-        gather_words(5)
+        gather_bytes(4)
+        for u in range(2):
+            lift(0, u)
+        late_gathers = [(gather_bytes, 5), (gather_words, 4), (gather_words, 5)]
 
-        masked(1, 0)
-        masked(1, 1)
-        quantise_pass(1, 0)
-        make_mask(2, 0)
-        blocks_through(sign_block(2, 1))
-        make_mask(2, 1)
-        lift(3, 0, signed[2, 1], LIFT_WIDTH[3])
-        quantise_pass(1, 1)
+        for g in range(last - 1):
+            if g > 0:
+                quantise_pass(g - 1, 0)
+            make_mask(g, 0)
+            make_mask(g, 1)
+            lift(g + 1)
+            if g > 0:
+                quantise_pass(g - 1, 1)
+            if g < len(late_gathers):
+                late_gathers[g][0](late_gathers[g][1])
+            if SIGN_AFTER[g + 1] <= TURN_AFTER[g, 1]:
+                sign_in_turn(g + 1)
+            masked(g, 0)
+            masked(g, 1)
+            if SIGN_AFTER[g + 1] > TURN_AFTER[g, 1]:
+                sign_in_turn(g + 1)
 
-        masked(2, 0)
-        masked(2, 1)
-        make_mask(3, 1)
-        make_mask(3, 0)
-        quantise_pass(2, 0)
-        lift(4, 0, da_of[2, 0], LIFT_WIDTH[4])
-        quantise_pass(2, 1)
-
-        masked(3, 0)
-        masked(3, 1)
-        quantise_pass(3, 0)
-        make_mask(4, 0)
-        quantise_pass(3, 1)
-        lift(5, 0, da_of[3, 1], LIFT_WIDTH[5])
-        make_mask(4, 1)
-
-        masked(4, 0)
-        masked(4, 1)
-        quantise_pass(4, 0)
-        make_mask(last, 0)
-        quantise_pass(4, 1)
+        g = last - 1
+        quantise_pass(g - 1, 0)
+        first_half_mask(g, 0)
+        first_half_mask(g, 1)
+        quantise_pass(g - 1, 1)
+        second_half_mask(g, 0)
+        second_half_mask(g, 1)
+        lift(last)
+        masked(g, 0)
+        sign_in_turn(last)
+        masked(g, 1)
+        quantise_pass(g, 0)
+        first_half_mask(last, 0)
+        first_half_mask(last, 1)
+        quantise_pass(g, 1)
+        second_half_mask(last, 0)
 
         blocks_through(LAST_BLOCK - 2)
         turn(last, 0, 0)
         blocks_through(LAST_BLOCK)
         turn(last, 0, 1)
         second_product(0)
+        second_half_mask(last, 1)
         masked(last, 0)
-        make_mask(last, 1)
         second_product(1)
         turn(last, 1, 0)
         second_product(2)
         turn(last, 1, 1)
         second_product(3)
-        sums_for_vector = second_sums(last - 1)
-        quantise_pass(last, 0)
-        accs, pieces = [], []
-        for c0, width in LAST_PIECES:
-            accs.append(bank("acc"))
-            second_pass(accs[-1][:, 0:width], last, 0, codes_of[last, 0][:, c0 : c0 + width], scales_of[last, 0][:, c0 : c0 + width])
+        last_e = E - 1
+        pieces = []
 
         def last_masked(n):
             c0, width = LAST_PIECES[n]
             pieces.append(made_on_vector(4 * width, BF16, "da"))
             masked_slots(last, 1, c0, width, pieces[n][:])
 
+        last_masked(0)
+        quantise_pass(last, 0)
+        sums_for_vector = second_sums(last_e - 1)
+        accs = []
+        for c0, width in LAST_PIECES:
+            accs.append(bank("acc"))
+            second_pass(accs[-1][:, 0:width], last_e, 0, codes_of[last_e, 0][:, c0 : c0 + width], scales_of[last_e, 0][:, c0 : c0 + width])
+
         def last_product(n):
             c0, width = LAST_PIECES[n]
-            quantise((last, 1, n), pieces[n][:], width)
-            second_pass(accs[n][:, 0:width], last, 1, codes_of[last, 1, n][:], scales_of[last, 1, n][:])
-            target = dx[:, last * C + c0 : last * C + c0 + width]
+            quantise((last_e, 1, n), pieces[n][:], width)
+            second_pass(accs[n][:, 0:width], last_e, 1, codes_of[last_e, 1, n][:], scales_of[last_e, 1, n][:])
+            target = dx[:, last_e * C + c0 : last_e * C + c0 + width]
             if n + 1 < len(LAST_PIECES):
                 nc.scalar.copy(target, accs[n][:, 0:width])
             else:
-                nc.vector.tensor_copy(dx[:, (last - 1) * C : last * C], sums_for_vector[:])
+                nc.vector.tensor_copy(dx[:, (last_e - 1) * C : last_e * C], sums_for_vector[:])
                 nc.vector.tensor_copy(target, accs[n][:, 0:width])
 
-        for n in range(len(LAST_PIECES)):
+        for n in range(1, len(LAST_PIECES)):
             last_masked(n)
         for n in range(len(LAST_PIECES)):
             last_product(n)

@@ -33,14 +33,15 @@ WIDE = 2 * C
 GROUPS = PAIRS * PASSES
 A_ROOMS = 6
 VECTOR_TILES = 26
-SCALAR_TILES = 6
+SCALAR_TILES = 12
 LIFT = 2.0**23
-SIGN_AFTER = {1: 15, 2: 22, 3: 27, 4: 32, 5: 41}
-TURN_AFTER = {(0, 0): 15, (0, 1): 15, (1, 0): 22, (1, 1): 22, (2, 0): 28, (2, 1): 28, (3, 0): 31, (3, 1): 34, (4, 0): 39, (4, 1): 42}
-LIFT_WIDTH = {4: 5 * WIDE // 8, 5: 5 * WIDE // 8}
+SIGN_AFTER = {1: 15, 2: 21, 3: 27, 4: 32}
+TURN_AFTER = {(0, 0): 15, (0, 1): 15, (1, 0): 22, (1, 1): 22, (2, 0): 27, (2, 1): 29, (3, 0): 31, (3, 1): 34, (4, 0): 39, (4, 1): 42}
+PASS_ORDER = ((0, 0), (0, 1), (1, 0), (1, 1), (2, 0), (3, 0), (2, 1), (3, 1), (4, 0), (4, 1), (5, 0), (5, 1))
+LIFT_WIDTH = {4: 5 * WIDE // 8, 5: C}
 FIRST_PIECE = P
 SCALE_GROUPS = {0: 1, 1: 1, 2: 2, 4: 2}
-W1_PIECES = 3
+W1_PIECES = 2
 W1_EXPERTS = E // W1_PIECES
 LAST_PIECES = ((0, HALF), (HALF, P), (HALF + P, P))
 OWN_PIECE = 320
@@ -61,17 +62,17 @@ def tile_moe_bdx_mlp_relu_kernel(
         pos2_sb = keep.tile([P, T // LIST_COL], U16, name="pos2_sb")
         dy_w = keep.tile([P, T], I32, name="dy_w", align_bytes=64)
         dy_s = keep.tile([P, T], U8, name="dy_s", align_bytes=64)
-        w2_s_group = {e0: keep.tile([P, n * H], U8, name="w2_s%d" % e0, align_bytes=64) for e0, n in SCALE_GROUPS.items()}
+        w2_s_group = {e0: keep.tile([P, n * H], U8, name="w2_s", tag="w2_s%d" % (e0 % 4), align_bytes=64) for e0, n in SCALE_GROUPS.items()}
         w2_s = [w2_s_group[e0][:, j * H : (j + 1) * H] for e0, n in SCALE_GROUPS.items() for j in range(n)]
-        w1_s = keep.tile([P, E * PASSES * K], U8, name="w1_s", align_bytes=64)
-        w1_w = [keep.tile([P, W1_EXPERTS * PASSES * 2 * K], U8, name="w1_w%d" % n, align_bytes=64) for n in range(W1_PIECES)]
-        w2_w = [keep.tile([P, 2 * H], U8, name="w2_w%d" % e, align_bytes=64) for e in range(E)]
+        w1_s = keep.tile([P, E * PASSES * K], U8, name="w1_s", tag="w2_s2", align_bytes=64)
+        w2_w = [keep.tile([P, 2 * H], U8, name="w2_w", tag="w%d" % (e % 4), align_bytes=64) for e in range(E)]
+        w1_w = [keep.tile([P, W1_EXPERTS * PASSES * 2 * K], U8, name="w1_w", tag="w%d" % (2 + n), align_bytes=64) for n in range(W1_PIECES)]
         ident = keep.tile([P, P], F32, name="ident")
         gate_rows = keep.tile([P, P], F32, name="gate_rows")
         gate_col = keep.tile([P, S // P], F32, name="gate_col")
         dx = keep.tile([P, S], F32, name="dx")
         signs = keep.tile([P, 2, 2 * WIDE], BF16, name="signs")
-        a_sb = {}
+        a_sb, room_of = {}, {}
         last = GROUPS - 1
 
         nc.gpsimd.memset(dy_s[:].bitcast(I32), 0)
@@ -80,7 +81,8 @@ def tile_moe_bdx_mlp_relu_kernel(
         def load_a(g, u):
             pair, s = divmod(g, PASSES)
             rows = a[s * PASS : (s + 1) * PASS, pair * WIDE : (pair + 1) * WIDE].rearrange("(p u d) c -> p u d c", u=2, d=2)
-            a_sb[g, u] = keep.tile([P, 2, WIDE], F32, name="a_sb", tag="a_room%d" % (len(a_sb) % A_ROOMS))
+            room_of[g, u] = "a_room%d" % (len(a_sb) % A_ROOMS)
+            a_sb[g, u] = keep.tile([P, 2, WIDE], F32, name="a_sb", tag=room_of[g, u])
             step = C if (g, u) == (last, 1) else WIDE
             for c in range(0, WIDE, step):
                 nc.sync.dma_start(a_sb[g, u][:, :, c : c + step], rows[:, u, :, c : c + step])
@@ -120,21 +122,29 @@ def tile_moe_bdx_mlp_relu_kernel(
         load_w2(1)
         load_w2_scales(1)
         load_a(0, 1)
-        for g in range(1, last):
-            if g % PASSES == 0:
-                load_w2(g)
-                load_w2_scales(g)
-                load_w2(g + 1)
-            load_a(g, 0)
-            load_a(g, 1)
-        load_a(last, 0)
-        load_w1_scales()
-        load_w1(0)
-        load_a(last, 1)
-        for n in range(1, W1_PIECES):
-            load_w1(n)
-        nc.sync.dma_start(pos1_sb[:], pos1)
-        nc.sync.dma_start(pos2_sb[:], pos2)
+        load_a(1, 0)
+        load_a(1, 1)
+        load_w2(2)
+        load_w2_scales(2)
+        load_a(2, 0)
+        load_a(2, 1)
+        load_w2(3)
+        load_a(3, 0)
+        load_a(3, 1)
+        load_w2(4)
+        load_w2_scales(4)
+        load_a(4, 0)
+        load_w2(5)
+
+        def last_loads():
+            load_a(4, 1)
+            load_a(last, 0)
+            load_a(last, 1)
+            load_w1_scales()
+            for n in range(W1_PIECES):
+                load_w1(n)
+            nc.sync.dma_start(pos1_sb[:], pos1)
+            nc.sync.dma_start(pos2_sb[:], pos2)
 
         def bank(name):
             return psum.tile([P, PASS], F32, name=name, tag="bank", bufs=BANKS)
@@ -196,7 +206,7 @@ def tile_moe_bdx_mlp_relu_kernel(
         def turn(g, j, h):
             turned = bank("turned")
             for b in (1, 0):
-                words = rounded[g, j][:, (2 * h + b) * PASS : (2 * h + b + 1) * PASS].bitcast(F32)
+                words = rounded[g, j, h][:, b * PASS : (b + 1) * PASS].bitcast(F32)
                 for u in range(2):
                     at = (2 * u + b) * P
                     nc.tensor.transpose(turned[:, at : at + P], words[:, u * P : (u + 1) * P], ident[:])
@@ -205,7 +215,7 @@ def tile_moe_bdx_mlp_relu_kernel(
         def next_block():
             k = len(blocks_done)
             blocks_done.append(k)
-            g, j, b = k // (2 * BLOCKS), k // BLOCKS % 2, k % BLOCKS
+            (g, j), b = PASS_ORDER[k // BLOCKS], k % BLOCKS
             e, s = expert(g, j), g % PASSES
             dh = bank("dh")
             nc.tensor.matmul_mx(
@@ -217,14 +227,20 @@ def tile_moe_bdx_mlp_relu_kernel(
                 start=True,
                 stop=True,
             )
-            if b == 0:
-                rounded[g, j] = made_on_scalar(4 * C, BF16, "x")
+            if b % 2 == 0:
+                behind = [n for n, at in SIGN_AFTER.items() if at == k - 1 and n not in LIFT_WIDTH]
+                if behind:
+                    rounded[g, j, b // 2] = keep.tile([P, 2 * PASS], BF16, name="x", tag=room_of[behind[0], 1])
+                else:
+                    rounded[g, j, b // 2] = made_on_scalar(2 * PASS, BF16, "x")
             nc.scalar.activation(
-                rounded[g, j][:, b * PASS : (b + 1) * PASS].rearrange("m (u p d) -> m u p d", u=2, d=2),
+                rounded[g, j, b // 2][:, b % 2 * PASS : (b % 2 + 1) * PASS].rearrange("m (u p d) -> m u p d", u=2, d=2),
                 dh[:].rearrange("m (p u d) -> m u p d", u=2, d=2),
                 ACT.Copy,
                 scale=gate_col[:, e * BLOCKS + b : e * BLOCKS + b + 1],
             )
+            if k == SIGN_AFTER[2] + 1:
+                last_loads()
             for (turned_g, turned_j), at in TURN_AFTER.items():
                 if k == at:
                     for h in range(2):
@@ -247,7 +263,8 @@ def tile_moe_bdx_mlp_relu_kernel(
 
         def first_half_mask(g, j):
             mask_of[g, j] = made_on_vector(4 * C, BF16, "mask")
-            compare(paired(mask_of[g, j][:])[:, 0], signed(g, 0)[:, j * C : (j + 1) * C, :])
+            source = saved(g, 0) if (g, j) == (last, 1) else signed(g, 0)
+            compare(paired(mask_of[g, j][:])[:, 0], source[:, j * C : (j + 1) * C, :])
 
         def second_half_mask(g, j):
             compare(paired(mask_of[g, j][:])[:, 1], saved(g, 1)[:, j * C : (j + 1) * C, :])
@@ -339,7 +356,6 @@ def tile_moe_bdx_mlp_relu_kernel(
         second_half_mask(g, 1)
         lift(last)
         masked(g, 0)
-        sign_in_turn(last)
         masked(g, 1)
         quantise_pass(g, 0)
         first_half_mask(last, 0)

@@ -35,10 +35,10 @@ A_ROOMS = 6
 VECTOR_TILES = 26
 SCALAR_TILES = 12
 LIFT = 2.0**23
-SIGN_AFTER = {1: 15, 2: 21, 3: 27, 4: 32}
+SIGN_AFTER = {1: 15, 2: 21, 3: 27, 4: 32, 5: 41}
 TURN_AFTER = {(0, 0): 15, (0, 1): 15, (1, 0): 22, (1, 1): 22, (2, 0): 27, (2, 1): 29, (3, 0): 31, (3, 1): 34, (4, 0): 39, (4, 1): 42}
 PASS_ORDER = ((0, 0), (0, 1), (1, 0), (1, 1), (2, 0), (3, 0), (2, 1), (3, 1), (4, 0), (4, 1), (5, 0), (5, 1))
-LIFT_WIDTH = {4: 5 * WIDE // 8, 5: C}
+LIFT_WIDTH = {4: 5 * WIDE // 8, 5: 5 * WIDE // 8}
 FIRST_PIECE = P
 SCALE_GROUPS = {0: 1, 1: 1, 2: 2, 4: 2}
 W1_PIECES = 2
@@ -263,8 +263,7 @@ def tile_moe_bdx_mlp_relu_kernel(
 
         def first_half_mask(g, j):
             mask_of[g, j] = made_on_vector(4 * C, BF16, "mask")
-            source = saved(g, 0) if (g, j) == (last, 1) else signed(g, 0)
-            compare(paired(mask_of[g, j][:])[:, 0], source[:, j * C : (j + 1) * C, :])
+            compare(paired(mask_of[g, j][:])[:, 0], signed(g, 0)[:, j * C : (j + 1) * C, :])
 
         def second_half_mask(g, j):
             compare(paired(mask_of[g, j][:])[:, 1], saved(g, 1)[:, j * C : (j + 1) * C, :])
@@ -356,6 +355,7 @@ def tile_moe_bdx_mlp_relu_kernel(
         second_half_mask(g, 1)
         lift(last)
         masked(g, 0)
+        sign_in_turn(last)
         masked(g, 1)
         quantise_pass(g, 0)
         first_half_mask(last, 0)

@@ -36,16 +36,16 @@ VECTOR_TILES = 26
 SCALAR_TILES = 12
 LIFT = 2.0**23
 SIGN_AFTER = {1: 15, 2: 21, 3: 27, 4: 32, 5: 41}
-TURN_AFTER = {(0, 0): 15, (0, 1): 15, (1, 0): 22, (1, 1): 22, (2, 0): 27, (2, 1): 29, (3, 0): 31, (3, 1): 34, (4, 0): 39, (4, 1): 42}
+TURN_AFTER = {(0, 1): 15, (0, 0): 15, (1, 1): 22, (1, 0): 22, (2, 0): 27, (2, 1): 29, (3, 0): 31, (3, 1): 34, (4, 0): 39, (4, 1): 42}
 PASS_ORDER = ((0, 0), (0, 1), (1, 0), (1, 1), (2, 0), (3, 0), (2, 1), (3, 1), (4, 0), (4, 1), (5, 0), (5, 1))
-LIFT_WIDTH = {4: 5 * WIDE // 8, 5: 5 * WIDE // 8}
+LIFT_WIDTH = {4: 11 * WIDE // 16, 5: 5 * WIDE // 8}
 FIRST_PIECE = P
 SCALE_GROUPS = {0: 1, 1: 1, 2: 2, 4: 2}
 W1_PIECES = 2
 W1_EXPERTS = E // W1_PIECES
 LAST_PIECES = ((0, HALF), (HALF, P), (HALF + P, P))
-OWN_PIECE = 320
-OUT_PIECES = (160, 384, 320, 224, 128)
+OWN_PIECE = 256
+OUT_PIECES = (128, 384, 352, 288, 128)
 
 
 def tile_moe_bdx_mlp_relu_kernel(
@@ -243,7 +243,7 @@ def tile_moe_bdx_mlp_relu_kernel(
                 last_loads()
             for (turned_g, turned_j), at in TURN_AFTER.items():
                 if k == at:
-                    for h in range(2):
+                    for h in (1, 0):
                         turn(turned_g, turned_j, h)
 
         def blocks_through(k):
@@ -332,8 +332,8 @@ def tile_moe_bdx_mlp_relu_kernel(
         for g in range(last - 1):
             if g > 0:
                 quantise_pass(g - 1, 0)
-            make_mask(g, 0)
             make_mask(g, 1)
+            make_mask(g, 0)
             lift(g + 1)
             if g > 0:
                 quantise_pass(g - 1, 1)

@@ -35,10 +35,10 @@ A_ROOMS = 6
 VECTOR_TILES = 26
 SCALAR_TILES = 12
 LIFT = 2.0**23
-SIGN_AFTER = {1: 15, 2: 21, 3: 27, 4: 32, 5: 41}
+SIGN_AFTER = {1: 15, 2: 21, 3: 27, 5: 41}
 TURN_AFTER = {(0, 1): 15, (0, 0): 15, (1, 1): 22, (1, 0): 22, (2, 0): 27, (2, 1): 29, (3, 0): 31, (3, 1): 34, (4, 0): 39, (4, 1): 42}
 PASS_ORDER = ((0, 0), (0, 1), (1, 0), (1, 1), (2, 0), (3, 0), (2, 1), (3, 1), (4, 0), (4, 1), (5, 0), (5, 1))
-LIFT_WIDTH = {4: 11 * WIDE // 16, 5: 5 * WIDE // 8}
+LIFT_WIDTH = {5: 5 * WIDE // 8}
 FIRST_PIECE = P
 SCALE_GROUPS = {0: 1, 1: 1, 2: 2, 4: 2}
 W1_PIECES = 2
@@ -339,12 +339,10 @@ def tile_moe_bdx_mlp_relu_kernel(
                 quantise_pass(g - 1, 1)
             if g < len(late_gathers):
                 late_gathers[g][0](late_gathers[g][1])
-            if SIGN_AFTER[g + 1] <= TURN_AFTER[g, 1]:
+            if g + 1 in SIGN_AFTER:
                 sign_in_turn(g + 1)
             masked(g, 0)
             masked(g, 1)
-            if SIGN_AFTER[g + 1] > TURN_AFTER[g, 1]:
-                sign_in_turn(g + 1)
 
         g = last - 1
         quantise_pass(g - 1, 0)

@@ -35,13 +35,13 @@ A_ROOMS = 6
 VECTOR_TILES = 26
 SCALAR_TILES = 12
 LIFT = 2.0**23
-SIGN_AFTER = {1: 15, 2: 21, 3: 27, 5: 41}
-TURN_AFTER = {(0, 1): 15, (0, 0): 15, (1, 1): 22, (1, 0): 22, (2, 0): 27, (2, 1): 29, (3, 0): 31, (3, 1): 34, (4, 0): 39, (4, 1): 42}
+SIGN_AFTER = {1: 15, 2: 21, 3: 27, 4: 33}
+TURN_AFTER = {(0, 1): 15, (0, 0): 15, (1, 1): 22, (1, 0): 22, (2, 0): 27, (2, 1): 29, (3, 0): 33, (3, 1): 35, (4, 0): 39, (4, 1): 41}
 PASS_ORDER = ((0, 0), (0, 1), (1, 0), (1, 1), (2, 0), (3, 0), (2, 1), (3, 1), (4, 0), (4, 1), (5, 0), (5, 1))
-LIFT_WIDTH = {5: 5 * WIDE // 8}
+EXTRA_LIFT = {1: WIDE // 8, 3: WIDE // 4}
 FIRST_PIECE = P
 SCALE_GROUPS = {0: 1, 1: 1, 2: 2, 4: 2}
-W1_PIECES = 2
+W1_PIECES = 1
 W1_EXPERTS = E // W1_PIECES
 LAST_PIECES = ((0, HALF), (HALF, P), (HALF + P, P))
 OWN_PIECE = 256
@@ -65,8 +65,8 @@ def tile_moe_bdx_mlp_relu_kernel(
         w2_s_group = {e0: keep.tile([P, n * H], U8, name="w2_s", tag="w2_s%d" % (e0 % 4), align_bytes=64) for e0, n in SCALE_GROUPS.items()}
         w2_s = [w2_s_group[e0][:, j * H : (j + 1) * H] for e0, n in SCALE_GROUPS.items() for j in range(n)]
         w1_s = keep.tile([P, E * PASSES * K], U8, name="w1_s", tag="w2_s2", align_bytes=64)
-        w2_w = [keep.tile([P, 2 * H], U8, name="w2_w", tag="w%d" % (e % 4), align_bytes=64) for e in range(E)]
-        w1_w = [keep.tile([P, W1_EXPERTS * PASSES * 2 * K], U8, name="w1_w", tag="w%d" % (2 + n), align_bytes=64) for n in range(W1_PIECES)]
+        w2_w = [keep.tile([P, 2 * H], U8, name="w2_w", tag="w%d" % (0, 1, 2, 3, 0, 2)[e], align_bytes=64) for e in range(E)]
+        w1_w = [keep.tile([P, W1_EXPERTS * PASSES * 2 * K], U8, name="w1_w", tag="w3", align_bytes=64) for n in range(W1_PIECES)]
         ident = keep.tile([P, P], F32, name="ident")
         gate_rows = keep.tile([P, P], F32, name="gate_rows")
         gate_col = keep.tile([P, S // P], F32, name="gate_col")
@@ -78,14 +78,12 @@ def tile_moe_bdx_mlp_relu_kernel(
         nc.gpsimd.memset(dy_s[:].bitcast(I32), 0)
         make_identity(nc, ident[:])
 
-        def load_a(g, u):
+        def load_a(g, u, room, c0=0, c1=WIDE):
             pair, s = divmod(g, PASSES)
             rows = a[s * PASS : (s + 1) * PASS, pair * WIDE : (pair + 1) * WIDE].rearrange("(p u d) c -> p u d c", u=2, d=2)
-            room_of[g, u] = "a_room%d" % (len(a_sb) % A_ROOMS)
-            a_sb[g, u] = keep.tile([P, 2, WIDE], F32, name="a_sb", tag=room_of[g, u])
-            step = C if (g, u) == (last, 1) else WIDE
-            for c in range(0, WIDE, step):
-                nc.sync.dma_start(a_sb[g, u][:, :, c : c + step], rows[:, u, :, c : c + step])
+            room_of[g, u, c0] = room if room == "w2_s1" else "a_room%d" % room
+            a_sb[g, u, c0] = keep.tile([P, 2, c1 - c0], F32, name="a_sb", tag=room_of[g, u, c0], align_bytes=64)
+            nc.sync.dma_start(a_sb[g, u, c0][:], rows[:, u, :, c0:c1])
 
         def load_w2(e):
             nc.sync.dma_start(w2_w[e][:].bitcast(I32), w2_words[e, 0].bitcast(I32))
@@ -118,28 +116,28 @@ def tile_moe_bdx_mlp_relu_kernel(
         nc.sync.dma_start(dy_w[:], dy_words[0].rearrange("p t d -> p (t d)").bitcast(I32))
         load_w2(0)
         load_w2_scales(0)
-        load_a(0, 0)
+        load_a(0, 0, 0)
         load_w2(1)
         load_w2_scales(1)
-        load_a(0, 1)
-        load_a(1, 0)
-        load_a(1, 1)
+        load_a(0, 1, 1)
+        load_a(1, 0, 2)
+        load_a(1, 1, 3)
         load_w2(2)
         load_w2_scales(2)
-        load_a(2, 0)
-        load_a(2, 1)
+        load_a(2, 0, 4)
+        load_a(2, 1, 5)
         load_w2(3)
-        load_a(3, 0)
-        load_a(3, 1)
+        load_a(3, 0, 0)
+        load_a(3, 1, 1)
         load_w2(4)
         load_w2_scales(4)
-        load_a(4, 0)
+        load_a(4, 1, "w2_s1")
+        load_a(4, 0, 2)
         load_w2(5)
 
         def last_loads():
-            load_a(4, 1)
-            load_a(last, 0)
-            load_a(last, 1)
+            load_a(last, 0, 4)
+            load_a(last, 1, 3)
             load_w1_scales()
             for n in range(W1_PIECES):
                 load_w1(n)
@@ -183,24 +181,20 @@ def tile_moe_bdx_mlp_relu_kernel(
         def paired(tile):
             return tile.rearrange("p (u c d) -> p u c d", u=2, d=2)
 
-        def saved(g, u):
-            return a_sb[g, u][:].rearrange("p d c -> p c d")
+        def saved(g, u, c0=0):
+            return a_sb[g, u, c0][:].rearrange("p d c -> p c d")
 
-        def signed(g, u):
-            if g == last:
-                room = a_sb[last - 1, 1][:].rearrange("p d c -> p (d c)").bitcast(BF16)[:, 0 : 2 * WIDE]
-            else:
-                room = signs[:, u, :]
-            return room.rearrange("p (c d) -> p c d", d=2)
+        def signed(u):
+            return signs[:, u, :].rearrange("p (c d) -> p c d", d=2)
 
         def sign(g):
-            u, c0 = (0, LIFT_WIDTH[g]) if g in LIFT_WIDTH else (1, 0)
-            nc.scalar.activation(signed(g, u)[:, c0:WIDE, :], saved(g, u)[:, c0:WIDE, :], ACT.Sign)
+            source = saved(g, 1)
+            c0, c1 = EXTRA_LIFT.get(g, 0), C if g == last - 1 else WIDE
+            nc.scalar.activation(signed(1)[:, c0:c1, :], source[:, c0:c1, :], ACT.Sign)
 
-        def lift(g, u=0):
-            width = LIFT_WIDTH.get(g, WIDE)
+        def lift(g, u=0, width=WIDE):
             nc.gpsimd.tensor_scalar(
-                out=signed(g, u)[:, 0:width, :], in0=saved(g, u)[:, 0:width, :], scalar1=LIFT, scalar2=0.0, op0=ALU.mult, op1=ALU.add
+                out=signed(u)[:, 0:width, :], in0=saved(g, u)[:, 0:width, :], scalar1=LIFT, scalar2=0.0, op0=ALU.mult, op1=ALU.add
             )
 
         def turn(g, j, h):
@@ -228,9 +222,9 @@ def tile_moe_bdx_mlp_relu_kernel(
                 stop=True,
             )
             if b % 2 == 0:
-                behind = [n for n, at in SIGN_AFTER.items() if at == k - 1 and n not in LIFT_WIDTH]
+                behind = [n for n, at in SIGN_AFTER.items() if at == k - 1 and n < 4]
                 if behind:
-                    rounded[g, j, b // 2] = keep.tile([P, 2 * PASS], BF16, name="x", tag=room_of[behind[0], 1])
+                    rounded[g, j, b // 2] = keep.tile([P, 2 * PASS], BF16, name="x", tag=room_of[behind[0], 1, 0], align_bytes=64)
                 else:
                     rounded[g, j, b // 2] = made_on_scalar(2 * PASS, BF16, "x")
             nc.scalar.activation(
@@ -261,12 +255,11 @@ def tile_moe_bdx_mlp_relu_kernel(
             mask_of[g, j] = made_on_vector(4 * C, BF16, "mask")
             compare(paired(mask_of[g, j][:]), signs[:].rearrange("p u (c d) -> p u c d", d=2)[:, :, j * C : (j + 1) * C, :])
 
-        def first_half_mask(g, j):
-            mask_of[g, j] = made_on_vector(4 * C, BF16, "mask")
-            compare(paired(mask_of[g, j][:])[:, 0], signed(g, 0)[:, j * C : (j + 1) * C, :])
-
-        def second_half_mask(g, j):
-            compare(paired(mask_of[g, j][:])[:, 1], saved(g, 1)[:, j * C : (j + 1) * C, :])
+        def half_mask(g, j, u):
+            if (g, j) not in mask_of:
+                mask_of[g, j] = made_on_vector(4 * C, BF16, "mask")
+            source = signed(0) if u == 0 else saved(g, 1)
+            compare(paired(mask_of[g, j][:])[:, u], source[:, j * C : (j + 1) * C, :])
 
         def masked_slots(g, j, c0, width, da):
             mask = mask_of[g, j][:].rearrange("p (u c d) -> p c u d", u=2, d=2)
@@ -334,6 +327,8 @@ def tile_moe_bdx_mlp_relu_kernel(
                 quantise_pass(g - 1, 0)
             make_mask(g, 1)
             make_mask(g, 0)
+            if g + 1 in EXTRA_LIFT:
+                lift(g + 1, 1, EXTRA_LIFT[g + 1])
             lift(g + 1)
             if g > 0:
                 quantise_pass(g - 1, 1)
@@ -346,33 +341,30 @@ def tile_moe_bdx_mlp_relu_kernel(
 
         g = last - 1
         quantise_pass(g - 1, 0)
-        first_half_mask(g, 0)
-        first_half_mask(g, 1)
-        quantise_pass(g - 1, 1)
-        second_half_mask(g, 0)
-        second_half_mask(g, 1)
+        half_mask(g, 1, 1)
+        make_mask(g, 0)
+        half_mask(g, 1, 0)
         lift(last)
+        quantise_pass(g - 1, 1)
         masked(g, 0)
-        sign_in_turn(last)
         masked(g, 1)
         quantise_pass(g, 0)
-        first_half_mask(last, 0)
-        first_half_mask(last, 1)
+        half_mask(last, 0, 0)
+        half_mask(last, 1, 0)
         quantise_pass(g, 1)
-        second_half_mask(last, 0)
+        half_mask(last, 0, 1)
 
         blocks_through(LAST_BLOCK - 2)
         turn(last, 0, 0)
         blocks_through(LAST_BLOCK)
         turn(last, 0, 1)
-        second_product(0)
-        second_half_mask(last, 1)
-        masked(last, 0)
-        second_product(1)
         turn(last, 1, 0)
-        second_product(2)
+        second_product(0)
         turn(last, 1, 1)
-        second_product(3)
+        half_mask(last, 1, 1)
+        masked(last, 0)
+        for e in range(1, E - 2):
+            second_product(e)
         last_e = E - 1
         pieces = []
 

@@ -31,14 +31,14 @@ BANKS = 8
 PAIRS = E // 2
 WIDE = 2 * C
 GROUPS = PAIRS * PASSES
-A_ROOMS = 6
+A_ROOMS = 3
 VECTOR_TILES = 26
-SCALAR_TILES = 12
+SCALAR_TILES = 14
 LIFT = 2.0**23
-SIGN_AFTER = {1: 15, 2: 21, 3: 27, 4: 33}
-TURN_AFTER = {(0, 1): 15, (0, 0): 15, (1, 1): 22, (1, 0): 22, (2, 0): 27, (2, 1): 29, (3, 0): 33, (3, 1): 35, (4, 0): 39, (4, 1): 41}
+SIGN_AFTER = {(1, 2): 13, (1, 3): 15, (2, 3): 21, (3, 3): 27, (4, 2): 33, (4, 3): 35, (5, 2): 40}
+TURN_AFTER = {(0, 1): 15, (0, 0): 15, (1, 1): 23, (1, 0): 23, (2, 1): 31, (2, 0): 31, (3, 1): 36, (3, 0): 36, (4, 0): 40, (4, 1): 41}
 PASS_ORDER = ((0, 0), (0, 1), (1, 0), (1, 1), (2, 0), (3, 0), (2, 1), (3, 1), (4, 0), (4, 1), (5, 0), (5, 1))
-EXTRA_LIFT = {1: WIDE // 8, 3: WIDE // 4}
+LIFTED_QUARTERS = (4, 2, 3, 3, 2, 2)
 FIRST_PIECE = P
 SCALE_GROUPS = {0: 1, 1: 1, 2: 2, 4: 2}
 W1_PIECES = 1
@@ -71,19 +71,22 @@ def tile_moe_bdx_mlp_relu_kernel(
         gate_rows = keep.tile([P, P], F32, name="gate_rows")
         gate_col = keep.tile([P, S // P], F32, name="gate_col")
         dx = keep.tile([P, S], F32, name="dx")
-        signs = keep.tile([P, 2, 2 * WIDE], BF16, name="signs")
-        a_sb, room_of = {}, {}
+        lifted = keep.tile([P, 4 * WIDE], BF16, name="lifted")
+        a_sb = {}
         last = GROUPS - 1
 
         nc.gpsimd.memset(dy_s[:].bitcast(I32), 0)
         make_identity(nc, ident[:])
 
-        def load_a(g, u, room, c0=0, c1=WIDE):
+        def load_a(g):
             pair, s = divmod(g, PASSES)
             rows = a[s * PASS : (s + 1) * PASS, pair * WIDE : (pair + 1) * WIDE].rearrange("(p u d) c -> p u d c", u=2, d=2)
-            room_of[g, u, c0] = room if room == "w2_s1" else "a_room%d" % room
-            a_sb[g, u, c0] = keep.tile([P, 2, c1 - c0], F32, name="a_sb", tag=room_of[g, u, c0], align_bytes=64)
-            nc.sync.dma_start(a_sb[g, u, c0][:], rows[:, u, :, c0:c1])
+            a_sb[g] = keep.tile([P, 2, 2, WIDE], F32, name="a_sb", tag="a_room%d" % (g % A_ROOMS))
+            return [lambda u=u: nc.sync.dma_start(a_sb[g][:, u], rows[:, u]) for u in range(2)]
+
+        def load_group(g):
+            for load in load_a(g):
+                load()
 
         def load_w2(e):
             nc.sync.dma_start(w2_w[e][:].bitcast(I32), w2_words[e, 0].bitcast(I32))
@@ -116,33 +119,26 @@ def tile_moe_bdx_mlp_relu_kernel(
         nc.sync.dma_start(dy_w[:], dy_words[0].rearrange("p t d -> p (t d)").bitcast(I32))
         load_w2(0)
         load_w2_scales(0)
-        load_a(0, 0, 0)
+        first_half, second_half = load_a(0)
+        first_half()
         load_w2(1)
         load_w2_scales(1)
-        load_a(0, 1, 1)
-        load_a(1, 0, 2)
-        load_a(1, 1, 3)
+        second_half()
+        load_group(1)
         load_w2(2)
         load_w2_scales(2)
-        load_a(2, 0, 4)
-        load_a(2, 1, 5)
+        load_group(2)
         load_w2(3)
-        load_a(3, 0, 0)
-        load_a(3, 1, 1)
+        load_group(3)
         load_w2(4)
         load_w2_scales(4)
-        load_a(4, 1, "w2_s1")
-        load_a(4, 0, 2)
+        load_group(4)
         load_w2(5)
-
-        def last_loads():
-            load_a(last, 0, 4)
-            load_a(last, 1, 3)
-            load_w1_scales()
-            for n in range(W1_PIECES):
-                load_w1(n)
-            nc.sync.dma_start(pos1_sb[:], pos1)
-            nc.sync.dma_start(pos2_sb[:], pos2)
+        load_group(5)
+        load_w1_scales()
+        load_w1(0)
+        nc.sync.dma_start(pos1_sb[:], pos1)
+        nc.sync.dma_start(pos2_sb[:], pos2)
 
         def bank(name):
             return psum.tile([P, PASS], F32, name=name, tag="bank", bufs=BANKS)
@@ -157,7 +153,7 @@ def tile_moe_bdx_mlp_relu_kernel(
         nc.tensor.transpose(gate_ps[:, 0:P], gate_rows[:], ident[:])
         nc.scalar.activation(gate_col[:], gate_ps[:, 0 : S // P], ACT.Copy)
 
-        g_s, g_w, rounded, mask_of, turned_of, da_of, codes_of, scales_of = {}, {}, {}, {}, {}, {}, {}, {}
+        g_s, g_w, rounded, signed, mask_of, turned_of, da_of, codes_of, scales_of = {}, {}, {}, {}, {}, {}, {}, {}, {}
         blocks_done = []
 
         def expert(g, j):
@@ -181,21 +177,19 @@ def tile_moe_bdx_mlp_relu_kernel(
         def paired(tile):
             return tile.rearrange("p (u c d) -> p u c d", u=2, d=2)
 
-        def saved(g, u, c0=0):
-            return a_sb[g, u, c0][:].rearrange("p d c -> p c d")
+        def saved(g):
+            return a_sb[g][:].rearrange("p u d c -> p u c d")
 
-        def signed(u):
-            return signs[:, u, :].rearrange("p (c d) -> p c d", d=2)
+        def sign(g, quarter):
+            signed[g, quarter] = made_on_scalar(4 * HALF, BF16, "sign")
+            nc.scalar.activation(paired(signed[g, quarter][:]), saved(g)[:, :, quarter * HALF : (quarter + 1) * HALF, :], ACT.Sign)
 
-        def sign(g):
-            source = saved(g, 1)
-            c0, c1 = EXTRA_LIFT.get(g, 0), C if g == last - 1 else WIDE
-            nc.scalar.activation(signed(1)[:, c0:c1, :], source[:, c0:c1, :], ACT.Sign)
-
-        def lift(g, u=0, width=WIDE):
-            nc.gpsimd.tensor_scalar(
-                out=signed(u)[:, 0:width, :], in0=saved(g, u)[:, 0:width, :], scalar1=LIFT, scalar2=0.0, op0=ALU.mult, op1=ALU.add
-            )
+        def lift(g):
+            width = LIFTED_QUARTERS[g] * HALF
+            for u in range(2):
+                nc.gpsimd.tensor_scalar(
+                    out=paired(lifted[:])[:, u, 0:width, :], in0=saved(g)[:, u, 0:width, :], scalar1=LIFT, scalar2=0.0, op0=ALU.mult, op1=ALU.add
+                )
 
         def turn(g, j, h):
             turned = bank("turned")
@@ -222,19 +216,16 @@ def tile_moe_bdx_mlp_relu_kernel(
                 stop=True,
             )
             if b % 2 == 0:
-                behind = [n for n, at in SIGN_AFTER.items() if at == k - 1 and n < 4]
-                if behind:
-                    rounded[g, j, b // 2] = keep.tile([P, 2 * PASS], BF16, name="x", tag=room_of[behind[0], 1, 0], align_bytes=64)
-                else:
-                    rounded[g, j, b // 2] = made_on_scalar(2 * PASS, BF16, "x")
+                rounded[g, j, b // 2] = made_on_scalar(2 * PASS, BF16, "x")
             nc.scalar.activation(
                 rounded[g, j, b // 2][:, b % 2 * PASS : (b % 2 + 1) * PASS].rearrange("m (u p d) -> m u p d", u=2, d=2),
                 dh[:].rearrange("m (p u d) -> m u p d", u=2, d=2),
                 ACT.Copy,
                 scale=gate_col[:, e * BLOCKS + b : e * BLOCKS + b + 1],
             )
-            if k == SIGN_AFTER[2] + 1:
-                last_loads()
+            for (signed_g, quarter), at in SIGN_AFTER.items():
+                if k == at:
+                    sign(signed_g, quarter)
             for (turned_g, turned_j), at in TURN_AFTER.items():
                 if k == at:
                     for h in (1, 0):
@@ -244,30 +235,34 @@ def tile_moe_bdx_mlp_relu_kernel(
             while len(blocks_done) <= k:
                 next_block()
 
-        def sign_in_turn(g):
-            blocks_through(SIGN_AFTER[g])
-            sign(g)
-
         def compare(target, source):
             nc.vector.tensor_scalar(out=target, in0=source, scalar1=0.0, scalar2=None, op0=ALU.is_gt)
 
-        def make_mask(g, j):
-            mask_of[g, j] = made_on_vector(4 * C, BF16, "mask")
-            compare(paired(mask_of[g, j][:]), signs[:].rearrange("p u (c d) -> p u c d", d=2)[:, :, j * C : (j + 1) * C, :])
+        def make_mask(g, quarter, count, source):
+            mask = made_on_vector(4 * count * HALF, BF16, "mask")
+            compare(paired(mask[:]), source)
+            for n in range(count):
+                mask_of[g, quarter + n] = mask[:].rearrange("p (u c d) -> p c u d", u=2, d=2)[:, n * HALF : (n + 1) * HALF]
 
-        def half_mask(g, j, u):
-            if (g, j) not in mask_of:
-                mask_of[g, j] = made_on_vector(4 * C, BF16, "mask")
-            source = signed(0) if u == 0 else saved(g, 1)
-            compare(paired(mask_of[g, j][:])[:, u], source[:, j * C : (j + 1) * C, :])
+        def lifted_mask(g, quarter, count):
+            make_mask(g, quarter, count, paired(lifted[:])[:, :, quarter * HALF : (quarter + count) * HALF, :])
+
+        def make_masks(g):
+            for quarter in (3, 2):
+                if (g, quarter) in SIGN_AFTER:
+                    blocks_through(SIGN_AFTER[g, quarter])
+                    make_mask(g, quarter, 1, paired(signed[g, quarter][:]))
+            if LIFTED_QUARTERS[g] > 2:
+                lifted_mask(g, 2, LIFTED_QUARTERS[g] - 2)
+            lifted_mask(g, 0, 2)
 
         def masked_slots(g, j, c0, width, da):
-            mask = mask_of[g, j][:].rearrange("p (u c d) -> p c u d", u=2, d=2)
+            mask = mask_of[g, 2 * j + c0 // HALF]
             turned = turned_of[g, j, c0 // HALF].bitcast(BF16).rearrange("p (u c d) -> p c u d", u=2, d=2)
             nc.vector.tensor_tensor(
                 da.rearrange("p (c u d) -> p c u d", u=2, d=2),
                 turned[:, c0 % HALF : c0 % HALF + width],
-                mask[:, c0 : c0 + width],
+                mask[:, c0 % HALF : c0 % HALF + width],
                 ALU.mult,
             )
 
@@ -318,41 +313,27 @@ def tile_moe_bdx_mlp_relu_kernel(
         gather_words(2)
         gather_words(3)
         gather_bytes(4)
-        for u in range(2):
-            lift(0, u)
+        lift(0)
         late_gathers = [(gather_bytes, 5), (gather_words, 4), (gather_words, 5)]
 
-        for g in range(last - 1):
+        for g in range(last):
             if g > 0:
                 quantise_pass(g - 1, 0)
-            make_mask(g, 1)
-            make_mask(g, 0)
-            if g + 1 in EXTRA_LIFT:
-                lift(g + 1, 1, EXTRA_LIFT[g + 1])
+            make_masks(g)
             lift(g + 1)
             if g > 0:
                 quantise_pass(g - 1, 1)
             if g < len(late_gathers):
                 late_gathers[g][0](late_gathers[g][1])
-            if g + 1 in SIGN_AFTER:
-                sign_in_turn(g + 1)
             masked(g, 0)
             masked(g, 1)
 
-        g = last - 1
-        quantise_pass(g - 1, 0)
-        half_mask(g, 1, 1)
-        make_mask(g, 0)
-        half_mask(g, 1, 0)
-        lift(last)
-        quantise_pass(g - 1, 1)
-        masked(g, 0)
-        masked(g, 1)
-        quantise_pass(g, 0)
-        half_mask(last, 0, 0)
-        half_mask(last, 1, 0)
-        quantise_pass(g, 1)
-        half_mask(last, 0, 1)
+        quantise_pass(last - 1, 0)
+        make_masks(last)
+        nc.gpsimd.tensor_scalar(
+            out=paired(lifted[:])[:, :, 0:HALF, :], in0=saved(last)[:, :, 3 * HALF : WIDE, :], scalar1=LIFT, scalar2=0.0, op0=ALU.mult, op1=ALU.add
+        )
+        quantise_pass(last - 1, 1)
 
         blocks_through(LAST_BLOCK - 2)
         turn(last, 0, 0)
@@ -361,7 +342,6 @@ def tile_moe_bdx_mlp_relu_kernel(
         turn(last, 1, 0)
         second_product(0)
         turn(last, 1, 1)
-        half_mask(last, 1, 1)
         masked(last, 0)
         for e in range(1, E - 2):
             second_product(e)
@@ -374,6 +354,7 @@ def tile_moe_bdx_mlp_relu_kernel(
             masked_slots(last, 1, c0, width, pieces[n][:])
 
         last_masked(0)
+        make_mask(last, 3, 1, paired(lifted[:])[:, :, 0:HALF, :])
         quantise_pass(last, 0)
         sums_for_vector = second_sums(last_e - 1)
         accs = []

@@ -35,8 +35,8 @@ A_ROOMS = 3
 VECTOR_TILES = 26
 SCALAR_TILES = 14
 LIFT = 2.0**23
-SIGN_AFTER = {(1, 2): 13, (1, 3): 15, (2, 3): 21, (3, 3): 27, (4, 2): 33, (4, 3): 35, (5, 2): 40}
-TURN_AFTER = {(0, 1): 15, (0, 0): 15, (1, 1): 23, (1, 0): 23, (2, 1): 31, (2, 0): 31, (3, 1): 36, (3, 0): 36, (4, 0): 40, (4, 1): 41}
+SIGN_AFTER = {(1, 2): 14, (1, 3): 15, (2, 3): 21, (3, 3): 28, (4, 2): 35, (4, 3): 35}
+TURN_AFTER = {(0, 1): 15, (0, 0): 15, (1, 1): 23, (1, 0): 23, (2, 1): 31, (2, 0): 31, (3, 1): 35, (3, 0): 35, (4, 0): 40, (4, 1): 41}
 PASS_ORDER = ((0, 0), (0, 1), (1, 0), (1, 1), (2, 0), (3, 0), (2, 1), (3, 1), (4, 0), (4, 1), (5, 0), (5, 1))
 LIFTED_QUARTERS = (4, 2, 3, 3, 2, 2)
 FIRST_PIECE = P
@@ -329,6 +329,7 @@ def tile_moe_bdx_mlp_relu_kernel(
             masked(g, 1)
 
         quantise_pass(last - 1, 0)
+        make_mask(last, 2, 1, saved(last)[:, :, C : C + HALF, :])
         make_masks(last)
         nc.gpsimd.tensor_scalar(
             out=paired(lifted[:])[:, :, 0:HALF, :], in0=saved(last)[:, :, 3 * HALF : WIDE, :], scalar1=LIFT, scalar2=0.0, op0=ALU.mult, op1=ALU.add

@@ -35,10 +35,11 @@ A_ROOMS = 3
 VECTOR_TILES = 26
 SCALAR_TILES = 14
 LIFT = 2.0**23
-SIGN_AFTER = {(1, 2): 14, (1, 3): 15, (2, 3): 21, (3, 3): 28, (4, 2): 35, (4, 3): 35}
+SIGN_AFTER = {(1, 2): 14, (1, 3): 14, (2, 3): 21, (3, 3): 28, (4, 2): 35, (4, 3): 35}
 TURN_AFTER = {(0, 1): 15, (0, 0): 15, (1, 1): 23, (1, 0): 23, (2, 1): 31, (2, 0): 31, (3, 1): 35, (3, 0): 35, (4, 0): 40, (4, 1): 41}
 PASS_ORDER = ((0, 0), (0, 1), (1, 0), (1, 1), (2, 0), (3, 0), (2, 1), (3, 1), (4, 0), (4, 1), (5, 0), (5, 1))
 LIFTED_QUARTERS = (4, 2, 3, 3, 2, 2)
+BY_EXPERT = 4
 FIRST_PIECE = P
 SCALE_GROUPS = {0: 1, 1: 1, 2: 2, 4: 2}
 W1_PIECES = 1
@@ -80,9 +81,13 @@ def tile_moe_bdx_mlp_relu_kernel(
 
         def load_a(g):
             pair, s = divmod(g, PASSES)
-            rows = a[s * PASS : (s + 1) * PASS, pair * WIDE : (pair + 1) * WIDE].rearrange("(p u d) c -> p u d c", u=2, d=2)
-            a_sb[g] = keep.tile([P, 2, 2, WIDE], F32, name="a_sb", tag="a_room%d" % (g % A_ROOMS))
-            return [lambda u=u: nc.sync.dma_start(a_sb[g][:, u], rows[:, u]) for u in range(2)]
+            rows = a[s * PASS : (s + 1) * PASS, pair * WIDE : (pair + 1) * WIDE].rearrange("(p t) c -> p t c", t=4)
+            a_sb[g] = keep.tile([P, 4, WIDE], F32, name="a_sb", tag="a_room%d" % (g % A_ROOMS))
+            if g < BY_EXPERT:
+                parts = [(slice(2 * u, 2 * u + 2), slice(0, WIDE)) for u in range(2)]
+            else:
+                parts = [(slice(0, 4), slice(j * C, (j + 1) * C)) for j in range(2)]
+            return [lambda t=t, c=c: nc.sync.dma_start(a_sb[g][:, t, c], rows[:, t, c]) for t, c in parts]
 
         def load_group(g):
             for load in load_a(g):
@@ -172,13 +177,13 @@ def tile_moe_bdx_mlp_relu_kernel(
             gathered = made_on_vector(c1 - c0, U32, "g_w")
             nc.vector.tensor_copy(gathered[:], dy_w[:].bitcast(U32).indirect(slots(e, c0, c1)))
             for c in range(c0, c1, P):
-                g_w[e, c // P] = gathered[:, c - c0 : c - c0 + P]
+                g_w[e + c // C, c % C // P] = gathered[:, c - c0 : c - c0 + P]
 
         def paired(tile):
             return tile.rearrange("p (u c d) -> p u c d", u=2, d=2)
 
         def saved(g):
-            return a_sb[g][:].rearrange("p u d c -> p u c d")
+            return a_sb[g][:].rearrange("p (u d) c -> p u c d", u=2)
 
         def sign(g, quarter):
             signed[g, quarter] = made_on_scalar(4 * HALF, BF16, "sign")
@@ -186,7 +191,7 @@ def tile_moe_bdx_mlp_relu_kernel(
 
         def lift(g):
             width = LIFTED_QUARTERS[g] * HALF
-            for u in range(2):
+            for u in (slice(0, 1), slice(1, 2)) if g < BY_EXPERT else (slice(0, 2),):
                 nc.gpsimd.tensor_scalar(
                     out=paired(lifted[:])[:, u, 0:width, :], in0=saved(g)[:, u, 0:width, :], scalar1=LIFT, scalar2=0.0, op0=ALU.mult, op1=ALU.add
                 )
@@ -312,9 +317,13 @@ def tile_moe_bdx_mlp_relu_kernel(
         gather_bytes(2, 0, 2 * C)
         gather_words(2)
         gather_words(3)
-        gather_bytes(4)
+        gather_bytes(4, 0, HALF)
         lift(0)
-        late_gathers = [(gather_bytes, 5), (gather_words, 4), (gather_words, 5)]
+        late_gathers = [
+            [(gather_bytes, 4, HALF, C + HALF)],
+            [(gather_words, 4, 0, C - P), (gather_bytes, 5, HALF, C)],
+            [(gather_words, 4, C - P, 2 * C)],
+        ]
 
         for g in range(last):
             if g > 0:
@@ -323,8 +332,8 @@ def tile_moe_bdx_mlp_relu_kernel(
             lift(g + 1)
             if g > 0:
                 quantise_pass(g - 1, 1)
-            if g < len(late_gathers):
-                late_gathers[g][0](late_gathers[g][1])
+            for gather, e, c0, c1 in late_gathers[g] if g < len(late_gathers) else ():
+                gather(e, c0, c1)
             masked(g, 0)
             masked(g, 1)
 

@@ -35,10 +35,11 @@ A_ROOMS = 3
 VECTOR_TILES = 26
 SCALAR_TILES = 14
 LIFT = 2.0**23
-SIGN_AFTER = {(1, 2): 14, (1, 3): 14, (2, 3): 21, (3, 3): 28, (4, 2): 35, (4, 3): 35}
+SIGN_AFTER = {(1, 2): 14, (1, 3): 14, (2, 3): 21, (3, 3): 28, (4, 2): 37}
 TURN_AFTER = {(0, 1): 15, (0, 0): 15, (1, 1): 23, (1, 0): 23, (2, 1): 31, (2, 0): 31, (3, 1): 35, (3, 0): 35, (4, 0): 40, (4, 1): 41}
 PASS_ORDER = ((0, 0), (0, 1), (1, 0), (1, 1), (2, 0), (3, 0), (2, 1), (3, 1), (4, 0), (4, 1), (5, 0), (5, 1))
 LIFTED_QUARTERS = (4, 2, 3, 3, 2, 2)
+DIRECT = ((4, 3), (5, 2))
 BY_EXPERT = 4
 FIRST_PIECE = P
 SCALE_GROUPS = {0: 1, 1: 1, 2: 2, 4: 2}
@@ -66,7 +67,7 @@ def tile_moe_bdx_mlp_relu_kernel(
         w2_s_group = {e0: keep.tile([P, n * H], U8, name="w2_s", tag="w2_s%d" % (e0 % 4), align_bytes=64) for e0, n in SCALE_GROUPS.items()}
         w2_s = [w2_s_group[e0][:, j * H : (j + 1) * H] for e0, n in SCALE_GROUPS.items() for j in range(n)]
         w1_s = keep.tile([P, E * PASSES * K], U8, name="w1_s", tag="w2_s2", align_bytes=64)
-        w2_w = [keep.tile([P, 2 * H], U8, name="w2_w", tag="w%d" % (0, 1, 2, 3, 0, 2)[e], align_bytes=64) for e in range(E)]
+        w2_w = [keep.tile([P, 2 * H], U8, name="w2_w", tag="w%d" % (e % 4), align_bytes=64) for e in range(E)]
         w1_w = [keep.tile([P, W1_EXPERTS * PASSES * 2 * K], U8, name="w1_w", tag="w3", align_bytes=64) for n in range(W1_PIECES)]
         ident = keep.tile([P, P], F32, name="ident")
         gate_rows = keep.tile([P, P], F32, name="gate_rows")
@@ -137,8 +138,8 @@ def tile_moe_bdx_mlp_relu_kernel(
         load_group(3)
         load_w2(4)
         load_w2_scales(4)
-        load_group(4)
         load_w2(5)
+        load_group(4)
         load_group(5)
         load_w1_scales()
         load_w1(0)
@@ -257,6 +258,8 @@ def tile_moe_bdx_mlp_relu_kernel(
                 if (g, quarter) in SIGN_AFTER:
                     blocks_through(SIGN_AFTER[g, quarter])
                     make_mask(g, quarter, 1, paired(signed[g, quarter][:]))
+                elif (g, quarter) in DIRECT:
+                    make_mask(g, quarter, 1, saved(g)[:, :, quarter * HALF : (quarter + 1) * HALF, :])
             if LIFTED_QUARTERS[g] > 2:
                 lifted_mask(g, 2, LIFTED_QUARTERS[g] - 2)
             lifted_mask(g, 0, 2)
@@ -338,7 +341,6 @@ def tile_moe_bdx_mlp_relu_kernel(
             masked(g, 1)
 
         quantise_pass(last - 1, 0)
-        make_mask(last, 2, 1, saved(last)[:, :, C : C + HALF, :])
         make_masks(last)
         nc.gpsimd.tensor_scalar(
             out=paired(lifted[:])[:, :, 0:HALF, :], in0=saved(last)[:, :, 3 * HALF : WIDE, :], scalar1=LIFT, scalar2=0.0, op0=ALU.mult, op1=ALU.add

@@ -35,11 +35,11 @@ A_ROOMS = 3
 VECTOR_TILES = 26
 SCALAR_TILES = 14
 LIFT = 2.0**23
-SIGN_AFTER = {(1, 2): 14, (1, 3): 14, (2, 3): 21, (3, 3): 28, (4, 2): 37}
-TURN_AFTER = {(0, 1): 15, (0, 0): 15, (1, 1): 23, (1, 0): 23, (2, 1): 31, (2, 0): 31, (3, 1): 35, (3, 0): 35, (4, 0): 40, (4, 1): 41}
+SIGN_AFTER = {(1, 2): 14, (1, 3): 14, (2, 3): 21, (3, 3): 28, (4, 2): 37, (5, 2): 43}
+TURN_AFTER = {(0, 1): 15, (0, 0): 15, (1, 1): 23, (1, 0): 23, (2, 1): 31, (2, 0): 31, (3, 1): 35, (3, 0): 35, (4, 0): 40, (4, 1): 41, (5, 0): 45}
 PASS_ORDER = ((0, 0), (0, 1), (1, 0), (1, 1), (2, 0), (3, 0), (2, 1), (3, 1), (4, 0), (4, 1), (5, 0), (5, 1))
 LIFTED_QUARTERS = (4, 2, 3, 3, 2, 2)
-DIRECT = ((4, 3), (5, 2))
+DIRECT = ((4, 3),)
 BY_EXPERT = 4
 FIRST_PIECE = P
 SCALE_GROUPS = {0: 1, 1: 1, 2: 2, 4: 2}
@@ -341,16 +341,13 @@ def tile_moe_bdx_mlp_relu_kernel(
             masked(g, 1)
 
         quantise_pass(last - 1, 0)
-        make_masks(last)
+        lifted_mask(last, 0, 2)
         nc.gpsimd.tensor_scalar(
             out=paired(lifted[:])[:, :, 0:HALF, :], in0=saved(last)[:, :, 3 * HALF : WIDE, :], scalar1=LIFT, scalar2=0.0, op0=ALU.mult, op1=ALU.add
         )
         quantise_pass(last - 1, 1)
 
-        blocks_through(LAST_BLOCK - 2)
-        turn(last, 0, 0)
         blocks_through(LAST_BLOCK)
-        turn(last, 0, 1)
         turn(last, 1, 0)
         second_product(0)
         turn(last, 1, 1)
@@ -365,7 +362,7 @@ def tile_moe_bdx_mlp_relu_kernel(
             pieces.append(made_on_vector(4 * width, BF16, "da"))
             masked_slots(last, 1, c0, width, pieces[n][:])
 
-        last_masked(0)
+        make_mask(last, 2, 1, paired(signed[last, 2][:]))
         make_mask(last, 3, 1, paired(lifted[:])[:, :, 0:HALF, :])
         quantise_pass(last, 0)
         sums_for_vector = second_sums(last_e - 1)
@@ -385,7 +382,7 @@ def tile_moe_bdx_mlp_relu_kernel(
                 nc.vector.tensor_copy(dx[:, (last_e - 1) * C : last_e * C], sums_for_vector[:])
                 nc.vector.tensor_copy(target, accs[n][:, 0:width])
 
-        for n in range(1, len(LAST_PIECES)):
+        for n in range(len(LAST_PIECES)):
             last_masked(n)
         for n in range(len(LAST_PIECES)):
             last_product(n)

from contextlib import ExitStack

import concourse.mybir as mybir
from concourse.masks import make_identity

K, T, E, C, H, N = 128, 1536, 6, 512, 1024, 512
S = E * C
FLOPS = 2 * S * H * (N + K)
BYTES = N * T + N * T // 32 + 4 * H * S + E * H * (N + K) // 2 + E * H * (N + K) // 32 + 4 * S + 256 * (S + 2 * T) // 16 + 4 * K * T

F32 = mybir.dt.float32
BF16 = mybir.dt.bfloat16
I32 = mybir.dt.int32
U32 = mybir.dt.uint32
U16 = mybir.dt.uint16
U8 = mybir.dt.uint8
E5M2X4 = mybir.dt.float8_e5m2_x4
E2M1X4 = mybir.dt.float4_e2m1fn_x4
ALU = mybir.AluOpType
ACT = mybir.ActivationFunctionType

P = 128
PASS = 512
PASSES = H // PASS
BLOCKS = C // P
LAST_BLOCK = E * PASSES * BLOCKS - 1
HALF = C // 2
LIST_COL = 16
SCALE_ROWS = 4
BANKS = 8
PAIRS = E // 2
WIDE = 2 * C
GROUPS = PAIRS * PASSES
A_ROOMS = 3
VECTOR_TILES = 26
SCALAR_TILES = 14
LIFT = 2.0**23
SIGN_AFTER = {(1, 2): 14, (1, 3): 14, (2, 3): 21, (3, 3): 28, (4, 2): 37, (5, 2): 43}
TURN_AFTER = {(0, 1): 15, (0, 0): 15, (1, 1): 23, (1, 0): 23, (2, 1): 31, (2, 0): 31, (3, 1): 35, (3, 0): 35, (4, 0): 40, (4, 1): 41, (5, 0): 45}
PASS_ORDER = ((0, 0), (0, 1), (1, 0), (1, 1), (2, 0), (3, 0), (2, 1), (3, 1), (4, 0), (4, 1), (5, 0), (5, 1))
LIFTED_QUARTERS = (4, 2, 3, 3, 2, 2)
DIRECT = ((4, 3),)
BY_EXPERT = 4
FIRST_PIECE = P
SCALE_GROUPS = {0: 1, 1: 1, 2: 2, 4: 2}
W1_PIECES = 1
W1_EXPERTS = E // W1_PIECES
LAST_PIECES = ((0, HALF), (HALF, P), (HALF + P, P))
OWN_PIECE = 256
OUT_PIECES = (128, 384, 352, 288, 128)


def tile_moe_bdx_mlp_relu_kernel(
    tc, dy_words, dy_scales, a, w2_words, w2_scales, w1_words, w1_scales, gate, offs, pos1, pos2, out
):
    nc = tc.nc
    with ExitStack() as ctx:
        keep = ctx.enter_context(tc.tile_pool(name="keep", bufs=1))
        ring = ctx.enter_context(tc.tile_pool(name="ring", bufs=2))
        psum = ctx.enter_context(tc.psum_pool(name="psum", bufs=1))

        offs_sb = keep.tile([P, S // LIST_COL], U16, name="offs_sb")
        pos1_sb = keep.tile([P, T // LIST_COL], U16, name="pos1_sb")
        pos2_sb = keep.tile([P, T // LIST_COL], U16, name="pos2_sb")
        dy_w = keep.tile([P, T], I32, name="dy_w", align_bytes=64)
        dy_s = keep.tile([P, T], U8, name="dy_s", align_bytes=64)
        w2_s_group = {e0: keep.tile([P, n * H], U8, name="w2_s", tag="w2_s%d" % (e0 % 4), align_bytes=64) for e0, n in SCALE_GROUPS.items()}
        w2_s = [w2_s_group[e0][:, j * H : (j + 1) * H] for e0, n in SCALE_GROUPS.items() for j in range(n)]
        w1_s = keep.tile([P, E * PASSES * K], U8, name="w1_s", tag="w2_s2", align_bytes=64)
        w2_w = [keep.tile([P, 2 * H], U8, name="w2_w", tag="w%d" % (e % 4), align_bytes=64) for e in range(E)]
        w1_w = [keep.tile([P, W1_EXPERTS * PASSES * 2 * K], U8, name="w1_w", tag="w3", align_bytes=64) for n in range(W1_PIECES)]
        ident = keep.tile([P, P], F32, name="ident")
        gate_rows = keep.tile([P, P], F32, name="gate_rows")
        gate_col = keep.tile([P, S // P], F32, name="gate_col")
        dx = keep.tile([P, S], F32, name="dx")
        lifted = keep.tile([P, 4 * WIDE], BF16, name="lifted")
        a_sb = {}
        last = GROUPS - 1

        nc.gpsimd.memset(dy_s[:].bitcast(I32), 0)
        make_identity(nc, ident[:])

        def load_a(g):
            pair, s = divmod(g, PASSES)
            rows = a[s * PASS : (s + 1) * PASS, pair * WIDE : (pair + 1) * WIDE].rearrange("(p t) c -> p t c", t=4)
            a_sb[g] = keep.tile([P, 4, WIDE], F32, name="a_sb", tag="a_room%d" % (g % A_ROOMS))
            if g < BY_EXPERT:
                parts = [(slice(2 * u, 2 * u + 2), slice(0, WIDE)) for u in range(2)]
            else:
                parts = [(slice(0, 4), slice(j * C, (j + 1) * C)) for j in range(2)]
            return [lambda t=t, c=c: nc.sync.dma_start(a_sb[g][:, t, c], rows[:, t, c]) for t, c in parts]

        def load_group(g):
            for load in load_a(g):
                load()

        def load_w2(e):
            nc.sync.dma_start(w2_w[e][:].bitcast(I32), w2_words[e, 0].bitcast(I32))

        def load_w2_scales(e0):
            group = w2_s_group[e0]
            for r in range(SCALE_ROWS):
                nc.sync.dma_start(
                    group[r:P:32, :].bitcast(I32).rearrange("q (e i) -> q e i", i=H // 4),
                    w2_scales[e0 : e0 + SCALE_GROUPS[e0], 0, r:16:4, :].bitcast(I32).rearrange("e q i -> q e i"),
                )

        def load_w1_scales():
            for r in range(SCALE_ROWS):
                nc.sync.dma_start(
                    w1_s[r:P:32, :].bitcast(I32).rearrange("q (g k) -> q g k", g=E * PASSES),
                    w1_scales.rearrange("e s f k -> (e s) f k")[:, r:16:4, :].bitcast(I32).rearrange("g q k -> q g k"),
                )

        def load_w1(n):
            nc.sync.dma_start(
                w1_w[n][:].bitcast(I32).rearrange("p (g k) -> p g k", g=W1_EXPERTS * PASSES),
                w1_words[n * W1_EXPERTS : (n + 1) * W1_EXPERTS].rearrange("e s p k -> p (e s) k").bitcast(I32),
            )

        nc.sync.dma_start(offs_sb[:], offs)
        nc.sync.dma_start(gate_rows[:], gate.rearrange("h (b m) -> (h b) m", m=P)[0:P, :])
        for r in range(SCALE_ROWS):
            nc.sync.dma_start(dy_s[r:P:32, :].bitcast(I32), dy_scales[0, r:16:4, :].bitcast(I32))
        nc.sync.dma_start(dy_w[:], dy_words[0].rearrange("p t d -> p (t d)").bitcast(I32))
        load_w2(0)
        load_w2_scales(0)
        first_half, second_half = load_a(0)
        first_half()
        load_w2(1)
        load_w2_scales(1)
        second_half()
        load_group(1)
        load_w2(2)
        load_w2_scales(2)
        load_group(2)
        load_w2(3)
        load_group(3)
        load_w2(4)
        load_w2_scales(4)
        load_w2(5)
        load_group(4)
        load_group(5)
        load_w1_scales()
        load_w1(0)
        nc.sync.dma_start(pos1_sb[:], pos1)
        nc.sync.dma_start(pos2_sb[:], pos2)

        def bank(name):
            return psum.tile([P, PASS], F32, name=name, tag="bank", bufs=BANKS)

        def made_on_vector(columns, dtype, name):
            return ring.tile([P, columns], dtype, name=name, tag="made_on_vector", align_bytes=64, bufs=VECTOR_TILES)

        def made_on_scalar(columns, dtype, name):
            return ring.tile([P, columns], dtype, name=name, tag="made_on_scalar", bufs=SCALAR_TILES)

        gate_ps = bank("gate_ps")
        nc.tensor.transpose(gate_ps[:, 0:P], gate_rows[:], ident[:])
        nc.scalar.activation(gate_col[:], gate_ps[:, 0 : S // P], ACT.Copy)

        g_s, g_w, rounded, signed, mask_of, turned_of, da_of, codes_of, scales_of = {}, {}, {}, {}, {}, {}, {}, {}, {}
        blocks_done = []

        def expert(g, j):
            return g // PASSES * 2 + j

        def slots(e, c0, c1):
            return offs_sb[:, (e * C + c0) // LIST_COL : (e * C + c1) // LIST_COL]

        def gather_bytes(e, c0=0, c1=C):
            gathered = made_on_vector(c1 - c0, U8, "g_s")
            nc.vector.tensor_copy(gathered[:], dy_s[:].indirect(slots(e, c0, c1)))
            for c in range(c0, c1, P):
                g_s[e + c // C, c % C // P] = gathered[:, c - c0 : c - c0 + P]

        def gather_words(e, c0=0, c1=C):
            gathered = made_on_vector(c1 - c0, U32, "g_w")
            nc.vector.tensor_copy(gathered[:], dy_w[:].bitcast(U32).indirect(slots(e, c0, c1)))
            for c in range(c0, c1, P):
                g_w[e + c // C, c % C // P] = gathered[:, c - c0 : c - c0 + P]

        def paired(tile):
            return tile.rearrange("p (u c d) -> p u c d", u=2, d=2)

        def saved(g):
            return a_sb[g][:].rearrange("p (u d) c -> p u c d", u=2)

        def sign(g, quarter):
            signed[g, quarter] = made_on_scalar(4 * HALF, BF16, "sign")
            nc.scalar.activation(paired(signed[g, quarter][:]), saved(g)[:, :, quarter * HALF : (quarter + 1) * HALF, :], ACT.Sign)

        def lift(g):
            width = LIFTED_QUARTERS[g] * HALF
            for u in (slice(0, 1), slice(1, 2)) if g < BY_EXPERT else (slice(0, 2),):
                nc.gpsimd.tensor_scalar(
                    out=paired(lifted[:])[:, u, 0:width, :], in0=saved(g)[:, u, 0:width, :], scalar1=LIFT, scalar2=0.0, op0=ALU.mult, op1=ALU.add
                )

        def turn(g, j, h):
            turned = bank("turned")
            for b in (1, 0):
                words = rounded[g, j, h][:, b * PASS : (b + 1) * PASS].bitcast(F32)
                for u in range(2):
                    at = (2 * u + b) * P
                    nc.tensor.transpose(turned[:, at : at + P], words[:, u * P : (u + 1) * P], ident[:])
            turned_of[g, j, h] = turned[:]

        def next_block():
            k = len(blocks_done)
            blocks_done.append(k)
            (g, j), b = PASS_ORDER[k // BLOCKS], k % BLOCKS
            e, s = expert(g, j), g % PASSES
            dh = bank("dh")
            nc.tensor.matmul_mx(
                out=dh[:],
                lhsT=g_w[e, b].bitcast(E5M2X4),
                lhsT_scale=g_s[e, b],
                rhs=w2_w[e][:, 2 * s * PASS : 2 * (s + 1) * PASS].bitcast(E2M1X4),
                rhs_scale=w2_s[e][:, s * PASS : (s + 1) * PASS],
                start=True,
                stop=True,
            )
            if b % 2 == 0:
                rounded[g, j, b // 2] = made_on_scalar(2 * PASS, BF16, "x")
            nc.scalar.activation(
                rounded[g, j, b // 2][:, b % 2 * PASS : (b % 2 + 1) * PASS].rearrange("m (u p d) -> m u p d", u=2, d=2),
                dh[:].rearrange("m (p u d) -> m u p d", u=2, d=2),
                ACT.Copy,
                scale=gate_col[:, e * BLOCKS + b : e * BLOCKS + b + 1],
            )
            for (signed_g, quarter), at in SIGN_AFTER.items():
                if k == at:
                    sign(signed_g, quarter)
            for (turned_g, turned_j), at in TURN_AFTER.items():
                if k == at:
                    for h in (1, 0):
                        turn(turned_g, turned_j, h)

        def blocks_through(k):
            while len(blocks_done) <= k:
                next_block()

        def compare(target, source):
            nc.vector.tensor_scalar(out=target, in0=source, scalar1=0.0, scalar2=None, op0=ALU.is_gt)

        def make_mask(g, quarter, count, source):
            mask = made_on_vector(4 * count * HALF, BF16, "mask")
            compare(paired(mask[:]), source)
            for n in range(count):
                mask_of[g, quarter + n] = mask[:].rearrange("p (u c d) -> p c u d", u=2, d=2)[:, n * HALF : (n + 1) * HALF]

        def lifted_mask(g, quarter, count):
            make_mask(g, quarter, count, paired(lifted[:])[:, :, quarter * HALF : (quarter + count) * HALF, :])

        def make_masks(g):
            for quarter in (3, 2):
                if (g, quarter) in SIGN_AFTER:
                    blocks_through(SIGN_AFTER[g, quarter])
                    make_mask(g, quarter, 1, paired(signed[g, quarter][:]))
                elif (g, quarter) in DIRECT:
                    make_mask(g, quarter, 1, saved(g)[:, :, quarter * HALF : (quarter + 1) * HALF, :])
            if LIFTED_QUARTERS[g] > 2:
                lifted_mask(g, 2, LIFTED_QUARTERS[g] - 2)
            lifted_mask(g, 0, 2)

        def masked_slots(g, j, c0, width, da):
            mask = mask_of[g, 2 * j + c0 // HALF]
            turned = turned_of[g, j, c0 // HALF].bitcast(BF16).rearrange("p (u c d) -> p c u d", u=2, d=2)
            nc.vector.tensor_tensor(
                da.rearrange("p (c u d) -> p c u d", u=2, d=2),
                turned[:, c0 % HALF : c0 % HALF + width],
                mask[:, c0 % HALF : c0 % HALF + width],
                ALU.mult,
            )

        def masked(g, j):
            if g < last:
                blocks_through(TURN_AFTER[g, j])
            da_of[g, j] = made_on_vector(4 * C, BF16, "da")
            for h in range(2):
                masked_slots(g, j, h * HALF, HALF, da_of[g, j][:, 4 * h * HALF : 4 * (h + 1) * HALF])

        def quantise(key, da, width):
            codes_of[key] = made_on_vector(width, U32, "codes")
            scales_of[key] = ring.tile([P, width], U8, name="scales", align_bytes=64, bufs=E * PASSES - 1 + len(LAST_PIECES))
            nc.vector.quantize_mx(out=codes_of[key][:].bitcast(E5M2X4), scales=scales_of[key][:], in_=da)

        def quantise_pass(g, j):
            quantise((expert(g, j), g % PASSES), da_of[g, j][:], C)

        def second_pass(acc, e, s, codes, scales):
            n = e * PASSES + s
            in_piece = n % (W1_EXPERTS * PASSES)
            nc.tensor.matmul_mx(
                out=acc,
                lhsT=w1_w[e // W1_EXPERTS][:, 2 * in_piece * K : 2 * (in_piece + 1) * K].bitcast(E2M1X4),
                lhsT_scale=w1_s[:, n * K : (n + 1) * K],
                rhs=codes.bitcast(E5M2X4),
                rhs_scale=scales,
                start=(s == 0),
                stop=(s == PASSES - 1),
            )

        def second_sums(e):
            acc = bank("acc")
            for s in range(PASSES):
                second_pass(acc[:], e, s, codes_of[e, s][:], scales_of[e, s][:])
            return acc

        def second_product(e):
            nc.scalar.copy(dx[:, e * C : (e + 1) * C], second_sums(e)[:])

        gather_bytes(0)
        gather_bytes(1, 0, HALF)
        gather_words(0, 0, FIRST_PIECE)
        gather_words(0, FIRST_PIECE, C)
        gather_bytes(1, HALF, C)
        gather_words(1)
        gather_bytes(2, 0, 2 * C)
        gather_words(2)
        gather_words(3)
        gather_bytes(4, 0, HALF)
        lift(0)
        late_gathers = [
            [(gather_bytes, 4, HALF, C + HALF)],
            [(gather_words, 4, 0, C - P), (gather_bytes, 5, HALF, C)],
            [(gather_words, 4, C - P, 2 * C)],
        ]

        for g in range(last):
            if g > 0:
                quantise_pass(g - 1, 0)
            make_masks(g)
            lift(g + 1)
            if g > 0:
                quantise_pass(g - 1, 1)
            for gather, e, c0, c1 in late_gathers[g] if g < len(late_gathers) else ():
                gather(e, c0, c1)
            masked(g, 0)
            masked(g, 1)

        quantise_pass(last - 1, 0)
        lifted_mask(last, 0, 2)
        nc.gpsimd.tensor_scalar(
            out=paired(lifted[:])[:, :, 0:HALF, :], in0=saved(last)[:, :, 3 * HALF : WIDE, :], scalar1=LIFT, scalar2=0.0, op0=ALU.mult, op1=ALU.add
        )
        quantise_pass(last - 1, 1)

        blocks_through(LAST_BLOCK)
        turn(last, 1, 0)
        second_product(0)
        turn(last, 1, 1)
        masked(last, 0)
        for e in range(1, E - 2):
            second_product(e)
        last_e = E - 1
        pieces = []

        def last_masked(n):
            c0, width = LAST_PIECES[n]
            pieces.append(made_on_vector(4 * width, BF16, "da"))
            masked_slots(last, 1, c0, width, pieces[n][:])

        make_mask(last, 2, 1, paired(signed[last, 2][:]))
        make_mask(last, 3, 1, paired(lifted[:])[:, :, 0:HALF, :])
        quantise_pass(last, 0)
        sums_for_vector = second_sums(last_e - 1)
        accs = []
        for c0, width in LAST_PIECES:
            accs.append(bank("acc"))
            second_pass(accs[-1][:, 0:width], last_e, 0, codes_of[last_e, 0][:, c0 : c0 + width], scales_of[last_e, 0][:, c0 : c0 + width])

        def last_product(n):
            c0, width = LAST_PIECES[n]
            quantise((last_e, 1, n), pieces[n][:], width)
            second_pass(accs[n][:, 0:width], last_e, 1, codes_of[last_e, 1, n][:], scales_of[last_e, 1, n][:])
            target = dx[:, last_e * C + c0 : last_e * C + c0 + width]
            if n + 1 < len(LAST_PIECES):
                nc.scalar.copy(target, accs[n][:, 0:width])
            else:
                nc.vector.tensor_copy(dx[:, (last_e - 1) * C : last_e * C], sums_for_vector[:])
                nc.vector.tensor_copy(target, accs[n][:, 0:width])

        for n in range(len(LAST_PIECES)):
            last_masked(n)
        for n in range(len(LAST_PIECES)):
            last_product(n)

        def list_columns(t0, width):
            return slice(t0 // LIST_COL, (t0 + width) // LIST_COL)

        def add_second_and_store(t0, width, by_first):
            piece = made_on_vector(width, F32, "piece")
            nc.vector.tensor_tensor(piece[:], dx[:].indirect(pos2_sb[:, list_columns(t0, width)]), by_first[:], ALU.add)
            nc.sync.dma_start(out[:, t0 : t0 + width], piece[:])

        own_first = made_on_vector(OWN_PIECE, F32, "own_first")
        nc.vector.tensor_copy(own_first[:], dx[:].indirect(pos1_sb[:, list_columns(0, OWN_PIECE)]))
        t0 = OWN_PIECE
        for n, width in enumerate(OUT_PIECES):
            by_first = made_on_scalar(width, F32, "by_first")
            nc.scalar.activation(by_first[:], dx[:].indirect(pos1_sb[:, list_columns(t0, width)]), ACT.Copy)
            add_second_and_store(t0, width, by_first)
            if n == 0:
                add_second_and_store(0, OWN_PIECE, own_first)
            t0 = t0 + width
